import numpy as np
import ml_dtypes


def mxq(x, axis, fmt="e4m3"):
    dtype, down = {"e4m3": (ml_dtypes.float8_e4m3fn, 7), "e5m2": (ml_dtypes.float8_e5m2, 14)}[fmt]
    v = np.moveaxis(np.asarray(x, np.float32).astype(ml_dtypes.bfloat16).astype(np.float64), axis, -1)
    blocks = v.reshape(v.shape[:-1] + (-1, 32))
    amax = np.abs(blocks).max(-1, keepdims=True)
    byte = np.maximum(np.where(amax > 0, np.frexp(amax)[1] - 1 + 127, 0) - down, 1)
    scale = np.exp2(byte - 127.0)
    codes = (blocks / scale).astype(np.float32).astype(dtype).astype(np.float64)
    return np.moveaxis((codes * scale).reshape(v.shape), -1, axis)


WIDE = False


def mx_kscale(k):
    if not WIDE:
        return np.ones(k)
    levels = np.array([10, -10, 5, -5, 0])
    if k % 512:
        return np.exp2(np.random.permutation(np.resize(levels, k // 32))).repeat(32)
    a = np.empty((k // 512, 16))
    for p in range(k // 512):
        a[p, :8] = np.random.permutation(np.resize(levels, 8))
        for g in range(8):
            far = levels[np.abs(levels - a[p, g]) >= 10]
            a[p, g + 8] = far[np.random.randint(len(far))]
    return np.exp2(a.ravel()).repeat(32)


def f64(x):
    return np.asarray(x).astype(np.float64)


def striped(idx):
    return np.tile(idx.reshape(-1, 16).T, (8, 1)).astype(np.uint16)


def unstriped(offs):
    return offs[:16].T.reshape(-1).astype(np.int64)


E2M1 = np.array([0.0, 0.5, 1.0, 1.5, 2.0, 3.0, 4.0, 6.0, -0.0, -0.5, -1.0, -1.5, -2.0, -3.0, -4.0, -6.0])


def pack_weight(w, fmt):
    k, n = w.shape
    w = f64(np.asarray(w, np.float32).astype(ml_dtypes.bfloat16)).reshape(k // 32, 32, n)
    amax = np.abs(w).max(1)
    if fmt == "e4m3":
        byte = np.frexp(amax)[1] - 1 + 127 - 7
    else:
        mant, ex = np.frexp(amax / 6.0)
        byte = np.where(mant > 0.5, ex, ex - 1) + 127
    byte = np.clip(np.where(amax > 0, byte, 1), 1, 254)
    scaled = (w * np.exp2(127.0 - byte)[:, None, :]).reshape(k, n).astype(np.float32)
    by_word = np.ascontiguousarray(scaled.reshape(k // 512, 128, 4, n).transpose(0, 1, 3, 2))
    if fmt == "e4m3":
        words = by_word.astype(ml_dtypes.float8_e4m3fn).view(np.uint8)
    else:
        c = by_word.astype(ml_dtypes.float4_e2m1fn).view(np.uint8) & 0xF
        words = (c[..., 0::2] | (c[..., 1::2] << 4)).reshape(k // 512, 128, 2 * n)
    return np.ascontiguousarray(words), np.ascontiguousarray(byte.astype(np.uint8).reshape(k // 512, 16, n))


def unpack_weight(words, scales, fmt):
    g, _, n = scales.shape
    words = np.ascontiguousarray(words).reshape(g, 128, n, -1)
    if fmt == "e4m3":
        vals = words.view(ml_dtypes.float8_e4m3fn).astype(np.float64)
    else:
        nib = np.empty((g, 128, n, 4), np.uint8)
        nib[..., 0::2] = words & 0xF
        nib[..., 1::2] = words >> 4
        vals = E2M1[nib]
    vals = vals * np.repeat(np.exp2(scales.astype(np.float64) - 127.0), 8, axis=1)[..., None]
    return vals.transpose(0, 1, 3, 2).reshape(g * 512, n)


def d_sigmoid(v):
    s = 1.0 / (1.0 + np.exp(-np.maximum(v, -700.0)))
    return s * (1.0 - s)


def sigmoid(v):
    return 1.0 / (1.0 + np.exp(-np.maximum(v, -700.0)))


K, T, E, C, H, N = 512, 512, 4, 256, 512, 1024


def by_expert(wq, xq):
    return np.concatenate([wq[e].T @ xq[:, e * C:(e + 1) * C] for e in range(E)], axis=1)


def setup_inputs():
    n = np.random.standard_normal
    s = mx_kscale(K)
    v = mx_kscale(N)
    u = mx_kscale(H)
    first = np.random.permutation(np.repeat(np.arange(E), T // E))
    second = (first + 1 + np.random.permutation(np.repeat(np.arange(E - 1), -(-T // (E - 1)))[:T])) % E
    while np.bincount(second, minlength=E).max() != T // E:
        load = np.bincount(second, minlength=E); hi, lo = int(load.argmax()), int(load.argmin())
        t = np.flatnonzero((second == hi) & (first != lo))[0]; second[t] = lo
    slot_token = np.empty(E * C, np.int64); pos = np.empty((2, T), np.int64); fill = np.zeros(E, np.int64)
    place = np.stack([np.random.permutation(C) for _ in range(E)])
    for r, deal in enumerate((first, second)):
        for t in np.random.permutation(T):
            e = deal[t]; j = e * C + place[e, fill[e]]; fill[e] += 1; slot_token[j] = t; pos[r, t] = j
    g = np.random.uniform(0.2, 0.8, T)
    w_slot = np.empty(E * C); w_slot[pos[0]] = g; w_slot[pos[1]] = 1.0 - g
    x = pack_weight(n((K, T)) * s[:, None], "e4m3")
    dy = pack_weight(n((N, T)) * v[:, None], "e4m3")
    m1 = n((E, K, H))
    m3 = n((E, K, H))
    w1 = [pack_weight(m, "e2m1") for m in m1 / np.sqrt(K) / s[None, :, None]]
    w3 = [pack_weight(m, "e2m1") for m in m3 / np.sqrt(K) / s[None, :, None]]
    w2t = [pack_weight(m, "e2m1") for m in n((E, N, H)) / np.sqrt(N) / v[None, :, None] * u]
    w1t = [pack_weight(m, "e2m1") for m in m1.transpose(0, 2, 1) / np.sqrt(H) / u[None, :, None]]
    w3t = [pack_weight(m, "e2m1") for m in m3.transpose(0, 2, 1) / np.sqrt(H) / u[None, :, None]]
    return {
        "x_words": x[0],
        "x_scales": x[1],
        "dy_words": dy[0],
        "dy_scales": dy[1],
        "w1_words": np.stack([m[0] for m in w1]),
        "w1_scales": np.stack([m[1] for m in w1]),
        "w3_words": np.stack([m[0] for m in w3]),
        "w3_scales": np.stack([m[1] for m in w3]),
        "w2t_words": np.stack([m[0] for m in w2t]),
        "w2t_scales": np.stack([m[1] for m in w2t]),
        "w1t_words": np.stack([m[0] for m in w1t]),
        "w1t_scales": np.stack([m[1] for m in w1t]),
        "w3t_words": np.stack([m[0] for m in w3t]),
        "w3t_scales": np.stack([m[1] for m in w3t]),
        "gate": (np.tile(w_slot, (128, 1))).astype(np.float32),
        "offs": striped(slot_token),
        "pos1": striped(pos[0]),
        "pos2": striped(pos[1]),
    }


def reference(x_words, x_scales, dy_words, dy_scales, w1_words, w1_scales, w3_words, w3_scales, w2t_words, w2t_scales, w1t_words, w1t_scales, w3t_words, w3t_scales, gate, offs, pos1, pos2):
    w1 = np.stack([unpack_weight(w1_words[e], w1_scales[e], "e2m1") for e in range(E)])
    w3 = np.stack([unpack_weight(w3_words[e], w3_scales[e], "e2m1") for e in range(E)])
    w2t = np.stack([unpack_weight(w2t_words[e], w2t_scales[e], "e2m1") for e in range(E)])
    w1t = np.stack([unpack_weight(w1t_words[e], w1t_scales[e], "e2m1") for e in range(E)])
    w3t = np.stack([unpack_weight(w3t_words[e], w3t_scales[e], "e2m1") for e in range(E)])
    idx = unstriped(offs)
    xq = unpack_weight(x_words, x_scales, "e4m3")[:, idx]
    gq = unpack_weight(dy_words, dy_scales, "e4m3")[:, idx]
    dh = f64(gate[:1]) * by_expert(w2t, gq)
    a1, a3 = by_expert(w1, xq), by_expert(w3, xq)
    dx = by_expert(w1t, mxq(dh * a3 * d_sigmoid(a1), 0, "e4m3")) + by_expert(w3t, mxq(dh * sigmoid(a1), 0, "e4m3"))
    out = dx[:, unstriped(pos1)] + dx[:, unstriped(pos2)]
    return out

@@ -1,0 +1,236 @@
+from contextlib import ExitStack
+
+import concourse.mybir as mybir
+from concourse.masks import make_identity
+
+K, T, E, C, H, N = 512, 512, 4, 256, 512, 1024
+S = E * C
+P = 128
+TILES = S // P
+KT = K // P
+FLOPS = 2 * S * (2 * K * H + N * H + 2 * H * K)
+
+F32 = mybir.dt.float32
+BF16 = mybir.dt.bfloat16
+I32 = mybir.dt.int32
+U32 = mybir.dt.uint32
+U16 = mybir.dt.uint16
+U8 = mybir.dt.uint8
+FP8X4 = mybir.dt.float8_e4m3fn_x4
+FP4X4 = mybir.dt.float4_e2m1fn_x4
+ALU = mybir.AluOpType
+ACT = mybir.ActivationFunctionType
+
+
+def tile_moe_rec_glu_sigmoid_kernel(tc, x_words, x_scales, dy_words, dy_scales, w1_words, w1_scales, w3_words, w3_scales, w2t_words, w2t_scales, w1t_words, w1t_scales, w3t_words, w3t_scales, gate, offs, pos1, pos2, out):
+    nc = tc.nc
+    with ExitStack() as ctx:
+        keep = ctx.enter_context(tc.tile_pool(name="keep", bufs=1))
+        pair = ctx.enter_context(tc.tile_pool(name="pair", bufs=4))
+        work = ctx.enter_context(tc.tile_pool(name="work", bufs=3))
+        psum = ctx.enter_context(tc.psum_pool(name="psum", bufs=1))
+
+        offs_sb = keep.tile([P, S // 16], U16, name="offs_sb")
+        pos1_sb = keep.tile([P, T // 16], U16, name="pos1_sb")
+        pos2_sb = keep.tile([P, T // 16], U16, name="pos2_sb")
+        x_win = keep.tile([P, T], I32, name="x_win", align_bytes=64)
+        dy_win = keep.tile([P, 2, T], I32, name="dy_win", align_bytes=64)
+        xs_win = keep.tile([P, 1, T], U8, name="xs_win", align_bytes=64)
+        dys_win = keep.tile([P, 2 * S], U8, name="dys_win", align_bytes=64)
+        dys_both = keep.tile([P, S], U8, name="dys_both", align_bytes=64)
+        dys_second = keep.tile([P, S], U8, name="dys_second", align_bytes=64)
+        w1 = keep.tile([P, E, 2 * H], U8, name="w1", align_bytes=64)
+        w3 = keep.tile([P, E, 2 * H], U8, name="w3", align_bytes=64)
+        w2t = keep.tile([P, 2 * E, 2 * H], U8, name="w2t", align_bytes=64)
+        w1t = keep.tile([P, E, 2 * K], U8, name="w1t", align_bytes=64)
+        w3t = keep.tile([P, E, 2 * K], U8, name="w3t", align_bytes=64)
+        w1s = keep.tile([P, E, H], U8, name="w1s", align_bytes=64)
+        w3s = keep.tile([P, E, H], U8, name="w3s", align_bytes=64)
+        w2ts = keep.tile([P, 2 * E, H], U8, name="w2ts", align_bytes=64)
+        w1ts = keep.tile([P, E, K], U8, name="w1ts", align_bytes=64)
+        w3ts = keep.tile([P, E, K], U8, name="w3ts", align_bytes=64)
+        gate_rows = keep.tile([P, P], F32, name="gate_rows")
+        neg_gate = keep.tile([P, TILES], F32, name="neg_gate")
+        ident = keep.tile([P, P], F32, name="ident")
+        dx = [keep.tile([P, S], F32, name="dx%d" % kt) for kt in range(KT)]
+        codes = [keep.tile([P, 2 * P], U32, name="codes%d" % c, align_bytes=64) for c in range(TILES)]
+        scales = [keep.tile([P, 2 * P], U8, name="scales%d" % c, align_bytes=64) for c in range(TILES)]
+
+        for plane in (dys_win, xs_win, w1s, w3s, w2ts, dys_second):
+            nc.vector.memset(plane[:].bitcast(I32), 0)
+        make_identity(nc, ident[:])
+        for plane in (w1ts, w3ts):
+            nc.gpsimd.memset(plane[:].bitcast(I32), 0)
+
+        def load_scales(plane, rows):
+            for r in range(4):
+                nc.sync.dma_start(plane[r:P:32].bitcast(I32), rows.bitcast(I32)[:, r:16:4, :].rearrange("g q c -> q g c"))
+
+        def load_words(tile, words, first, last):
+            per = words.shape[1]
+            src = words.bitcast(I32)[first:last].rearrange("e s p b -> p (e s) b")
+            nc.sync.dma_start(tile[:, first * per:last * per, :].bitcast(I32), src)
+
+        def flat(rows):
+            return rows.rearrange("e s b c -> (e s) b c")
+
+        nc.sync.dma_start(offs_sb[:], offs)
+        nc.sync.dma_start(x_win[:], x_words[0].rearrange("p t d -> p (t d)").bitcast(I32))
+        for s in range(2):
+            for r in range(0):
+                nc.sync.dma_start(dys_win[4 * s + r:P:32, 0:T].bitcast(I32), dy_scales.bitcast(I32)[s, r:16:4, :])
+        for q in range(4):
+            nc.sync.dma_start(dys_win[32 * q:32 * q + 8, 0:T].bitcast(I32), dy_scales.bitcast(I32)[:, 4 * q:4 * q + 4, :])
+        nc.sync.dma_start(dy_win[:], dy_words.rearrange("s p t d -> p s (t d)").bitcast(I32))
+        load_scales(xs_win, x_scales)
+        load_scales(w1s, flat(w1_scales))
+        load_scales(w3s, flat(w3_scales))
+        load_scales(w2ts, flat(w2t_scales))
+        for tile, words in ((w1, w1_words), (w3, w3_words), (w2t, w2t_words)):
+            load_words(tile, words, 0, 1)
+        nc.sync.dma_start(gate_rows[:], gate[0:P // TILES, :].rearrange("r (c m) -> (r c) m", m=P))
+        load_scales(w1ts, flat(w1t_scales))
+        load_scales(w3ts, flat(w3t_scales))
+        for tile, words in ((w1t, w1t_words), (w3t, w3t_words)):
+            load_words(tile, words, 0, 1)
+        for first, last in ((1, 2), (2, 4)):
+            for tile, words in ((w1, w1_words), (w3, w3_words), (w2t, w2t_words), (w1t, w1t_words), (w3t, w3t_words)):
+                load_words(tile, words, first, last)
+        nc.sync.dma_start(pos1_sb[:], pos1)
+        nc.sync.dma_start(pos2_sb[:], pos2)
+
+        gate_t = psum.tile([P, 4, P], F32, name="gate_t", tag="turn", bufs=1)
+        nc.tensor.transpose(gate_t[:, 0, :], gate_rows[:], ident[:])
+        nc.vector.tensor_scalar(neg_gate[:], gate_t[:, 0, 0:TILES], -1.0, None, ALU.mult)
+
+        slots = {}
+
+        def gathers(e):
+            xg = pair.tile([P, C], U32, name="xg", align_bytes=64)
+            xgs = pair.tile([P, C], U8, name="xgs", align_bytes=64)
+            dyg0 = pair.tile([P, C], U32, name="dyg0", align_bytes=64)
+            dyg1 = pair.tile([P, C], U32, name="dyg1", align_bytes=64)
+            slots.setdefault(e, (xg, xgs, (dyg0, dyg1)))
+            lst = offs_sb[:, e * (C // 16):(e + 1) * (C // 16)]
+            return [
+                lambda: nc.vector.tensor_copy(xg[:], x_win[:].bitcast(U32).indirect(lst)),
+                lambda: nc.vector.tensor_copy(xgs[:], xs_win[:, 0, :].indirect(lst)),
+                lambda: nc.vector.tensor_copy(dyg0[:], dy_win[:, 0, :].bitcast(U32).indirect(lst)),
+                lambda: nc.vector.tensor_copy(dyg1[:], dy_win[:, 1, :].bitcast(U32).indirect(lst)),
+            ]
+
+        def forward(c):
+            e = c // 2
+            xg, xgs, dyg = slots[e]
+            cols = slice((c % 2) * P, (c % 2 + 1) * P)
+            a1 = psum.tile([P, H], F32, name="a1", tag="a1", bufs=2)
+            a3 = psum.tile([P, H], F32, name="a3", tag="a3", bufs=2)
+            dh = psum.tile([P, H], F32, name="dh", tag="dh", bufs=2)
+            nc.tensor.matmul_mx(a1[:], xg[:, cols].bitcast(FP8X4), xgs[:, cols], w1[:, e, :].bitcast(FP4X4), w1s[:, e, :], start=True, stop=True)
+            for s, plane in enumerate((dys_both, dys_second)):
+                nc.tensor.matmul_mx(dh[:], dyg[s][:, cols].bitcast(FP8X4), plane[:, c * P:(c + 1) * P], w2t[:, 2 * e + s, :].bitcast(FP4X4), w2ts[:, 2 * e + s, :], start=(s == 0), stop=(s == 1))
+            nc.tensor.matmul_mx(a3[:], xg[:, cols].bitcast(FP8X4), xgs[:, cols], w3[:, e, :].bitcast(FP4X4), w3s[:, e, :], start=True, stop=True)
+            sig = work.tile([P, H], F32, name="sig")
+            nc.scalar.activation(sig[:], a1[:], ACT.Sigmoid)
+            return sig, a3, dh
+
+        def by_pairs(ap):
+            return ap.rearrange("p (q u e) -> p u q e", u=2, e=2)
+
+        def in_pairs(ap):
+            return ap.rearrange("p (u q e) -> p u q e", u=2, e=2)
+
+        def first_product(c, sig, dh):
+            neg3 = work.tile([P, H], F32, name="neg3")
+            da = work.tile([P, 2, H], BF16, name="da", align_bytes=64)
+            nc.vector.scalar_tensor_tensor(neg3[:], dh[:], neg_gate[:, c:c + 1], sig[:], ALU.mult, ALU.mult)
+            nc.scalar.activation(in_pairs(da[:, 1, :]), by_pairs(neg3[:]), ACT.Copy, scale=-1.0)
+            return neg3, da
+
+        def second_product(sig, a3):
+            negq = work.tile([P, H], F32, name="negq")
+            nc.vector.scalar_tensor_tensor(negq[:], sig[:], 1.0, a3[:], ALU.subtract, ALU.mult)
+            return negq
+
+        def turn(engine, neg3, negq, da):
+            engine.tensor_tensor(in_pairs(da[:, 0, :]), by_pairs(neg3[:]), by_pairs(negq[:]), ALU.mult)
+            words = da[:].rearrange("p a i -> p (a i)").bitcast(F32)
+            turned = psum.tile([P, 4, P], F32, name="turned", tag="turn", bufs=1)
+            for j in (2, 3, 0, 1):
+                nc.tensor.transpose(turned[:, j, :], words[:, j * P:(j + 1) * P], ident[:])
+            grouped = work.tile([P, 2 * 4 * P], BF16, name="grouped", align_bytes=64)
+            nc.scalar.copy(grouped[:].bitcast(F32).rearrange("p (a s u) -> p a s u", a=2, u=2), turned[:].rearrange("p (a u) s -> p a s u", u=2))
+            return grouped
+
+        def back(acc, kt, c):
+            e = c // 2
+            for a, (w, ws) in enumerate(((w1t, w1ts), (w3t, w3ts))):
+                nc.tensor.matmul_mx(acc, w[:, e, 2 * P * kt:2 * P * (kt + 1)].bitcast(FP4X4), ws[:, e, P * kt:P * (kt + 1)], codes[c][:, a * P:(a + 1) * P].bitcast(FP8X4), scales[c][:, a * P:(a + 1) * P], start=(a == 0), stop=(a == 1))
+
+        runs = {0: 4, 4: 3, 7: 1}
+        bank = {}
+
+        def backward(c, grouped):
+            nc.vector.quantize_mx(codes[c][:].bitcast(FP8X4), scales[c][:], grouped[:])
+            start = max(r for r in runs if r <= c)
+            if c == start:
+                bank.setdefault(start, psum.tile([P, runs[start] * P], F32, name="acc", tag="acc", bufs=1))
+            back(bank[start][:, (c - start) * P:(c - start + 1) * P], 0, c)
+            if c == start + runs[start] - 1:
+                nc.scalar.copy(dx[0][:, start * P:(c + 1) * P], bank[start][:])
+
+        head = gathers(0)
+        head[0]()
+        nc.vector.tensor_copy(dys_both[:], dys_win[:].indirect(offs_sb[:]))
+        for r in range(4):
+            nc.scalar.dma_start(dys_second[r:P:32, :].bitcast(I32), dys_both[4 + r:P:32, :].bitcast(I32))
+        for g in head[1:] + gathers(1):
+            g()
+        share = [1,2,1,2,2,0,0,0]
+        later = []
+        sig, a3, dh = forward(0)
+        neg3, da = first_product(0, sig, dh)
+        waiting = None
+        for c in range(TILES):
+            if c in (0, 3):
+                later = later + gathers(2 if c == 0 else 3)
+            negq = second_product(sig, a3)
+            if c + 1 < TILES:
+                sig, a3, dh = forward(c + 1)
+            if waiting is not None:
+                backward(c - 1, waiting)
+            for g in later[:share[c]]:
+                g()
+            later = later[share[c]:]
+            waiting = turn(nc.vector, neg3, negq, da)
+            if c + 1 < TILES:
+                neg3, da = first_product(c + 1, sig, dh)
+        backward(TILES - 1, waiting)
+
+        for kt in range(1, KT):
+            for half in range(2):
+                acc = psum.tile([P, 4 * P], F32, name="late", tag=("a1", "a3", "dh")[kt - 1], bufs=2)
+                for c in range(4 * half, 4 * half + 4):
+                    back(acc[:, (c % 4) * P:(c % 4 + 1) * P], kt, c)
+                nc.scalar.copy(dx[kt][:, half * 4 * P:(half + 1) * 4 * P], acc[:])
+
+        pieces = [(kt, 0, T) for kt in range(KT - 1)] + [(KT - 1, 0, T // 2), (KT - 1, T // 2, T)]
+        pending = None
+
+        def combine(engine, kt, lo, hi, one, two):
+            total = work.tile([P, hi - lo], F32, name="total")
+            engine.tensor_tensor(total[:], one[:], two[:], ALU.add)
+            nc.sync.dma_start(out[kt * P:(kt + 1) * P, lo:hi], total[:])
+
+        for n, (kt, lo, hi) in enumerate(pieces):
+            one = work.tile([P, hi - lo], F32, name="one")
+            two = work.tile([P, hi - lo], F32, name="two")
+            nc.vector.tensor_copy(one[:], dx[kt][:].indirect(pos1_sb[:, lo // 16:hi // 16]))
+            if pending is not None:
+                combine(nc.vector, *pending)
+            nc.vector.tensor_copy(two[:], dx[kt][:].indirect(pos2_sb[:, lo // 16:hi // 16]))
+            pending = (kt, lo, hi, one, two)
+            if n < 0:
+                combine(nc.gpsimd, *pending)
+                pending = None
+        combine(nc.vector, *pending)

@@ -26,8 +26,8 @@ def tile_moe_rec_glu_sigmoid_kernel(tc, x_words, x_scales, dy_words, dy_scales, 
     nc = tc.nc
     with ExitStack() as ctx:
         keep = ctx.enter_context(tc.tile_pool(name="keep", bufs=1))
-        pair = ctx.enter_context(tc.tile_pool(name="pair", bufs=4))
-        work = ctx.enter_context(tc.tile_pool(name="work", bufs=3))
+        pair = ctx.enter_context(tc.tile_pool(name="pair", bufs=3))
+        work = ctx.enter_context(tc.tile_pool(name="work", bufs=4))
         psum = ctx.enter_context(tc.psum_pool(name="psum", bufs=1))
 
         offs_sb = keep.tile([P, S // 16], U16, name="offs_sb")
@@ -36,72 +36,75 @@ def tile_moe_rec_glu_sigmoid_kernel(tc, x_words, x_scales, dy_words, dy_scales, 
         x_win = keep.tile([P, T], I32, name="x_win", align_bytes=64)
         dy_win = keep.tile([P, 2, T], I32, name="dy_win", align_bytes=64)
         xs_win = keep.tile([P, 1, T], U8, name="xs_win", align_bytes=64)
-        dys_win = keep.tile([P, 2 * S], U8, name="dys_win", align_bytes=64)
+        dys_win = keep.tile([P, 2 * S], U8, name="dys_win", tag="reused", align_bytes=64)
         dys_both = keep.tile([P, S], U8, name="dys_both", align_bytes=64)
         dys_second = keep.tile([P, S], U8, name="dys_second", align_bytes=64)
-        w1 = keep.tile([P, E, 2 * H], U8, name="w1", align_bytes=64)
-        w3 = keep.tile([P, E, 2 * H], U8, name="w3", align_bytes=64)
-        w2t = keep.tile([P, 2 * E, 2 * H], U8, name="w2t", align_bytes=64)
-        w1t = keep.tile([P, E, 2 * K], U8, name="w1t", align_bytes=64)
-        w3t = keep.tile([P, E, 2 * K], U8, name="w3t", align_bytes=64)
+        early = keep.tile([P, 4, 2 * H], U8, name="early", align_bytes=64)
         w1s = keep.tile([P, E, H], U8, name="w1s", align_bytes=64)
         w3s = keep.tile([P, E, H], U8, name="w3s", align_bytes=64)
         w2ts = keep.tile([P, 2 * E, H], U8, name="w2ts", align_bytes=64)
-        w1ts = keep.tile([P, E, K], U8, name="w1ts", align_bytes=64)
-        w3ts = keep.tile([P, E, K], U8, name="w3ts", align_bytes=64)
         gate_rows = keep.tile([P, P], F32, name="gate_rows")
         neg_gate = keep.tile([P, TILES], F32, name="neg_gate")
         ident = keep.tile([P, P], F32, name="ident")
-        dx = [keep.tile([P, S], F32, name="dx%d" % kt) for kt in range(KT)]
+        dx = keep.tile([P, KT, S], F32, name="dx")
         codes = [keep.tile([P, 2 * P], U32, name="codes%d" % c, align_bytes=64) for c in range(TILES)]
         scales = [keep.tile([P, 2 * P], U8, name="scales%d" % c, align_bytes=64) for c in range(TILES)]
 
-        for plane in (dys_win, xs_win, w1s, w3s, w2ts, dys_second):
+        for plane in (dys_win[:, 0:T], xs_win[:], dys_win[:, T:]):
+            nc.gpsimd.memset(plane.bitcast(I32), 0)
+        for plane in (w2ts, w1s, w3s, dys_second):
             nc.vector.memset(plane[:].bitcast(I32), 0)
         make_identity(nc, ident[:])
-        for plane in (w1ts, w3ts):
-            nc.gpsimd.memset(plane[:].bitcast(I32), 0)
 
-        def load_scales(plane, rows):
+        def load_scales(plane, rows, queue=nc.sync):
             for r in range(4):
-                nc.sync.dma_start(plane[r:P:32].bitcast(I32), rows.bitcast(I32)[:, r:16:4, :].rearrange("g q c -> q g c"))
+                queue.dma_start(plane[r:P:32].bitcast(I32), rows.bitcast(I32)[:, r:16:4, :].rearrange("g q c -> q g c"))
 
-        def load_words(tile, words, first, last):
-            per = words.shape[1]
-            src = words.bitcast(I32)[first:last].rearrange("e s p b -> p (e s) b")
-            nc.sync.dma_start(tile[:, first * per:last * per, :].bitcast(I32), src)
+        def load_words(rows, words, first, last):
+            nc.sync.dma_start(rows.bitcast(I32), words.bitcast(I32)[first:last].rearrange("e s p b -> p (e s) b"))
 
         def flat(rows):
             return rows.rearrange("e s b c -> (e s) b c")
 
         nc.sync.dma_start(offs_sb[:], offs)
-        nc.sync.dma_start(x_win[:], x_words[0].rearrange("p t d -> p (t d)").bitcast(I32))
-        for s in range(2):
-            for r in range(0):
-                nc.sync.dma_start(dys_win[4 * s + r:P:32, 0:T].bitcast(I32), dy_scales.bitcast(I32)[s, r:16:4, :])
         for q in range(4):
             nc.sync.dma_start(dys_win[32 * q:32 * q + 8, 0:T].bitcast(I32), dy_scales.bitcast(I32)[:, 4 * q:4 * q + 4, :])
-        nc.sync.dma_start(dy_win[:], dy_words.rearrange("s p t d -> p s (t d)").bitcast(I32))
-        load_scales(xs_win, x_scales)
-        load_scales(w1s, flat(w1_scales))
-        load_scales(w3s, flat(w3_scales))
-        load_scales(w2ts, flat(w2t_scales))
-        for tile, words in ((w1, w1_words), (w3, w3_words), (w2t, w2t_words)):
-            load_words(tile, words, 0, 1)
         nc.sync.dma_start(gate_rows[:], gate[0:P // TILES, :].rearrange("r (c m) -> (r c) m", m=P))
-        load_scales(w1ts, flat(w1t_scales))
-        load_scales(w3ts, flat(w3t_scales))
-        for tile, words in ((w1t, w1t_words), (w3t, w3t_words)):
-            load_words(tile, words, 0, 1)
-        for first, last in ((1, 2), (2, 4)):
-            for tile, words in ((w1, w1_words), (w3, w3_words), (w2t, w2t_words), (w1t, w1t_words), (w3t, w3t_words)):
-                load_words(tile, words, first, last)
+        nc.sync.dma_start(x_win[:], x_words[0].rearrange("p t d -> p (t d)").bitcast(I32))
+        nc.sync.dma_start(dy_win[:], dy_words.rearrange("s p t d -> p s (t d)").bitcast(I32))
+        load_words(early[:, 0:1, :], w1_words, 0, 1)
+        load_words(early[:, 2:4, :], w2t_words, 0, 1)
+        load_words(early[:, 1:2, :], w3_words, 0, 1)
+        load_scales(xs_win, x_scales)
+        load_scales(w2ts, flat(w2t_scales), nc.gpsimd)
+        load_scales(w1s, flat(w1_scales))
+        load_scales(w3s, flat(w3_scales), nc.sync)
         nc.sync.dma_start(pos1_sb[:], pos1)
         nc.sync.dma_start(pos2_sb[:], pos2)
 
-        gate_t = psum.tile([P, 4, P], F32, name="gate_t", tag="turn", bufs=1)
+        nc.vector.tensor_copy(dys_both[:], dys_win[:].indirect(offs_sb[:]))
+        nc.scalar.dma_start(dys_second[0:100, :].bitcast(I32), dys_both[4:104, :].bitcast(I32))
+
+        gate_t = psum.tile([P, 4, P], F32, name="gate_t", tag="turn", bufs=2)
         nc.tensor.transpose(gate_t[:, 0, :], gate_rows[:], ident[:])
         nc.vector.tensor_scalar(neg_gate[:], gate_t[:, 0, 0:TILES], -1.0, None, ALU.mult)
+
+        late = keep.tile([P, 24, 2 * H], U8, name="late", tag="reused", align_bytes=64)
+        w1ts = late[:, 20:22, :].rearrange("p a (b c) -> p (a b) c", b=2)
+        w3ts = late[:, 22:24, :].rearrange("p a (b c) -> p (a b) c", b=2)
+        nc.gpsimd.memset(late[:, 20:24, :].bitcast(I32), 0)
+        load_words(late[:, 0:3, :], w1_words, 1, E)
+        load_words(late[:, 6:12, :], w2t_words, 1, E)
+        load_words(late[:, 3:6, :], w3_words, 1, E)
+        load_scales(w1ts, flat(w1t_scales))
+        load_scales(w3ts, flat(w3t_scales))
+        load_words(late[:, 12:16, :], w1t_words, 0, E)
+        load_words(late[:, 16:20, :], w3t_words, 0, E)
+        w1 = [early[:, 0, :]] + [late[:, e, :] for e in range(3)]
+        w3 = [early[:, 1, :]] + [late[:, 3 + e, :] for e in range(3)]
+        w2t = [early[:, 2, :], early[:, 3, :]] + [late[:, 6 + g, :] for g in range(6)]
+        w1t = late[:, 12:16, :]
+        w3t = late[:, 16:20, :]
 
         slots = {}
 
@@ -123,13 +126,13 @@ def tile_moe_rec_glu_sigmoid_kernel(tc, x_words, x_scales, dy_words, dy_scales, 
             e = c // 2
             xg, xgs, dyg = slots[e]
             cols = slice((c % 2) * P, (c % 2 + 1) * P)
-            a1 = psum.tile([P, H], F32, name="a1", tag="a1", bufs=2)
+            a1 = psum.tile([P, H], F32, name="a1", tag="a1", bufs=1)
             a3 = psum.tile([P, H], F32, name="a3", tag="a3", bufs=2)
             dh = psum.tile([P, H], F32, name="dh", tag="dh", bufs=2)
-            nc.tensor.matmul_mx(a1[:], xg[:, cols].bitcast(FP8X4), xgs[:, cols], w1[:, e, :].bitcast(FP4X4), w1s[:, e, :], start=True, stop=True)
+            nc.tensor.matmul_mx(a1[:], xg[:, cols].bitcast(FP8X4), xgs[:, cols], w1[e].bitcast(FP4X4), w1s[:, e, :], start=True, stop=True)
             for s, plane in enumerate((dys_both, dys_second)):
-                nc.tensor.matmul_mx(dh[:], dyg[s][:, cols].bitcast(FP8X4), plane[:, c * P:(c + 1) * P], w2t[:, 2 * e + s, :].bitcast(FP4X4), w2ts[:, 2 * e + s, :], start=(s == 0), stop=(s == 1))
-            nc.tensor.matmul_mx(a3[:], xg[:, cols].bitcast(FP8X4), xgs[:, cols], w3[:, e, :].bitcast(FP4X4), w3s[:, e, :], start=True, stop=True)
+                nc.tensor.matmul_mx(dh[:], dyg[s][:, cols].bitcast(FP8X4), plane[:, c * P:(c + 1) * P], w2t[2 * e + s].bitcast(FP4X4), w2ts[:, 2 * e + s, :], start=(s == 0), stop=(s == 1))
+            nc.tensor.matmul_mx(a3[:], xg[:, cols].bitcast(FP8X4), xgs[:, cols], w3[e].bitcast(FP4X4), w3s[:, e, :], start=True, stop=True)
             sig = work.tile([P, H], F32, name="sig")
             nc.scalar.activation(sig[:], a1[:], ACT.Sigmoid)
             return sig, a3, dh
@@ -155,7 +158,7 @@ def tile_moe_rec_glu_sigmoid_kernel(tc, x_words, x_scales, dy_words, dy_scales, 
         def turn(engine, neg3, negq, da):
             engine.tensor_tensor(in_pairs(da[:, 0, :]), by_pairs(neg3[:]), by_pairs(negq[:]), ALU.mult)
             words = da[:].rearrange("p a i -> p (a i)").bitcast(F32)
-            turned = psum.tile([P, 4, P], F32, name="turned", tag="turn", bufs=1)
+            turned = psum.tile([P, 4, P], F32, name="turned", tag="turn", bufs=2)
             for j in (2, 3, 0, 1):
                 nc.tensor.transpose(turned[:, j, :], words[:, j * P:(j + 1) * P], ident[:])
             grouped = work.tile([P, 2 * 4 * P], BF16, name="grouped", align_bytes=64)
@@ -167,52 +170,53 @@ def tile_moe_rec_glu_sigmoid_kernel(tc, x_words, x_scales, dy_words, dy_scales, 
             for a, (w, ws) in enumerate(((w1t, w1ts), (w3t, w3ts))):
                 nc.tensor.matmul_mx(acc, w[:, e, 2 * P * kt:2 * P * (kt + 1)].bitcast(FP4X4), ws[:, e, P * kt:P * (kt + 1)], codes[c][:, a * P:(a + 1) * P].bitcast(FP8X4), scales[c][:, a * P:(a + 1) * P], start=(a == 0), stop=(a == 1))
 
-        runs = {0: 4, 4: 3, 7: 1}
-        bank = {}
+        def four(kt, tag, bufs):
+            acc = psum.tile([P, 4 * P], F32, name="four", tag=tag, bufs=bufs)
+            for c in range(4):
+                back(acc[:, c * P:(c + 1) * P], kt, c)
+            nc.scalar.copy(dx[:, kt, 0:4 * P], acc[:])
+
+        def whole(c, kts, tag):
+            acc = psum.tile([P, len(kts), P], F32, name="whole", tag=tag, bufs=1)
+            for n, kt in enumerate(kts):
+                back(acc[:, n, :], kt, c)
+            nc.scalar.copy(dx[:, kts[0]:kts[-1] + 1, c * P:(c + 1) * P], acc[:])
 
         def backward(c, grouped):
             nc.vector.quantize_mx(codes[c][:].bitcast(FP8X4), scales[c][:], grouped[:])
-            start = max(r for r in runs if r <= c)
-            if c == start:
-                bank.setdefault(start, psum.tile([P, runs[start] * P], F32, name="acc", tag="acc", bufs=1))
-            back(bank[start][:, (c - start) * P:(c - start + 1) * P], 0, c)
-            if c == start + runs[start] - 1:
-                nc.scalar.copy(dx[0][:, start * P:(c + 1) * P], bank[start][:])
+            if c < 4:
+                if c == 3:
+                    four(0, "acc", 1)
+            elif c < TILES - 1:
+                whole(c, [0, 1, 2, 3], "a1" if c == 5 else "acc")
+            else:
+                whole(c, [0], "a1")
+                whole(c, [1, 2, 3], "acc")
 
-        head = gathers(0)
-        head[0]()
-        nc.vector.tensor_copy(dys_both[:], dys_win[:].indirect(offs_sb[:]))
-        for r in range(4):
-            nc.scalar.dma_start(dys_second[r:P:32, :].bitcast(I32), dys_both[4 + r:P:32, :].bitcast(I32))
-        for g in head[1:] + gathers(1):
+        for g in gathers(0) + gathers(1) + gathers(2):
             g()
-        share = [1,2,1,2,2,0,0,0]
+        share = [1,1,1,1,0,0,0,0]
         later = []
         sig, a3, dh = forward(0)
-        neg3, da = first_product(0, sig, dh)
-        waiting = None
+        waiting = []
         for c in range(TILES):
-            if c in (0, 3):
-                later = later + gathers(2 if c == 0 else 3)
+            if c == 0:
+                later = gathers(3)
+            neg3, da = first_product(c, sig, dh)
             negq = second_product(sig, a3)
             if c + 1 < TILES:
                 sig, a3, dh = forward(c + 1)
-            if waiting is not None:
-                backward(c - 1, waiting)
+            if c >= 2:
+                backward(c - 2, waiting[c - 2])
+            waiting.append(turn(nc.gpsimd if c < 7 else nc.vector, neg3, negq, da))
             for g in later[:share[c]]:
                 g()
             later = later[share[c]:]
-            waiting = turn(nc.vector, neg3, negq, da)
-            if c + 1 < TILES:
-                neg3, da = first_product(c + 1, sig, dh)
-        backward(TILES - 1, waiting)
+        for c in range(TILES - 2, TILES):
+            backward(c, waiting[c])
 
-        for kt in range(1, KT):
-            for half in range(2):
-                acc = psum.tile([P, 4 * P], F32, name="late", tag=("a1", "a3", "dh")[kt - 1], bufs=2)
-                for c in range(4 * half, 4 * half + 4):
-                    back(acc[:, (c % 4) * P:(c % 4 + 1) * P], kt, c)
-                nc.scalar.copy(dx[kt][:, half * 4 * P:(half + 1) * 4 * P], acc[:])
+        for kt, tag in ((1, "dh"), (2, "a3"), (3, "dh")):
+            four(kt, tag, 2)
 
         pieces = [(kt, 0, T) for kt in range(KT - 1)] + [(KT - 1, 0, T // 2), (KT - 1, T // 2, T)]
         pending = None
@@ -225,12 +229,12 @@ def tile_moe_rec_glu_sigmoid_kernel(tc, x_words, x_scales, dy_words, dy_scales, 
         for n, (kt, lo, hi) in enumerate(pieces):
             one = work.tile([P, hi - lo], F32, name="one")
             two = work.tile([P, hi - lo], F32, name="two")
-            nc.vector.tensor_copy(one[:], dx[kt][:].indirect(pos1_sb[:, lo // 16:hi // 16]))
+            nc.vector.tensor_copy(one[:], dx[:, kt, :].indirect(pos1_sb[:, lo // 16:hi // 16]))
             if pending is not None:
                 combine(nc.vector, *pending)
-            nc.vector.tensor_copy(two[:], dx[kt][:].indirect(pos2_sb[:, lo // 16:hi // 16]))
+            nc.vector.tensor_copy(two[:], dx[:, kt, :].indirect(pos2_sb[:, lo // 16:hi // 16]))
             pending = (kt, lo, hi, one, two)
-            if n < 0:
+            if n < 4:
                 combine(nc.gpsimd, *pending)
                 pending = None
         combine(nc.vector, *pending)

@@ -27,7 +27,7 @@ def tile_moe_rec_glu_sigmoid_kernel(tc, x_words, x_scales, dy_words, dy_scales, 
     with ExitStack() as ctx:
         keep = ctx.enter_context(tc.tile_pool(name="keep", bufs=1))
         pair = ctx.enter_context(tc.tile_pool(name="pair", bufs=3))
-        work = ctx.enter_context(tc.tile_pool(name="work", bufs=4))
+        work = ctx.enter_context(tc.tile_pool(name="work", bufs=5))
         psum = ctx.enter_context(tc.psum_pool(name="psum", bufs=1))
 
         offs_sb = keep.tile([P, S // 16], U16, name="offs_sb")
@@ -57,8 +57,8 @@ def tile_moe_rec_glu_sigmoid_kernel(tc, x_words, x_scales, dy_words, dy_scales, 
         make_identity(nc, ident[:])
 
         def load_scales(plane, rows, queue=nc.sync):
-            for r in range(4):
-                queue.dma_start(plane[r:P:32].bitcast(I32), rows.bitcast(I32)[:, r:16:4, :].rearrange("g q c -> q g c"))
+            for q in range(4):
+                queue.dma_start(plane[32 * q:32 * q + 4].bitcast(I32), rows.bitcast(I32)[:, 4 * q:4 * q + 4, :].rearrange("g j c -> j g c"))
 
         def load_words(rows, words, first, last):
             nc.sync.dma_start(rows.bitcast(I32), words.bitcast(I32)[first:last].rearrange("e s p b -> p (e s) b"))
@@ -165,10 +165,21 @@ def tile_moe_rec_glu_sigmoid_kernel(tc, x_words, x_scales, dy_words, dy_scales, 
             nc.scalar.copy(grouped[:].bitcast(F32).rearrange("p (a s u) -> p a s u", a=2, u=2), turned[:].rearrange("p (a u) s -> p a s u", u=2))
             return grouped
 
+        def turn_last(neg3, negq, da):
+            words = da[:].rearrange("p a i -> p (a i)").bitcast(F32)
+            turned = psum.tile([P, 4, P], F32, name="turned", tag="turn", bufs=2)
+            grouped = work.tile([P, 2 * 4 * P], BF16, name="grouped", align_bytes=64)
+            nc.vector.tensor_tensor(in_pairs(da[:, 0, :]), by_pairs(neg3[:]), by_pairs(negq[:]), ALU.mult)
+            for a in (1, 0):
+                for j in (2 * a, 2 * a + 1):
+                    nc.tensor.transpose(turned[:, j, :], words[:, j * P:(j + 1) * P], ident[:])
+                nc.scalar.copy(grouped[:, a * 4 * P:(a + 1) * 4 * P].bitcast(F32).rearrange("p (s u) -> p s u", u=2), turned[:, 2 * a:2 * a + 2, :].rearrange("p u s -> p s u"))
+            return grouped
+
         def back(acc, kt, c):
             e = c // 2
-            for a, (w, ws) in enumerate(((w1t, w1ts), (w3t, w3ts))):
-                nc.tensor.matmul_mx(acc, w[:, e, 2 * P * kt:2 * P * (kt + 1)].bitcast(FP4X4), ws[:, e, P * kt:P * (kt + 1)], codes[c][:, a * P:(a + 1) * P].bitcast(FP8X4), scales[c][:, a * P:(a + 1) * P], start=(a == 0), stop=(a == 1))
+            for a, w, ws in ((1, w3t, w3ts), (0, w1t, w1ts)):
+                nc.tensor.matmul_mx(acc, w[:, e, 2 * P * kt:2 * P * (kt + 1)].bitcast(FP4X4), ws[:, e, P * kt:P * (kt + 1)], codes[c][:, a * P:(a + 1) * P].bitcast(FP8X4), scales[c][:, a * P:(a + 1) * P], start=(a == 1), stop=(a == 0))
 
         def four(kt, tag, bufs):
             acc = psum.tile([P, 4 * P], F32, name="four", tag=tag, bufs=bufs)
@@ -183,7 +194,11 @@ def tile_moe_rec_glu_sigmoid_kernel(tc, x_words, x_scales, dy_words, dy_scales, 
             nc.scalar.copy(dx[:, kts[0]:kts[-1] + 1, c * P:(c + 1) * P], acc[:])
 
         def backward(c, grouped):
-            nc.vector.quantize_mx(codes[c][:].bitcast(FP8X4), scales[c][:], grouped[:])
+            if c < TILES - 1:
+                nc.vector.quantize_mx(codes[c][:].bitcast(FP8X4), scales[c][:], grouped[:])
+            else:
+                for a in (1, 0):
+                    nc.vector.quantize_mx(codes[c][:, a * P:(a + 1) * P].bitcast(FP8X4), scales[c][:, a * P:(a + 1) * P], grouped[:, a * 4 * P:(a + 1) * 4 * P])
             if c < 4:
                 if c == 3:
                     four(0, "acc", 1)
@@ -193,26 +208,29 @@ def tile_moe_rec_glu_sigmoid_kernel(tc, x_words, x_scales, dy_words, dy_scales, 
                 whole(c, [0], "a1")
                 whole(c, [1, 2, 3], "acc")
 
-        for g in gathers(0) + gathers(1) + gathers(2):
+        for g in gathers(0) + gathers(1):
             g()
-        share = [1,1,1,1,0,0,0,0]
+        share = [2,1,2,1,2,0,0,0]
         later = []
         sig, a3, dh = forward(0)
         waiting = []
         for c in range(TILES):
-            if c == 0:
-                later = gathers(3)
+            if c in (0, 2):
+                later = later + gathers(2 if c == 0 else 3)
             neg3, da = first_product(c, sig, dh)
             negq = second_product(sig, a3)
             if c + 1 < TILES:
                 sig, a3, dh = forward(c + 1)
-            if c >= 2:
-                backward(c - 2, waiting[c - 2])
-            waiting.append(turn(nc.gpsimd if c < 7 else nc.vector, neg3, negq, da))
+            if c >= 3:
+                backward(c - 3, waiting[c - 3])
+            if c < TILES - 1:
+                waiting.append(turn(nc.gpsimd if c < 7 else nc.vector, neg3, negq, da))
+            else:
+                waiting.append(turn_last(neg3, negq, da))
             for g in later[:share[c]]:
                 g()
             later = later[share[c]:]
-        for c in range(TILES - 2, TILES):
+        for c in range(TILES - 3, TILES):
             backward(c, waiting[c])
 
         for kt, tag in ((1, "dh"), (2, "a3"), (3, "dh")):

@@ -7,8 +7,13 @@ K, T, E, C, H, N = 512, 512, 4, 256, 512, 1024
 S = E * C
 P = 128
 TILES = S // P
+LAST = TILES - 1
 KT = K // P
+ROW = 2 * H
 FLOPS = 2 * S * (2 * K * H + N * H + 2 * H * K)
+
+GATHERS_AFTER = (2, 1, 2, 1, 2, 0, 0, 0)
+LAG = 3
 
 F32 = mybir.dt.float32
 BF16 = mybir.dt.bfloat16
@@ -22,12 +27,15 @@ ALU = mybir.AluOpType
 ACT = mybir.ActivationFunctionType
 
 
-def tile_moe_rec_glu_sigmoid_kernel(tc, x_words, x_scales, dy_words, dy_scales, w1_words, w1_scales, w3_words, w3_scales, w2t_words, w2t_scales, w1t_words, w1t_scales, w3t_words, w3t_scales, gate, offs, pos1, pos2, out):
+def tile_moe_rec_glu_sigmoid_kernel(
+    tc, x_words, x_scales, dy_words, dy_scales, w1_words, w1_scales, w3_words, w3_scales, w2t_words, w2t_scales,
+    w1t_words, w1t_scales, w3t_words, w3t_scales, gate, offs, pos1, pos2, out,
+):
     nc = tc.nc
     with ExitStack() as ctx:
         keep = ctx.enter_context(tc.tile_pool(name="keep", bufs=1))
-        pair = ctx.enter_context(tc.tile_pool(name="pair", bufs=3))
-        work = ctx.enter_context(tc.tile_pool(name="work", bufs=5))
+        routed = ctx.enter_context(tc.tile_pool(name="routed", bufs=3))
+        work = ctx.enter_context(tc.tile_pool(name="work", bufs=LAG + 2))
         psum = ctx.enter_context(tc.psum_pool(name="psum", bufs=1))
 
         offs_sb = keep.tile([P, S // 16], U16, name="offs_sb")
@@ -39,7 +47,7 @@ def tile_moe_rec_glu_sigmoid_kernel(tc, x_words, x_scales, dy_words, dy_scales, 
         dys_win = keep.tile([P, 2 * S], U8, name="dys_win", tag="reused", align_bytes=64)
         dys_both = keep.tile([P, S], U8, name="dys_both", align_bytes=64)
         dys_second = keep.tile([P, S], U8, name="dys_second", align_bytes=64)
-        early = keep.tile([P, 4, 2 * H], U8, name="early", align_bytes=64)
+        early = keep.tile([P, 4, ROW], U8, name="early", align_bytes=64)
         w1s = keep.tile([P, E, H], U8, name="w1s", align_bytes=64)
         w3s = keep.tile([P, E, H], U8, name="w3s", align_bytes=64)
         w2ts = keep.tile([P, 2 * E, H], U8, name="w2ts", align_bytes=64)
@@ -56,14 +64,15 @@ def tile_moe_rec_glu_sigmoid_kernel(tc, x_words, x_scales, dy_words, dy_scales, 
             nc.vector.memset(plane[:].bitcast(I32), 0)
         make_identity(nc, ident[:])
 
-        def load_scales(plane, rows, queue=nc.sync):
+        def load_planes(planes, rows, queue):
             for q in range(4):
-                queue.dma_start(plane[32 * q:32 * q + 4].bitcast(I32), rows.bitcast(I32)[:, 4 * q:4 * q + 4, :].rearrange("g j c -> j g c"))
+                src = rows.bitcast(I32)[:, 4 * q:4 * q + 4, :].rearrange("g j c -> j g c")
+                queue.dma_start(planes[32 * q:32 * q + 4].bitcast(I32), src)
 
-        def load_words(rows, words, first, last):
-            nc.sync.dma_start(rows.bitcast(I32), words.bitcast(I32)[first:last].rearrange("e s p b -> p (e s) b"))
+        def load_words(dst, words, first, last):
+            nc.sync.dma_start(dst.bitcast(I32), words.bitcast(I32)[first:last].rearrange("e s p b -> p (e s) b"))
 
-        def flat(rows):
+        def all_passes(rows):
             return rows.rearrange("e s b c -> (e s) b c")
 
         nc.sync.dma_start(offs_sb[:], offs)
@@ -75,10 +84,10 @@ def tile_moe_rec_glu_sigmoid_kernel(tc, x_words, x_scales, dy_words, dy_scales, 
         load_words(early[:, 0:1, :], w1_words, 0, 1)
         load_words(early[:, 2:4, :], w2t_words, 0, 1)
         load_words(early[:, 1:2, :], w3_words, 0, 1)
-        load_scales(xs_win, x_scales)
-        load_scales(w2ts, flat(w2t_scales), nc.gpsimd)
-        load_scales(w1s, flat(w1_scales))
-        load_scales(w3s, flat(w3_scales), nc.sync)
+        load_planes(xs_win, x_scales, nc.sync)
+        load_planes(w2ts, all_passes(w2t_scales), nc.gpsimd)
+        load_planes(w1s, all_passes(w1_scales), nc.sync)
+        load_planes(w3s, all_passes(w3_scales), nc.sync)
         nc.sync.dma_start(pos1_sb[:], pos1)
         nc.sync.dma_start(pos2_sb[:], pos2)
 
@@ -89,37 +98,37 @@ def tile_moe_rec_glu_sigmoid_kernel(tc, x_words, x_scales, dy_words, dy_scales, 
         nc.tensor.transpose(gate_t[:, 0, :], gate_rows[:], ident[:])
         nc.vector.tensor_scalar(neg_gate[:], gate_t[:, 0, 0:TILES], -1.0, None, ALU.mult)
 
-        late = keep.tile([P, 24, 2 * H], U8, name="late", tag="reused", align_bytes=64)
+        late = keep.tile([P, 24, ROW], U8, name="late", tag="reused", align_bytes=64)
         w1ts = late[:, 20:22, :].rearrange("p a (b c) -> p (a b) c", b=2)
         w3ts = late[:, 22:24, :].rearrange("p a (b c) -> p (a b) c", b=2)
         nc.gpsimd.memset(late[:, 20:24, :].bitcast(I32), 0)
         load_words(late[:, 0:3, :], w1_words, 1, E)
         load_words(late[:, 6:12, :], w2t_words, 1, E)
         load_words(late[:, 3:6, :], w3_words, 1, E)
-        load_scales(w1ts, flat(w1t_scales))
-        load_scales(w3ts, flat(w3t_scales))
+        load_planes(w1ts, all_passes(w1t_scales), nc.sync)
+        load_planes(w3ts, all_passes(w3t_scales), nc.sync)
         load_words(late[:, 12:16, :], w1t_words, 0, E)
         load_words(late[:, 16:20, :], w3t_words, 0, E)
-        w1 = [early[:, 0, :]] + [late[:, e, :] for e in range(3)]
-        w3 = [early[:, 1, :]] + [late[:, 3 + e, :] for e in range(3)]
-        w2t = [early[:, 2, :], early[:, 3, :]] + [late[:, 6 + g, :] for g in range(6)]
+        w1 = [early[:, 0, :]] + [late[:, r, :] for r in range(0, 3)]
+        w3 = [early[:, 1, :]] + [late[:, r, :] for r in range(3, 6)]
+        w2t = [early[:, 2, :], early[:, 3, :]] + [late[:, r, :] for r in range(6, 12)]
         w1t = late[:, 12:16, :]
         w3t = late[:, 16:20, :]
 
         slots = {}
 
         def gathers(e):
-            xg = pair.tile([P, C], U32, name="xg", align_bytes=64)
-            xgs = pair.tile([P, C], U8, name="xgs", align_bytes=64)
-            dyg0 = pair.tile([P, C], U32, name="dyg0", align_bytes=64)
-            dyg1 = pair.tile([P, C], U32, name="dyg1", align_bytes=64)
+            xg = routed.tile([P, C], U32, name="xg", align_bytes=64)
+            xgs = routed.tile([P, C], U8, name="xgs", align_bytes=64)
+            dyg0 = routed.tile([P, C], U32, name="dyg0", align_bytes=64)
+            dyg1 = routed.tile([P, C], U32, name="dyg1", align_bytes=64)
             slots.setdefault(e, (xg, xgs, (dyg0, dyg1)))
-            lst = offs_sb[:, e * (C // 16):(e + 1) * (C // 16)]
+            entries = offs_sb[:, e * (C // 16):(e + 1) * (C // 16)]
             return [
-                lambda: nc.vector.tensor_copy(xg[:], x_win[:].bitcast(U32).indirect(lst)),
-                lambda: nc.vector.tensor_copy(xgs[:], xs_win[:, 0, :].indirect(lst)),
-                lambda: nc.vector.tensor_copy(dyg0[:], dy_win[:, 0, :].bitcast(U32).indirect(lst)),
-                lambda: nc.vector.tensor_copy(dyg1[:], dy_win[:, 1, :].bitcast(U32).indirect(lst)),
+                lambda: nc.vector.tensor_copy(xg[:], x_win[:].bitcast(U32).indirect(entries)),
+                lambda: nc.vector.tensor_copy(xgs[:], xs_win[:, 0, :].indirect(entries)),
+                lambda: nc.vector.tensor_copy(dyg0[:], dy_win[:, 0, :].bitcast(U32).indirect(entries)),
+                lambda: nc.vector.tensor_copy(dyg1[:], dy_win[:, 1, :].bitcast(U32).indirect(entries)),
             ]
 
         def forward(c):
@@ -129,130 +138,105 @@ def tile_moe_rec_glu_sigmoid_kernel(tc, x_words, x_scales, dy_words, dy_scales, 
             a1 = psum.tile([P, H], F32, name="a1", tag="a1", bufs=1)
             a3 = psum.tile([P, H], F32, name="a3", tag="a3", bufs=2)
             dh = psum.tile([P, H], F32, name="dh", tag="dh", bufs=2)
-            nc.tensor.matmul_mx(a1[:], xg[:, cols].bitcast(FP8X4), xgs[:, cols], w1[e].bitcast(FP4X4), w1s[:, e, :], start=True, stop=True)
+            tokens = xg[:, cols].bitcast(FP8X4)
+            nc.tensor.matmul_mx(a1[:], tokens, xgs[:, cols], w1[e].bitcast(FP4X4), w1s[:, e, :], start=True, stop=True)
             for s, plane in enumerate((dys_both, dys_second)):
-                nc.tensor.matmul_mx(dh[:], dyg[s][:, cols].bitcast(FP8X4), plane[:, c * P:(c + 1) * P], w2t[2 * e + s].bitcast(FP4X4), w2ts[:, 2 * e + s, :], start=(s == 0), stop=(s == 1))
-            nc.tensor.matmul_mx(a3[:], xg[:, cols].bitcast(FP8X4), xgs[:, cols], w3[e].bitcast(FP4X4), w3s[:, e, :], start=True, stop=True)
+                nc.tensor.matmul_mx(
+                    dh[:], dyg[s][:, cols].bitcast(FP8X4), plane[:, c * P:(c + 1) * P],
+                    w2t[2 * e + s].bitcast(FP4X4), w2ts[:, 2 * e + s, :], start=(s == 0), stop=(s == 1),
+                )
+            nc.tensor.matmul_mx(a3[:], tokens, xgs[:, cols], w3[e].bitcast(FP4X4), w3s[:, e, :], start=True, stop=True)
             sig = work.tile([P, H], F32, name="sig")
             nc.scalar.activation(sig[:], a1[:], ACT.Sigmoid)
             return sig, a3, dh
 
-        def by_pairs(ap):
-            return ap.rearrange("p (q u e) -> p u q e", u=2, e=2)
+        def by_pairs(natural):
+            return natural.rearrange("p (q u v) -> p u q v", u=2, v=2)
 
-        def in_pairs(ap):
-            return ap.rearrange("p (u q e) -> p u q e", u=2, e=2)
+        def in_pairs(placed):
+            return placed.rearrange("p (u q v) -> p u q v", u=2, v=2)
 
-        def first_product(c, sig, dh):
+        def products(c, sig, a3, dh):
             neg3 = work.tile([P, H], F32, name="neg3")
             da = work.tile([P, 2, H], BF16, name="da", align_bytes=64)
             nc.vector.scalar_tensor_tensor(neg3[:], dh[:], neg_gate[:, c:c + 1], sig[:], ALU.mult, ALU.mult)
             nc.scalar.activation(in_pairs(da[:, 1, :]), by_pairs(neg3[:]), ACT.Copy, scale=-1.0)
-            return neg3, da
-
-        def second_product(sig, a3):
             negq = work.tile([P, H], F32, name="negq")
             nc.vector.scalar_tensor_tensor(negq[:], sig[:], 1.0, a3[:], ALU.subtract, ALU.mult)
-            return negq
+            return neg3, negq, da
 
-        def turn(engine, neg3, negq, da):
+        def turn(c, neg3, negq, da):
+            engine = nc.vector if c == LAST else nc.gpsimd
             engine.tensor_tensor(in_pairs(da[:, 0, :]), by_pairs(neg3[:]), by_pairs(negq[:]), ALU.mult)
             words = da[:].rearrange("p a i -> p (a i)").bitcast(F32)
             turned = psum.tile([P, 4, P], F32, name="turned", tag="turn", bufs=2)
-            for j in (2, 3, 0, 1):
-                nc.tensor.transpose(turned[:, j, :], words[:, j * P:(j + 1) * P], ident[:])
             grouped = work.tile([P, 2 * 4 * P], BF16, name="grouped", align_bytes=64)
-            nc.scalar.copy(grouped[:].bitcast(F32).rearrange("p (a s u) -> p a s u", a=2, u=2), turned[:].rearrange("p (a u) s -> p a s u", u=2))
-            return grouped
-
-        def turn_last(neg3, negq, da):
-            words = da[:].rearrange("p a i -> p (a i)").bitcast(F32)
-            turned = psum.tile([P, 4, P], F32, name="turned", tag="turn", bufs=2)
-            grouped = work.tile([P, 2 * 4 * P], BF16, name="grouped", align_bytes=64)
-            nc.vector.tensor_tensor(in_pairs(da[:, 0, :]), by_pairs(neg3[:]), by_pairs(negq[:]), ALU.mult)
+            turned_words = turned[:].rearrange("p (a u) s -> p a s u", u=2)
+            grouped_words = grouped[:].bitcast(F32).rearrange("p (a s u) -> p a s u", a=2, u=2)
             for a in (1, 0):
                 for j in (2 * a, 2 * a + 1):
                     nc.tensor.transpose(turned[:, j, :], words[:, j * P:(j + 1) * P], ident[:])
-                nc.scalar.copy(grouped[:, a * 4 * P:(a + 1) * 4 * P].bitcast(F32).rearrange("p (s u) -> p s u", u=2), turned[:, 2 * a:2 * a + 2, :].rearrange("p u s -> p s u"))
+                if c == LAST:
+                    nc.scalar.copy(grouped_words[:, a], turned_words[:, a])
+            if c < LAST:
+                nc.scalar.copy(grouped_words, turned_words)
             return grouped
 
-        def back(acc, kt, c):
-            e = c // 2
-            for a, w, ws in ((1, w3t, w3ts), (0, w1t, w1ts)):
-                nc.tensor.matmul_mx(acc, w[:, e, 2 * P * kt:2 * P * (kt + 1)].bitcast(FP4X4), ws[:, e, P * kt:P * (kt + 1)], codes[c][:, a * P:(a + 1) * P].bitcast(FP8X4), scales[c][:, a * P:(a + 1) * P], start=(a == 1), stop=(a == 0))
+        def group(kt, tiles, tag, bufs):
+            acc = psum.tile([P, len(tiles) * P], F32, name="acc", tag=tag, bufs=bufs)
+            for n, c in enumerate(tiles):
+                e = c // 2
+                for a, w, ws in ((1, w3t, w3ts), (0, w1t, w1ts)):
+                    nc.tensor.matmul_mx(
+                        acc[:, n * P:(n + 1) * P], w[:, e, 2 * P * kt:2 * P * (kt + 1)].bitcast(FP4X4),
+                        ws[:, e, P * kt:P * (kt + 1)], codes[c][:, a * P:(a + 1) * P].bitcast(FP8X4),
+                        scales[c][:, a * P:(a + 1) * P], start=(a == 1), stop=(a == 0),
+                    )
+            nc.scalar.copy(dx[:, kt, tiles[0] * P:(tiles[-1] + 1) * P], acc[:])
 
-        def four(kt, tag, bufs):
-            acc = psum.tile([P, 4 * P], F32, name="four", tag=tag, bufs=bufs)
-            for c in range(4):
-                back(acc[:, c * P:(c + 1) * P], kt, c)
-            nc.scalar.copy(dx[:, kt, 0:4 * P], acc[:])
+        first_rows = {3: ([0, 1, 2, 3], "acc"), 6: ([4, 5, 6], "acc"), LAST: ([LAST], "a1")}
 
-        def whole(c, kts, tag):
-            acc = psum.tile([P, len(kts), P], F32, name="whole", tag=tag, bufs=1)
-            for n, kt in enumerate(kts):
-                back(acc[:, n, :], kt, c)
-            nc.scalar.copy(dx[:, kts[0]:kts[-1] + 1, c * P:(c + 1) * P], acc[:])
-
-        def backward(c, grouped):
-            if c < TILES - 1:
+        def quantise(c, grouped):
+            if c < LAST:
                 nc.vector.quantize_mx(codes[c][:].bitcast(FP8X4), scales[c][:], grouped[:])
             else:
                 for a in (1, 0):
-                    nc.vector.quantize_mx(codes[c][:, a * P:(a + 1) * P].bitcast(FP8X4), scales[c][:, a * P:(a + 1) * P], grouped[:, a * 4 * P:(a + 1) * 4 * P])
-            if c < 4:
-                if c == 3:
-                    four(0, "acc", 1)
-            elif c < TILES - 1:
-                whole(c, [0, 1, 2, 3], "a1" if c == 5 else "acc")
-            else:
-                whole(c, [0], "a1")
-                whole(c, [1, 2, 3], "acc")
+                    cols = slice(a * P, (a + 1) * P)
+                    nc.vector.quantize_mx(codes[c][:, cols].bitcast(FP8X4), scales[c][:, cols], grouped[:, a * 4 * P:(a + 1) * 4 * P])
+            if c in first_rows:
+                group(0, *first_rows[c], 1)
 
-        for g in gathers(0) + gathers(1):
-            g()
-        share = [2,1,2,1,2,0,0,0]
-        later = []
-        sig, a3, dh = forward(0)
-        waiting = []
+        for gather in gathers(0) + gathers(1):
+            gather()
+        to_gather = []
+        turned_tiles = []
+        ahead = forward(0)
         for c in range(TILES):
             if c in (0, 2):
-                later = later + gathers(2 if c == 0 else 3)
-            neg3, da = first_product(c, sig, dh)
-            negq = second_product(sig, a3)
-            if c + 1 < TILES:
-                sig, a3, dh = forward(c + 1)
-            if c >= 3:
-                backward(c - 3, waiting[c - 3])
-            if c < TILES - 1:
-                waiting.append(turn(nc.gpsimd if c < 7 else nc.vector, neg3, negq, da))
-            else:
-                waiting.append(turn_last(neg3, negq, da))
-            for g in later[:share[c]]:
-                g()
-            later = later[share[c]:]
-        for c in range(TILES - 3, TILES):
-            backward(c, waiting[c])
+                to_gather = to_gather + gathers(2 + c // 2)
+            made = products(c, *ahead)
+            if c < LAST:
+                ahead = forward(c + 1)
+            if c >= LAG:
+                quantise(c - LAG, turned_tiles[c - LAG])
+            turned_tiles.append(turn(c, *made))
+            for gather in to_gather[:GATHERS_AFTER[c]]:
+                gather()
+            to_gather = to_gather[GATHERS_AFTER[c]:]
+        for c in range(TILES - LAG, TILES):
+            quantise(c, turned_tiles[c])
 
-        for kt, tag in ((1, "dh"), (2, "a3"), (3, "dh")):
-            four(kt, tag, 2)
+        for kt in range(1, KT):
+            group(kt, [0, 1, 2, 3], "dh", 2)
+            group(kt, [4, 5, 6, 7], "a3", 2)
 
         pieces = [(kt, 0, T) for kt in range(KT - 1)] + [(KT - 1, 0, T // 2), (KT - 1, T // 2, T)]
-        pending = None
-
-        def combine(engine, kt, lo, hi, one, two):
-            total = work.tile([P, hi - lo], F32, name="total")
-            engine.tensor_tensor(total[:], one[:], two[:], ALU.add)
-            nc.sync.dma_start(out[kt * P:(kt + 1) * P, lo:hi], total[:])
-
         for n, (kt, lo, hi) in enumerate(pieces):
             one = work.tile([P, hi - lo], F32, name="one")
             two = work.tile([P, hi - lo], F32, name="two")
+            total = work.tile([P, hi - lo], F32, name="total")
             nc.vector.tensor_copy(one[:], dx[:, kt, :].indirect(pos1_sb[:, lo // 16:hi // 16]))
-            if pending is not None:
-                combine(nc.vector, *pending)
             nc.vector.tensor_copy(two[:], dx[:, kt, :].indirect(pos2_sb[:, lo // 16:hi // 16]))
-            pending = (kt, lo, hi, one, two)
-            if n < 4:
-                combine(nc.gpsimd, *pending)
-                pending = None
-        combine(nc.vector, *pending)
+            engine = nc.vector if n == len(pieces) - 1 else nc.gpsimd
+            engine.tensor_tensor(total[:], one[:], two[:], ALU.add)
+            nc.sync.dma_start(out[kt * P:(kt + 1) * P, lo:hi], total[:])

@@ -54,7 +54,7 @@ def tile_moe_rec_glu_sigmoid_kernel(
         gate_rows = keep.tile([P, P], F32, name="gate_rows")
         neg_gate = keep.tile([P, TILES], F32, name="neg_gate")
         ident = keep.tile([P, P], F32, name="ident")
-        dx = keep.tile([P, KT, S], F32, name="dx")
+        dx = [keep.tile([P, S], F32, name="dx%d" % kt) for kt in range(KT)]
         codes = [keep.tile([P, 2 * P], U32, name="codes%d" % c, align_bytes=64) for c in range(TILES)]
         scales = [keep.tile([P, 2 * P], U8, name="scales%d" % c, align_bytes=64) for c in range(TILES)]
 
@@ -192,7 +192,7 @@ def tile_moe_rec_glu_sigmoid_kernel(
                         ws[:, e, P * kt:P * (kt + 1)], codes[c][:, a * P:(a + 1) * P].bitcast(FP8X4),
                         scales[c][:, a * P:(a + 1) * P], start=(a == 1), stop=(a == 0),
                     )
-            nc.scalar.copy(dx[:, kt, tiles[0] * P:(tiles[-1] + 1) * P], acc[:])
+            nc.scalar.copy(dx[kt][:, tiles[0] * P:(tiles[-1] + 1) * P], acc[:])
 
         first_rows = {3: ([0, 1, 2, 3], "acc"), 6: ([4, 5, 6], "acc"), LAST: ([LAST], "a1")}
 
@@ -230,13 +230,13 @@ def tile_moe_rec_glu_sigmoid_kernel(
             group(kt, [0, 1, 2, 3], "dh", 2)
             group(kt, [4, 5, 6, 7], "a3", 2)
 
-        pieces = [(kt, 0, T) for kt in range(KT - 1)] + [(KT - 1, 0, T // 2), (KT - 1, T // 2, T)]
-        for n, (kt, lo, hi) in enumerate(pieces):
-            one = work.tile([P, hi - lo], F32, name="one")
-            two = work.tile([P, hi - lo], F32, name="two")
-            total = work.tile([P, hi - lo], F32, name="total")
-            nc.vector.tensor_copy(one[:], dx[:, kt, :].indirect(pos1_sb[:, lo // 16:hi // 16]))
-            nc.vector.tensor_copy(two[:], dx[:, kt, :].indirect(pos2_sb[:, lo // 16:hi // 16]))
-            engine = nc.vector if n == len(pieces) - 1 else nc.gpsimd
-            engine.tensor_tensor(total[:], one[:], two[:], ALU.add)
-            nc.sync.dma_start(out[kt * P:(kt + 1) * P, lo:hi], total[:])
+        halves = [slice(0, T // 2), slice(T // 2, T)]
+        entries = [slice(0, T // 32), slice(T // 32, T // 16)]
+        for kt in range(KT):
+            one = work.tile([P, T], F32, name="one")
+            for h in range(2):
+                nc.vector.tensor_copy(one[:, halves[h]], dx[kt][:].indirect(pos1_sb[:, entries[h]]))
+            for h in range(2):
+                total = work.tile([P, T // 2], F32, name="total")
+                nc.vector.tensor_tensor(total[:], dx[kt][:].indirect(pos2_sb[:, entries[h]]), one[:, halves[h]], ALU.add)
+                nc.sync.dma_start(out[kt * P:(kt + 1) * P, halves[h]], total[:])

@@ -12,8 +12,10 @@ KT = K // P
 ROW = 2 * H
 FLOPS = 2 * S * (2 * K * H + N * H + 2 * H * K)
 
-GATHERS_AFTER = (2, 1, 2, 1, 2, 0, 0, 0)
-LAG = 3
+FIRST = C
+CALLS = ((0, 8), (8, 12), (12, 14), (15, 16), (14, 15))
+WIDE = 1024
+WIDEST = 1408
 
 F32 = mybir.dt.float32
 BF16 = mybir.dt.bfloat16
@@ -34,20 +36,25 @@ def tile_moe_rec_glu_sigmoid_kernel(
     nc = tc.nc
     with ExitStack() as ctx:
         keep = ctx.enter_context(tc.tile_pool(name="keep", bufs=1))
-        routed = ctx.enter_context(tc.tile_pool(name="routed", bufs=3))
-        work = ctx.enter_context(tc.tile_pool(name="work", bufs=LAG + 2))
+        work = ctx.enter_context(tc.tile_pool(name="work", bufs=5))
         psum = ctx.enter_context(tc.psum_pool(name="psum", bufs=1))
 
         offs_sb = keep.tile([P, S // 16], U16, name="offs_sb")
         pos1_sb = keep.tile([P, T // 16], U16, name="pos1_sb")
         pos2_sb = keep.tile([P, T // 16], U16, name="pos2_sb")
-        x_win = keep.tile([P, T], I32, name="x_win", align_bytes=64)
-        dy_win = keep.tile([P, 2, T], I32, name="dy_win", align_bytes=64)
-        xs_win = keep.tile([P, 1, T], U8, name="xs_win", align_bytes=64)
-        dys_win = keep.tile([P, 2 * S], U8, name="dys_win", tag="reused", align_bytes=64)
+        x_win = keep.tile([P, WIDEST], I32, name="x_win", align_bytes=64)
+        dy_win = keep.tile([P, T + WIDE], I32, name="dy_win", align_bytes=64)
+        xs_win = keep.tile([P, 1, WIDEST], U8, name="xs_win", align_bytes=64)
+        dys_win = keep.tile([P, WIDEST], U8, name="dys_win", tag="reused", align_bytes=64)
         dys_both = keep.tile([P, S], U8, name="dys_both", align_bytes=64)
         dys_second = keep.tile([P, S], U8, name="dys_second", align_bytes=64)
-        early = keep.tile([P, 4, ROW], U8, name="early", align_bytes=64)
+        dyg = [
+            [keep.tile([P, width], U32, name="dyg%d%d" % (part, s), align_bytes=64) for s in range(2)]
+            for part, width in enumerate((FIRST, S - FIRST))
+        ]
+        xg = keep.tile([P, S], U32, name="xg", align_bytes=64)
+        xgs = keep.tile([P, S], U8, name="xgs", align_bytes=64)
+        early = keep.tile([P, 10, ROW], U8, name="early", align_bytes=64)
         w1s = keep.tile([P, E, H], U8, name="w1s", align_bytes=64)
         w3s = keep.tile([P, E, H], U8, name="w3s", align_bytes=64)
         w2ts = keep.tile([P, 2 * E, H], U8, name="w2ts", align_bytes=64)
@@ -55,13 +62,16 @@ def tile_moe_rec_glu_sigmoid_kernel(
         neg_gate = keep.tile([P, TILES], F32, name="neg_gate")
         ident = keep.tile([P, P], F32, name="ident")
         dx = [keep.tile([P, S], F32, name="dx%d" % kt) for kt in range(KT)]
-        codes = [keep.tile([P, 2 * P], U32, name="codes%d" % c, align_bytes=64) for c in range(TILES)]
-        scales = [keep.tile([P, 2 * P], U8, name="scales%d" % c, align_bytes=64) for c in range(TILES)]
+        grouped = {
+            first: keep.tile([P, (last - first) * H], BF16, name="grouped%d" % first, align_bytes=64)
+            for first, last in CALLS
+        }
+        scales = keep.tile([P, TILES * 2 * P], U8, name="scales", align_bytes=64)
 
-        for plane in (dys_win[:, 0:T], xs_win[:], dys_win[:, T:]):
+        for plane in (xs_win[:, 0, 0:T], dys_win[:], w2ts[:]):
             nc.gpsimd.memset(plane.bitcast(I32), 0)
-        for plane in (w2ts, w1s, w3s, dys_second):
-            nc.vector.memset(plane[:].bitcast(I32), 0)
+        for plane in (x_win[:, T:], w1s[:].bitcast(I32), xs_win[:, 0, T:].bitcast(I32), w3s[:].bitcast(I32)):
+            nc.vector.memset(plane, 0)
         make_identity(nc, ident[:])
 
         def load_planes(planes, rows, queue):
@@ -76,79 +86,82 @@ def tile_moe_rec_glu_sigmoid_kernel(
             return rows.rearrange("e s b c -> (e s) b c")
 
         nc.sync.dma_start(offs_sb[:], offs)
+        nc.sync.dma_start(x_win[:, 0:T], x_words[0].rearrange("p t d -> p (t d)").bitcast(I32))
+        load_planes(xs_win[:, :, 0:T], x_scales, nc.sync)
         for q in range(4):
             nc.sync.dma_start(dys_win[32 * q:32 * q + 8, 0:T].bitcast(I32), dy_scales.bitcast(I32)[:, 4 * q:4 * q + 4, :])
+        nc.sync.dma_start(
+            dy_win[:, 0:2 * T].rearrange("p (s t) -> p s t", s=2), dy_words.rearrange("s p t d -> p s (t d)").bitcast(I32)
+        )
         nc.sync.dma_start(gate_rows[:], gate[0:P // TILES, :].rearrange("r (c m) -> (r c) m", m=P))
-        nc.sync.dma_start(x_win[:], x_words[0].rearrange("p t d -> p (t d)").bitcast(I32))
-        nc.sync.dma_start(dy_win[:], dy_words.rearrange("s p t d -> p s (t d)").bitcast(I32))
-        load_words(early[:, 0:1, :], w1_words, 0, 1)
-        load_words(early[:, 2:4, :], w2t_words, 0, 1)
-        load_words(early[:, 1:2, :], w3_words, 0, 1)
-        load_planes(xs_win, x_scales, nc.sync)
-        load_planes(w2ts, all_passes(w2t_scales), nc.gpsimd)
+        load_words(early[:, 0:4, :], w1_words, 0, E)
         load_planes(w1s, all_passes(w1_scales), nc.sync)
+        load_planes(w2ts, all_passes(w2t_scales), nc.gpsimd)
+        for spare in (dys_second[:].bitcast(I32), dy_win[:, 2 * T:]):
+            nc.gpsimd.memset(spare, 0)
+        load_words(early[:, 4:8, :], w2t_words, 0, 2)
+        load_words(early[:, 8:10, :], w3_words, 0, 2)
         load_planes(w3s, all_passes(w3_scales), nc.sync)
         nc.sync.dma_start(pos1_sb[:], pos1)
         nc.sync.dma_start(pos2_sb[:], pos2)
 
+        nc.vector.tensor_copy(xg[:], x_win[:].bitcast(U32).indirect(offs_sb[:]))
+        nc.vector.tensor_copy(xgs[:], xs_win[:, 0, :].indirect(offs_sb[:]))
         nc.vector.tensor_copy(dys_both[:], dys_win[:].indirect(offs_sb[:]))
         nc.scalar.dma_start(dys_second[0:100, :].bitcast(I32), dys_both[4:104, :].bitcast(I32))
 
         gate_t = psum.tile([P, 4, P], F32, name="gate_t", tag="turn", bufs=2)
         nc.tensor.transpose(gate_t[:, 0, :], gate_rows[:], ident[:])
-        nc.vector.tensor_scalar(neg_gate[:], gate_t[:, 0, 0:TILES], -1.0, None, ALU.mult)
+        nc.scalar.activation(neg_gate[:], gate_t[:, 0, 0:TILES], ACT.Copy, scale=-1.0)
 
-        late = keep.tile([P, 24, ROW], U8, name="late", tag="reused", align_bytes=64)
-        w1ts = late[:, 20:22, :].rearrange("p a (b c) -> p (a b) c", b=2)
-        w3ts = late[:, 22:24, :].rearrange("p a (b c) -> p (a b) c", b=2)
-        nc.gpsimd.memset(late[:, 20:24, :].bitcast(I32), 0)
-        load_words(late[:, 0:3, :], w1_words, 1, E)
-        load_words(late[:, 6:12, :], w2t_words, 1, E)
-        load_words(late[:, 3:6, :], w3_words, 1, E)
+        late = keep.tile([P, 18, ROW], U8, name="late", tag="reused", align_bytes=64)
+        w1ts, w3ts = [late[:, r:r + 2, :].rearrange("p a (b c) -> p (a b) c", b=2) for r in (14, 16)]
+        nc.gpsimd.memset(late[:, 14:18, :].bitcast(I32), 0)
+        load_words(late[:, 0:4, :], w2t_words, 2, E)
+        load_words(late[:, 4:6, :], w3_words, 2, E)
         load_planes(w1ts, all_passes(w1t_scales), nc.sync)
         load_planes(w3ts, all_passes(w3t_scales), nc.sync)
-        load_words(late[:, 12:16, :], w1t_words, 0, E)
-        load_words(late[:, 16:20, :], w3t_words, 0, E)
-        w1 = [early[:, 0, :]] + [late[:, r, :] for r in range(0, 3)]
-        w3 = [early[:, 1, :]] + [late[:, r, :] for r in range(3, 6)]
-        w2t = [early[:, 2, :], early[:, 3, :]] + [late[:, r, :] for r in range(6, 12)]
-        w1t = late[:, 12:16, :]
-        w3t = late[:, 16:20, :]
+        load_words(late[:, 6:10, :], w1t_words, 0, E)
+        load_words(late[:, 10:14, :], w3t_words, 0, E)
+        w1 = early[:, 0:4, :]
+        w2t = [early[:, r, :] for r in range(4, 8)] + [late[:, r, :] for r in range(0, 4)]
+        w3 = [early[:, 8, :], early[:, 9, :], late[:, 4, :], late[:, 5, :]]
+        w1t = late[:, 6:10, :]
+        w3t = late[:, 10:14, :]
 
-        slots = {}
+        for part, (lo, hi, width) in enumerate(((0, FIRST, T), (FIRST, S, WIDE))):
+            for s in range(2):
+                window = dy_win[:, s * T:s * T + width].bitcast(U32)
+                nc.vector.tensor_copy(dyg[part][s][:], window.indirect(offs_sb[:, lo // 16:hi // 16]))
 
-        def gathers(e):
-            xg = routed.tile([P, C], U32, name="xg", align_bytes=64)
-            xgs = routed.tile([P, C], U8, name="xgs", align_bytes=64)
-            dyg0 = routed.tile([P, C], U32, name="dyg0", align_bytes=64)
-            dyg1 = routed.tile([P, C], U32, name="dyg1", align_bytes=64)
-            slots.setdefault(e, (xg, xgs, (dyg0, dyg1)))
-            entries = offs_sb[:, e * (C // 16):(e + 1) * (C // 16)]
-            return [
-                lambda: nc.vector.tensor_copy(xg[:], x_win[:].bitcast(U32).indirect(entries)),
-                lambda: nc.vector.tensor_copy(xgs[:], xs_win[:, 0, :].indirect(entries)),
-                lambda: nc.vector.tensor_copy(dyg0[:], dy_win[:, 0, :].bitcast(U32).indirect(entries)),
-                lambda: nc.vector.tensor_copy(dyg1[:], dy_win[:, 1, :].bitcast(U32).indirect(entries)),
-            ]
+        def bank(name, turn_no):
+            return psum.tile([P, H], F32, name=name, tag="sums%d" % (turn_no % 4), bufs=1)
 
-        def forward(c):
+        def tokens(c):
+            return xg[:, c * P:(c + 1) * P].bitcast(FP8X4), xgs[:, c * P:(c + 1) * P]
+
+        def sigmoid(c):
+            a1 = psum.tile([P, H], F32, name="a1", tag="a1_%d" % (c % 2), bufs=1)
+            nc.tensor.matmul_mx(a1[:], *tokens(c), w1[:, c // 2, :].bitcast(FP4X4), w1s[:, c // 2, :], start=True, stop=True)
+            if c < LAST:
+                sig = work.tile([P, H], F32, name="sig", bufs=LAST)
+            else:
+                sig = keep.tile([P, H], F32, name="last_sig", tag="then_codes", align_bytes=64)
+            nc.scalar.activation(sig[:], a1[:], ACT.Sigmoid)
+            return sig
+
+        def sums(c):
             e = c // 2
-            xg, xgs, dyg = slots[e]
-            cols = slice((c % 2) * P, (c % 2 + 1) * P)
-            a1 = psum.tile([P, H], F32, name="a1", tag="a1", bufs=1)
-            a3 = psum.tile([P, H], F32, name="a3", tag="a3", bufs=2)
-            dh = psum.tile([P, H], F32, name="dh", tag="dh", bufs=2)
-            tokens = xg[:, cols].bitcast(FP8X4)
-            nc.tensor.matmul_mx(a1[:], tokens, xgs[:, cols], w1[e].bitcast(FP4X4), w1s[:, e, :], start=True, stop=True)
+            part, place = (0, c) if c * P < FIRST else (1, c - FIRST // P)
+            dh = bank("dh", 2 * c)
             for s, plane in enumerate((dys_both, dys_second)):
                 nc.tensor.matmul_mx(
-                    dh[:], dyg[s][:, cols].bitcast(FP8X4), plane[:, c * P:(c + 1) * P],
+                    dh[:], dyg[part][s][:, place * P:(place + 1) * P].bitcast(FP8X4), plane[:, c * P:(c + 1) * P],
                     w2t[2 * e + s].bitcast(FP4X4), w2ts[:, 2 * e + s, :], start=(s == 0), stop=(s == 1),
                 )
-            nc.tensor.matmul_mx(a3[:], tokens, xgs[:, cols], w3[e].bitcast(FP4X4), w3s[:, e, :], start=True, stop=True)
-            sig = work.tile([P, H], F32, name="sig")
-            nc.scalar.activation(sig[:], a1[:], ACT.Sigmoid)
-            return sig, a3, dh
+            a3 = bank("a3", 2 * c + 1)
+            nc.tensor.matmul_mx(a3[:], *tokens(c), w3[e].bitcast(FP4X4), w3s[:, e, :], start=True, stop=True)
+            return dh, a3
 
         def by_pairs(natural):
             return natural.rearrange("p (q u v) -> p u q v", u=2, v=2)
@@ -156,12 +169,12 @@ def tile_moe_rec_glu_sigmoid_kernel(
         def in_pairs(placed):
             return placed.rearrange("p (u q v) -> p u q v", u=2, v=2)
 
-        def products(c, sig, a3, dh):
+        def products(c, sig, dh, a3):
             neg3 = work.tile([P, H], F32, name="neg3")
+            negq = work.tile([P, H], F32, name="negq")
             da = work.tile([P, 2, H], BF16, name="da", align_bytes=64)
             nc.vector.scalar_tensor_tensor(neg3[:], dh[:], neg_gate[:, c:c + 1], sig[:], ALU.mult, ALU.mult)
             nc.scalar.activation(in_pairs(da[:, 1, :]), by_pairs(neg3[:]), ACT.Copy, scale=-1.0)
-            negq = work.tile([P, H], F32, name="negq")
             nc.vector.scalar_tensor_tensor(negq[:], sig[:], 1.0, a3[:], ALU.subtract, ALU.mult)
             return neg3, negq, da
 
@@ -170,65 +183,52 @@ def tile_moe_rec_glu_sigmoid_kernel(
             engine.tensor_tensor(in_pairs(da[:, 0, :]), by_pairs(neg3[:]), by_pairs(negq[:]), ALU.mult)
             words = da[:].rearrange("p a i -> p (a i)").bitcast(F32)
             turned = psum.tile([P, 4, P], F32, name="turned", tag="turn", bufs=2)
-            grouped = work.tile([P, 2 * 4 * P], BF16, name="grouped", align_bytes=64)
             turned_words = turned[:].rearrange("p (a u) s -> p a s u", u=2)
-            grouped_words = grouped[:].bitcast(F32).rearrange("p (a s u) -> p a s u", a=2, u=2)
             for a in (1, 0):
                 for j in (2 * a, 2 * a + 1):
                     nc.tensor.transpose(turned[:, j, :], words[:, j * P:(j + 1) * P], ident[:])
                 if c == LAST:
-                    nc.scalar.copy(grouped_words[:, a], turned_words[:, a])
+                    half = grouped[2 * c + a][:].bitcast(F32).rearrange("p (s u) -> p s u", u=2)
+                    nc.scalar.copy(half, turned_words[:, a])
             if c < LAST:
-                nc.scalar.copy(grouped_words, turned_words)
-            return grouped
+                first = max(f for f in grouped if f <= 2 * c)
+                both = grouped[first][:, (2 * c - first) * H:(2 * c + 2 - first) * H]
+                nc.scalar.copy(both.bitcast(F32).rearrange("p (a s u) -> p a s u", a=2, u=2), turned_words)
 
-        def group(kt, tiles, tag, bufs):
-            acc = psum.tile([P, len(tiles) * P], F32, name="acc", tag=tag, bufs=bufs)
+        def group(kt, tiles, tag):
+            acc = psum.tile([P, len(tiles) * P], F32, name="acc", tag=tag, bufs=1)
             for n, c in enumerate(tiles):
                 e = c // 2
                 for a, w, ws in ((1, w3t, w3ts), (0, w1t, w1ts)):
                     nc.tensor.matmul_mx(
                         acc[:, n * P:(n + 1) * P], w[:, e, 2 * P * kt:2 * P * (kt + 1)].bitcast(FP4X4),
-                        ws[:, e, P * kt:P * (kt + 1)], codes[c][:, a * P:(a + 1) * P].bitcast(FP8X4),
-                        scales[c][:, a * P:(a + 1) * P], start=(a == 1), stop=(a == 0),
+                        ws[:, e, P * kt:P * (kt + 1)], codes[:, (2 * c + a) * P:(2 * c + a + 1) * P].bitcast(FP8X4),
+                        scales[:, (2 * c + a) * P:(2 * c + a + 1) * P], start=(a == 1), stop=(a == 0),
                     )
             nc.scalar.copy(dx[kt][:, tiles[0] * P:(tiles[-1] + 1) * P], acc[:])
 
-        first_rows = {3: ([0, 1, 2, 3], "acc"), 6: ([4, 5, 6], "acc"), LAST: ([LAST], "a1")}
-
-        def quantise(c, grouped):
-            if c < LAST:
-                nc.vector.quantize_mx(codes[c][:].bitcast(FP8X4), scales[c][:], grouped[:])
-            else:
-                for a in (1, 0):
-                    cols = slice(a * P, (a + 1) * P)
-                    nc.vector.quantize_mx(codes[c][:, cols].bitcast(FP8X4), scales[c][:, cols], grouped[:, a * 4 * P:(a + 1) * 4 * P])
-            if c in first_rows:
-                group(0, *first_rows[c], 1)
-
-        for gather in gathers(0) + gathers(1):
-            gather()
-        to_gather = []
-        turned_tiles = []
-        ahead = forward(0)
+        ahead = [(sigmoid(c), *sums(c)) for c in range(2)]
         for c in range(TILES):
-            if c in (0, 2):
-                to_gather = to_gather + gathers(2 + c // 2)
-            made = products(c, *ahead)
-            if c < LAST:
-                ahead = forward(c + 1)
-            if c >= LAG:
-                quantise(c - LAG, turned_tiles[c - LAG])
-            turned_tiles.append(turn(c, *made))
-            for gather in to_gather[:GATHERS_AFTER[c]]:
-                gather()
-            to_gather = to_gather[GATHERS_AFTER[c]:]
-        for c in range(TILES - LAG, TILES):
-            quantise(c, turned_tiles[c])
+            made = products(c, *ahead[c])
+            if c + 2 < TILES:
+                ahead.append((sigmoid(c + 2), *sums(c + 2)))
+            turn(c, *made)
 
-        for kt in range(1, KT):
-            group(kt, [0, 1, 2, 3], "dh", 2)
-            group(kt, [4, 5, 6, 7], "a3", 2)
+        codes = keep.tile([P, TILES * 2 * P], U32, name="codes", tag="then_codes", align_bytes=64)
+
+        def quantise(first, last):
+            cols = slice(first * P, last * P)
+            nc.vector.quantize_mx(codes[:, cols].bitcast(FP8X4), scales[:, cols], grouped[first][:])
+
+        first_rows = {0: ([0, 1, 2, 3], "a1_0"), 12: ([4, 5, 6], "a1_1"), 14: ([LAST], "a1_0")}
+        for first, last in CALLS:
+            quantise(first, last)
+            if first in first_rows:
+                group(0, *first_rows[first])
+
+        for kt, first_bank, second_bank in ((1, "a1_1", "sums1"), (2, "a1_0", "sums2"), (3, "a1_1", "sums3")):
+            group(kt, [0, 1, 2, 3], first_bank)
+            group(kt, [4, 5, 6, 7], second_bank)
 
         halves = [slice(0, T // 2), slice(T // 2, T)]
         entries = [slice(0, T // 32), slice(T // 32, T // 16)]

@@ -59,7 +59,8 @@ def tile_moe_rec_glu_sigmoid_kernel(
         w3s = keep.tile([P, E, H], U8, name="w3s", align_bytes=64)
         w2ts = keep.tile([P, 2 * E, H], U8, name="w2ts", align_bytes=64)
         gate_rows = keep.tile([P, P], F32, name="gate_rows")
-        neg_gate = keep.tile([P, TILES], F32, name="neg_gate")
+        gates = keep.tile([P, TILES], F32, name="gates")
+        neg_gates = keep.tile([P, TILES], F32, name="neg_gates")
         ident = keep.tile([P, P], F32, name="ident")
         dx = [keep.tile([P, S], F32, name="dx%d" % kt) for kt in range(KT)]
         grouped = {
@@ -73,6 +74,8 @@ def tile_moe_rec_glu_sigmoid_kernel(
         for plane in (x_win[:, T:], w1s[:].bitcast(I32), xs_win[:, 0, T:].bitcast(I32), w3s[:].bitcast(I32)):
             nc.vector.memset(plane, 0)
         make_identity(nc, ident[:])
+        for spare in (dys_second[:].bitcast(I32), dy_win[:, 2 * T:]):
+            nc.gpsimd.memset(spare, 0)
 
         def load_planes(planes, rows, queue):
             for q in range(4):
@@ -97,8 +100,6 @@ def tile_moe_rec_glu_sigmoid_kernel(
         load_words(early[:, 0:4, :], w1_words, 0, E)
         load_planes(w1s, all_passes(w1_scales), nc.sync)
         load_planes(w2ts, all_passes(w2t_scales), nc.gpsimd)
-        for spare in (dys_second[:].bitcast(I32), dy_win[:, 2 * T:]):
-            nc.gpsimd.memset(spare, 0)
         load_words(early[:, 4:8, :], w2t_words, 0, 2)
         load_words(early[:, 8:10, :], w3_words, 0, 2)
         load_planes(w3s, all_passes(w3_scales), nc.sync)
@@ -108,11 +109,12 @@ def tile_moe_rec_glu_sigmoid_kernel(
         nc.vector.tensor_copy(xg[:], x_win[:].bitcast(U32).indirect(offs_sb[:]))
         nc.vector.tensor_copy(xgs[:], xs_win[:, 0, :].indirect(offs_sb[:]))
         nc.vector.tensor_copy(dys_both[:], dys_win[:].indirect(offs_sb[:]))
-        nc.scalar.dma_start(dys_second[0:100, :].bitcast(I32), dys_both[4:104, :].bitcast(I32))
+        nc.sync.dma_start(dys_second[0:100, :].bitcast(I32), dys_both[4:104, :].bitcast(I32))
 
         gate_t = psum.tile([P, 4, P], F32, name="gate_t", tag="turn", bufs=2)
         nc.tensor.transpose(gate_t[:, 0, :], gate_rows[:], ident[:])
-        nc.scalar.activation(neg_gate[:], gate_t[:, 0, 0:TILES], ACT.Copy, scale=-1.0)
+        nc.scalar.copy(gates[:], gate_t[:, 0, 0:TILES])
+        nc.scalar.activation(neg_gates[:], gate_t[:, 0, 0:TILES], ACT.Copy, scale=-1.0)
 
         late = keep.tile([P, 18, ROW], U8, name="late", tag="reused", align_bytes=64)
         w1ts, w3ts = [late[:, r:r + 2, :].rearrange("p a (b c) -> p (a b) c", b=2) for r in (14, 16)]
@@ -135,33 +137,10 @@ def tile_moe_rec_glu_sigmoid_kernel(
                 nc.vector.tensor_copy(dyg[part][s][:], window.indirect(offs_sb[:, lo // 16:hi // 16]))
 
         def bank(name, turn_no):
-            return psum.tile([P, H], F32, name=name, tag="sums%d" % (turn_no % 4), bufs=1)
+            return psum.tile([P, H], F32, name=name, tag="sums%d" % (turn_no % 6), bufs=1)
 
         def tokens(c):
             return xg[:, c * P:(c + 1) * P].bitcast(FP8X4), xgs[:, c * P:(c + 1) * P]
-
-        def sigmoid(c):
-            a1 = psum.tile([P, H], F32, name="a1", tag="a1_%d" % (c % 2), bufs=1)
-            nc.tensor.matmul_mx(a1[:], *tokens(c), w1[:, c // 2, :].bitcast(FP4X4), w1s[:, c // 2, :], start=True, stop=True)
-            if c < LAST:
-                sig = work.tile([P, H], F32, name="sig", bufs=LAST)
-            else:
-                sig = keep.tile([P, H], F32, name="last_sig", tag="then_codes", align_bytes=64)
-            nc.scalar.activation(sig[:], a1[:], ACT.Sigmoid)
-            return sig
-
-        def sums(c):
-            e = c // 2
-            part, place = (0, c) if c * P < FIRST else (1, c - FIRST // P)
-            dh = bank("dh", 2 * c)
-            for s, plane in enumerate((dys_both, dys_second)):
-                nc.tensor.matmul_mx(
-                    dh[:], dyg[part][s][:, place * P:(place + 1) * P].bitcast(FP8X4), plane[:, c * P:(c + 1) * P],
-                    w2t[2 * e + s].bitcast(FP4X4), w2ts[:, 2 * e + s, :], start=(s == 0), stop=(s == 1),
-                )
-            a3 = bank("a3", 2 * c + 1)
-            nc.tensor.matmul_mx(a3[:], *tokens(c), w3[e].bitcast(FP4X4), w3s[:, e, :], start=True, stop=True)
-            return dh, a3
 
         def by_pairs(natural):
             return natural.rearrange("p (q u v) -> p u q v", u=2, v=2)
@@ -169,18 +148,43 @@ def tile_moe_rec_glu_sigmoid_kernel(
         def in_pairs(placed):
             return placed.rearrange("p (u q v) -> p u q v", u=2, v=2)
 
-        def products(c, sig, dh, a3):
-            neg3 = work.tile([P, H], F32, name="neg3")
-            negq = work.tile([P, H], F32, name="negq")
-            da = work.tile([P, 2, H], BF16, name="da", align_bytes=64)
-            nc.vector.scalar_tensor_tensor(neg3[:], dh[:], neg_gate[:, c:c + 1], sig[:], ALU.mult, ALU.mult)
-            nc.scalar.activation(in_pairs(da[:, 1, :]), by_pairs(neg3[:]), ACT.Copy, scale=-1.0)
-            nc.vector.scalar_tensor_tensor(negq[:], sig[:], 1.0, a3[:], ALU.subtract, ALU.mult)
-            return neg3, negq, da
+        def sigmoid(c):
+            a1 = bank("a1", c)
+            nc.tensor.matmul_mx(a1[:], *tokens(c), w1[:, c // 2, :].bitcast(FP4X4), w1s[:, c // 2, :], start=True, stop=True)
+            sig = keep.tile([P, H], F32, name="sig%d" % c, align_bytes=64)
+            nc.scalar.activation(in_pairs(sig[:]), by_pairs(a1[:]), ACT.Sigmoid)
+            rest = keep.tile([P, H], F32, name="rest%d" % c, align_bytes=64)
+            if c < TILES - 2:
+                nc.gpsimd.tensor_scalar(rest[:], sig[:], neg_gates[:, c:c + 1], gates[:, c:c + 1], ALU.mult, ALU.add)
+            else:
+                nc.scalar.activation(rest[:], sig[:], ACT.Identity, bias=gates[:, c:c + 1], scale=neg_gates[:, c:c + 1])
+            return sig, rest
 
-        def turn(c, neg3, negq, da):
+        def sums(c):
+            e = c // 2
+            part, place = (0, c) if c * P < FIRST else (1, c - FIRST // P)
+            dh = bank("dh", TILES + 2 * c)
+            for s, plane in enumerate((dys_both, dys_second)):
+                nc.tensor.matmul_mx(
+                    dh[:], dyg[part][s][:, place * P:(place + 1) * P].bitcast(FP8X4), plane[:, c * P:(c + 1) * P],
+                    w2t[2 * e + s].bitcast(FP4X4), w2ts[:, 2 * e + s, :], start=(s == 0), stop=(s == 1),
+                )
+            a3 = bank("a3", TILES + 2 * c + 1)
+            nc.tensor.matmul_mx(a3[:], *tokens(c), w3[e].bitcast(FP4X4), w3s[:, e, :], start=True, stop=True)
+            return dh, a3
+
+        def products(c, sig, rest, dh, a3):
+            ungated = work.tile([P, H], F32, name="ungated")
+            factor = work.tile([P, H], F32, name="factor")
+            da = work.tile([P, 2, H], BF16, name="da", align_bytes=64)
+            nc.vector.tensor_tensor(in_pairs(ungated[:]), by_pairs(dh[:]), in_pairs(sig[:]), ALU.mult)
+            nc.scalar.activation(da[:, 1, :], ungated[:], ACT.Copy, scale=gates[:, c:c + 1])
+            nc.vector.tensor_tensor(in_pairs(factor[:]), by_pairs(a3[:]), in_pairs(rest[:]), ALU.mult)
+            return ungated, factor, da
+
+        def turn(c, ungated, factor, da):
             engine = nc.vector if c == LAST else nc.gpsimd
-            engine.tensor_tensor(in_pairs(da[:, 0, :]), by_pairs(neg3[:]), by_pairs(negq[:]), ALU.mult)
+            engine.tensor_tensor(da[:, 0, :], ungated[:], factor[:], ALU.mult)
             words = da[:].rearrange("p a i -> p (a i)").bitcast(F32)
             turned = psum.tile([P, 4, P], F32, name="turned", tag="turn", bufs=2)
             turned_words = turned[:].rearrange("p (a u) s -> p a s u", u=2)
@@ -202,31 +206,36 @@ def tile_moe_rec_glu_sigmoid_kernel(
                 for a, w, ws in ((1, w3t, w3ts), (0, w1t, w1ts)):
                     nc.tensor.matmul_mx(
                         acc[:, n * P:(n + 1) * P], w[:, e, 2 * P * kt:2 * P * (kt + 1)].bitcast(FP4X4),
-                        ws[:, e, P * kt:P * (kt + 1)], codes[:, (2 * c + a) * P:(2 * c + a + 1) * P].bitcast(FP8X4),
+                        ws[:, e, P * kt:P * (kt + 1)], codes[c // 4][:, (2 * (c % 4) + a) * P:(2 * (c % 4) + a + 1) * P].bitcast(FP8X4),
                         scales[:, (2 * c + a) * P:(2 * c + a + 1) * P], start=(a == 1), stop=(a == 0),
                     )
             nc.scalar.copy(dx[kt][:, tiles[0] * P:(tiles[-1] + 1) * P], acc[:])
 
-        ahead = [(sigmoid(c), *sums(c)) for c in range(2)]
-        for c in range(TILES):
-            made = products(c, *ahead[c])
-            if c + 2 < TILES:
-                ahead.append((sigmoid(c + 2), *sums(c + 2)))
-            turn(c, *made)
-
-        codes = keep.tile([P, TILES * 2 * P], U32, name="codes", tag="then_codes", align_bytes=64)
+        codes = [
+            keep.tile([P, 8 * P], U32, name="codes%d" % n, tag="rest%d" % c, align_bytes=64)
+            for n, c in enumerate((5, LAST))
+        ]
+        first_rows = {0: ([0, 1, 2, 3], "sums0"), 12: ([4, 5, 6], "sums1"), 14: ([LAST], "sums0")}
 
         def quantise(first, last):
-            cols = slice(first * P, last * P)
-            nc.vector.quantize_mx(codes[:, cols].bitcast(FP8X4), scales[:, cols], grouped[first][:])
-
-        first_rows = {0: ([0, 1, 2, 3], "a1_0"), 12: ([4, 5, 6], "a1_1"), 14: ([LAST], "a1_0")}
-        for first, last in CALLS:
-            quantise(first, last)
+            words = codes[first // 8][:, (first % 8) * P:(first % 8 + last - first) * P]
+            nc.vector.quantize_mx(words.bitcast(FP8X4), scales[:, first * P:last * P], grouped[first][:])
             if first in first_rows:
                 group(0, *first_rows[first])
 
-        for kt, first_bank, second_bank in ((1, "a1_1", "sums1"), (2, "a1_0", "sums2"), (3, "a1_1", "sums3")):
+        sigmoids = [sigmoid(c) for c in range(TILES)]
+        ahead = [sums(c) for c in range(3)]
+        for c in range(TILES):
+            made = products(c, *sigmoids[c], *ahead[c])
+            if c == 5:
+                quantise(*CALLS[0])
+            if c + 3 < TILES:
+                ahead.append(sums(c + 3))
+            turn(c, *made)
+        for call in CALLS[1:]:
+            quantise(*call)
+
+        for kt, first_bank, second_bank in ((1, "sums1", "sums2"), (2, "sums0", "sums3"), (3, "sums1", "sums4")):
             group(kt, [0, 1, 2, 3], first_bank)
             group(kt, [4, 5, 6, 7], second_bank)
 

@@ -12,9 +12,8 @@ KT = K // P
 ROW = 2 * H
 FLOPS = 2 * S * (2 * K * H + N * H + 2 * H * K)
 
-FIRST = C
 CALLS = ((0, 8), (8, 12), (12, 14), (15, 16), (14, 15))
-WIDE = 1024
+WIDE = 704
 WIDEST = 1408
 
 F32 = mybir.dt.float32
@@ -48,10 +47,6 @@ def tile_moe_rec_glu_sigmoid_kernel(
         dys_win = keep.tile([P, WIDEST], U8, name="dys_win", tag="reused", align_bytes=64)
         dys_both = keep.tile([P, S], U8, name="dys_both", align_bytes=64)
         dys_second = keep.tile([P, S], U8, name="dys_second", align_bytes=64)
-        dyg = [
-            [keep.tile([P, width], U32, name="dyg%d%d" % (part, s), align_bytes=64) for s in range(2)]
-            for part, width in enumerate((FIRST, S - FIRST))
-        ]
         xg = keep.tile([P, S], U32, name="xg", align_bytes=64)
         xgs = keep.tile([P, S], U8, name="xgs", align_bytes=64)
         early = keep.tile([P, 10, ROW], U8, name="early", align_bytes=64)
@@ -131,10 +126,18 @@ def tile_moe_rec_glu_sigmoid_kernel(
         w1t = late[:, 6:10, :]
         w3t = late[:, 10:14, :]
 
-        for part, (lo, hi, width) in enumerate(((0, FIRST, T), (FIRST, S, WIDE))):
+        dyg = {}
+
+        def gather_gradients(first, last, s, tag):
+            words = keep.tile([P, (last - first) * C], U32, name="dyg%d%d" % (first, s), tag=tag, align_bytes=64)
+            window = dy_win[:, s * T:s * T + (T if last - first == 1 else WIDE)].bitcast(U32)
+            nc.vector.tensor_copy(words[:], window.indirect(offs_sb[:, first * (C // 16):last * (C // 16)]))
+            for c in range(2 * first, 2 * last):
+                dyg.setdefault((c, s), words[:, (c - 2 * first) * P:(c - 2 * first + 1) * P])
+
+        for first, last in ((0, 2), (2, 3)):
             for s in range(2):
-                window = dy_win[:, s * T:s * T + width].bitcast(U32)
-                nc.vector.tensor_copy(dyg[part][s][:], window.indirect(offs_sb[:, lo // 16:hi // 16]))
+                gather_gradients(first, last, s, "dyg%d%d" % (first, s))
 
         def bank(name, turn_no):
             return psum.tile([P, H], F32, name=name, tag="sums%d" % (turn_no % 6), bufs=1)
@@ -162,11 +165,10 @@ def tile_moe_rec_glu_sigmoid_kernel(
 
         def sums(c):
             e = c // 2
-            part, place = (0, c) if c * P < FIRST else (1, c - FIRST // P)
             dh = bank("dh", TILES + 2 * c)
             for s, plane in enumerate((dys_both, dys_second)):
                 nc.tensor.matmul_mx(
-                    dh[:], dyg[part][s][:, place * P:(place + 1) * P].bitcast(FP8X4), plane[:, c * P:(c + 1) * P],
+                    dh[:], dyg[(c, s)].bitcast(FP8X4), plane[:, c * P:(c + 1) * P],
                     w2t[2 * e + s].bitcast(FP4X4), w2ts[:, 2 * e + s, :], start=(s == 0), stop=(s == 1),
                 )
             a3 = bank("a3", TILES + 2 * c + 1)
@@ -206,19 +208,16 @@ def tile_moe_rec_glu_sigmoid_kernel(
                 for a, w, ws in ((1, w3t, w3ts), (0, w1t, w1ts)):
                     nc.tensor.matmul_mx(
                         acc[:, n * P:(n + 1) * P], w[:, e, 2 * P * kt:2 * P * (kt + 1)].bitcast(FP4X4),
-                        ws[:, e, P * kt:P * (kt + 1)], codes[c // 4][:, (2 * (c % 4) + a) * P:(2 * (c % 4) + a + 1) * P].bitcast(FP8X4),
+                        ws[:, e, P * kt:P * (kt + 1)], codes[:, (2 * c + a) * P:(2 * c + a + 1) * P].bitcast(FP8X4),
                         scales[:, (2 * c + a) * P:(2 * c + a + 1) * P], start=(a == 1), stop=(a == 0),
                     )
             nc.scalar.copy(dx[kt][:, tiles[0] * P:(tiles[-1] + 1) * P], acc[:])
 
-        codes = [
-            keep.tile([P, 8 * P], U32, name="codes%d" % n, tag="rest%d" % c, align_bytes=64)
-            for n, c in enumerate((5, LAST))
-        ]
-        first_rows = {0: ([0, 1, 2, 3], "sums0"), 12: ([4, 5, 6], "sums1"), 14: ([LAST], "sums0")}
+        codes = keep.tile([P, TILES * 2 * P], U32, name="codes", tag="rest%d" % LAST, align_bytes=64)
+        first_rows = {0: ([0, 1, 2, 3], "sums0"), 8: ([4, 5], "sums1"), 14: ([6, 7], "sums2")}
 
         def quantise(first, last):
-            words = codes[first // 8][:, (first % 8) * P:(first % 8 + last - first) * P]
+            words = codes[:, first * P:last * P]
             nc.vector.quantize_mx(words.bitcast(FP8X4), scales[:, first * P:last * P], grouped[first][:])
             if first in first_rows:
                 group(0, *first_rows[first])
@@ -227,17 +226,17 @@ def tile_moe_rec_glu_sigmoid_kernel(
         ahead = [sums(c) for c in range(3)]
         for c in range(TILES):
             made = products(c, *sigmoids[c], *ahead[c])
-            if c == 5:
-                quantise(*CALLS[0])
+            if c in (0, 2):
+                gather_gradients(E - 1, E, c // 2, "rest%d" % c)
             if c + 3 < TILES:
                 ahead.append(sums(c + 3))
             turn(c, *made)
-        for call in CALLS[1:]:
+        for call in CALLS:
             quantise(*call)
 
-        for kt, first_bank, second_bank in ((1, "sums1", "sums2"), (2, "sums0", "sums3"), (3, "sums1", "sums4")):
-            group(kt, [0, 1, 2, 3], first_bank)
-            group(kt, [4, 5, 6, 7], second_bank)
+        for kt in range(1, KT):
+            group(kt, [4, 5, 6, 7], "sums%d" % (kt + 2))
+            group(kt, [0, 1, 2, 3], "sums%d" % (kt + 1))
 
         halves = [slice(0, T // 2), slice(T // 2, T)]
         entries = [slice(0, T // 32), slice(T // 32, T // 16)]

@@ -54,7 +54,6 @@ def tile_moe_rec_glu_sigmoid_kernel(
         w3s = keep.tile([P, E, H], U8, name="w3s", align_bytes=64)
         w2ts = keep.tile([P, 2 * E, H], U8, name="w2ts", align_bytes=64)
         gate_rows = keep.tile([P, P], F32, name="gate_rows")
-        gates = keep.tile([P, TILES], F32, name="gates")
         neg_gates = keep.tile([P, TILES], F32, name="neg_gates")
         ident = keep.tile([P, P], F32, name="ident")
         dx = [keep.tile([P, S], F32, name="dx%d" % kt) for kt in range(KT)]
@@ -108,7 +107,6 @@ def tile_moe_rec_glu_sigmoid_kernel(
 
         gate_t = psum.tile([P, 4, P], F32, name="gate_t", tag="turn", bufs=2)
         nc.tensor.transpose(gate_t[:, 0, :], gate_rows[:], ident[:])
-        nc.scalar.copy(gates[:], gate_t[:, 0, 0:TILES])
         nc.scalar.activation(neg_gates[:], gate_t[:, 0, 0:TILES], ACT.Copy, scale=-1.0)
 
         late = keep.tile([P, 18, ROW], U8, name="late", tag="reused", align_bytes=64)
@@ -145,23 +143,12 @@ def tile_moe_rec_glu_sigmoid_kernel(
         def tokens(c):
             return xg[:, c * P:(c + 1) * P].bitcast(FP8X4), xgs[:, c * P:(c + 1) * P]
 
-        def by_pairs(natural):
-            return natural.rearrange("p (q u v) -> p u q v", u=2, v=2)
-
-        def in_pairs(placed):
-            return placed.rearrange("p (u q v) -> p u q v", u=2, v=2)
-
         def sigmoid(c):
             a1 = bank("a1", c)
             nc.tensor.matmul_mx(a1[:], *tokens(c), w1[:, c // 2, :].bitcast(FP4X4), w1s[:, c // 2, :], start=True, stop=True)
             sig = keep.tile([P, H], F32, name="sig%d" % c, align_bytes=64)
-            nc.scalar.activation(in_pairs(sig[:]), by_pairs(a1[:]), ACT.Sigmoid)
-            rest = keep.tile([P, H], F32, name="rest%d" % c, align_bytes=64)
-            if c < TILES - 2:
-                nc.gpsimd.tensor_scalar(rest[:], sig[:], neg_gates[:, c:c + 1], gates[:, c:c + 1], ALU.mult, ALU.add)
-            else:
-                nc.scalar.activation(rest[:], sig[:], ACT.Identity, bias=gates[:, c:c + 1], scale=neg_gates[:, c:c + 1])
-            return sig, rest
+            nc.scalar.activation(sig[:], a1[:], ACT.Sigmoid)
+            return sig
 
         def sums(c):
             e = c // 2
@@ -175,24 +162,24 @@ def tile_moe_rec_glu_sigmoid_kernel(
             nc.tensor.matmul_mx(a3[:], *tokens(c), w3[e].bitcast(FP4X4), w3s[:, e, :], start=True, stop=True)
             return dh, a3
 
-        def products(c, sig, rest, dh, a3):
-            ungated = work.tile([P, H], F32, name="ungated")
-            factor = work.tile([P, H], F32, name="factor")
+        def products(c, sig, dh, a3):
+            neg3 = work.tile([P, H], F32, name="neg3")
+            negq = work.tile([P, H], F32, name="negq")
             da = work.tile([P, 2, H], BF16, name="da", align_bytes=64)
-            nc.vector.tensor_tensor(in_pairs(ungated[:]), by_pairs(dh[:]), in_pairs(sig[:]), ALU.mult)
-            nc.scalar.activation(da[:, 1, :], ungated[:], ACT.Copy, scale=gates[:, c:c + 1])
-            nc.vector.tensor_tensor(in_pairs(factor[:]), by_pairs(a3[:]), in_pairs(rest[:]), ALU.mult)
-            return ungated, factor, da
+            nc.vector.scalar_tensor_tensor(neg3[:], dh[:], neg_gates[:, c:c + 1], sig[:], ALU.mult, ALU.mult)
+            nc.scalar.activation(da[:, 1, :], neg3[:], ACT.Copy, scale=-1.0)
+            nc.vector.scalar_tensor_tensor(negq[:], sig[:], 1.0, a3[:], ALU.subtract, ALU.mult)
+            return neg3, negq, da
 
-        def turn(c, ungated, factor, da):
+        def turn(c, neg3, negq, da):
             engine = nc.vector if c == LAST else nc.gpsimd
-            engine.tensor_tensor(da[:, 0, :], ungated[:], factor[:], ALU.mult)
+            engine.tensor_tensor(da[:, 0, :], neg3[:], negq[:], ALU.mult)
             words = da[:].rearrange("p a i -> p (a i)").bitcast(F32)
             turned = psum.tile([P, 4, P], F32, name="turned", tag="turn", bufs=2)
             turned_words = turned[:].rearrange("p (a u) s -> p a s u", u=2)
             for a in (1, 0):
-                for j in (2 * a, 2 * a + 1):
-                    nc.tensor.transpose(turned[:, j, :], words[:, j * P:(j + 1) * P], ident[:])
+                for u in range(2):
+                    nc.tensor.transpose(turned[:, 2 * a + u, :], words[:, 2 * a * P + u:2 * (a + 1) * P:2], ident[:])
                 if c == LAST:
                     half = grouped[2 * c + a][:].bitcast(F32).rearrange("p (s u) -> p s u", u=2)
                     nc.scalar.copy(half, turned_words[:, a])
@@ -213,7 +200,7 @@ def tile_moe_rec_glu_sigmoid_kernel(
                     )
             nc.scalar.copy(dx[kt][:, tiles[0] * P:(tiles[-1] + 1) * P], acc[:])
 
-        codes = keep.tile([P, TILES * 2 * P], U32, name="codes", tag="rest%d" % LAST, align_bytes=64)
+        codes = keep.tile([P, TILES * 2 * P], U32, name="codes", tag="sig%d" % LAST, align_bytes=64)
         first_rows = {0: ([0, 1, 2, 3], "sums0"), 8: ([4, 5], "sums1"), 14: ([6, 7], "sums2")}
 
         def quantise(first, last):
@@ -225,9 +212,9 @@ def tile_moe_rec_glu_sigmoid_kernel(
         sigmoids = [sigmoid(c) for c in range(TILES)]
         ahead = [sums(c) for c in range(3)]
         for c in range(TILES):
-            made = products(c, *sigmoids[c], *ahead[c])
+            made = products(c, sigmoids[c], *ahead[c])
             if c in (0, 2):
-                gather_gradients(E - 1, E, c // 2, "rest%d" % c)
+                gather_gradients(E - 1, E, c // 2, "sig%d" % c)
             if c + 3 < TILES:
                 ahead.append(sums(c + 3))
             turn(c, *made)

@@ -63,9 +63,9 @@ def tile_moe_rec_glu_sigmoid_kernel(
         }
         scales = keep.tile([P, TILES * 2 * P], U8, name="scales", align_bytes=64)
 
-        for plane in (xs_win[:, 0, 0:T], dys_win[:], w2ts[:]):
+        for plane in (dys_win[:], xs_win[:], w2ts[:]):
             nc.gpsimd.memset(plane.bitcast(I32), 0)
-        for plane in (x_win[:, T:], w1s[:].bitcast(I32), xs_win[:, 0, T:].bitcast(I32), w3s[:].bitcast(I32)):
+        for plane in (x_win[:, T:], w1s[:].bitcast(I32), w3s[:].bitcast(I32)):
             nc.vector.memset(plane, 0)
         make_identity(nc, ident[:])
         for spare in (dys_second[:].bitcast(I32), dy_win[:, 2 * T:]):
@@ -84,9 +84,9 @@ def tile_moe_rec_glu_sigmoid_kernel(
 
         nc.sync.dma_start(offs_sb[:], offs)
         nc.sync.dma_start(x_win[:, 0:T], x_words[0].rearrange("p t d -> p (t d)").bitcast(I32))
-        load_planes(xs_win[:, :, 0:T], x_scales, nc.sync)
         for q in range(4):
             nc.sync.dma_start(dys_win[32 * q:32 * q + 8, 0:T].bitcast(I32), dy_scales.bitcast(I32)[:, 4 * q:4 * q + 4, :])
+        load_planes(xs_win[:, :, 0:T], x_scales, nc.sync)
         nc.sync.dma_start(
             dy_win[:, 0:2 * T].rearrange("p (s t) -> p s t", s=2), dy_words.rearrange("s p t d -> p s (t d)").bitcast(I32)
         )
@@ -101,9 +101,9 @@ def tile_moe_rec_glu_sigmoid_kernel(
         nc.sync.dma_start(pos2_sb[:], pos2)
 
         nc.vector.tensor_copy(xg[:], x_win[:].bitcast(U32).indirect(offs_sb[:]))
-        nc.vector.tensor_copy(xgs[:], xs_win[:, 0, :].indirect(offs_sb[:]))
         nc.vector.tensor_copy(dys_both[:], dys_win[:].indirect(offs_sb[:]))
-        nc.sync.dma_start(dys_second[0:100, :].bitcast(I32), dys_both[4:104, :].bitcast(I32))
+        nc.gpsimd.dma_start(dys_second[0:100, :].bitcast(I32), dys_both[4:104, :].bitcast(I32))
+        nc.vector.tensor_copy(xgs[:], xs_win[:, 0, :].indirect(offs_sb[:]))
 
         gate_t = psum.tile([P, 4, P], F32, name="gate_t", tag="turn", bufs=2)
         nc.tensor.transpose(gate_t[:, 0, :], gate_rows[:], ident[:])

@@ -13,6 +13,8 @@ ROW = 2 * H
 FLOPS = 2 * S * (2 * K * H + N * H + 2 * H * K)
 
 CALLS = ((0, 8), (8, 12), (12, 14), (15, 16), (14, 15))
+EARLY = 3
+XS_AT = 12288
 WIDE = 704
 WIDEST = 1408
 
@@ -35,20 +37,20 @@ def tile_moe_rec_glu_sigmoid_kernel(
     nc = tc.nc
     with ExitStack() as ctx:
         keep = ctx.enter_context(tc.tile_pool(name="keep", bufs=1))
+        placed = ctx.enter_context(tc.tile_pool(name="placed", bufs=1))
         work = ctx.enter_context(tc.tile_pool(name="work", bufs=5))
         psum = ctx.enter_context(tc.psum_pool(name="psum", bufs=1))
 
         offs_sb = keep.tile([P, S // 16], U16, name="offs_sb")
         pos1_sb = keep.tile([P, T // 16], U16, name="pos1_sb")
         pos2_sb = keep.tile([P, T // 16], U16, name="pos2_sb")
-        x_win = keep.tile([P, WIDEST], I32, name="x_win", align_bytes=64)
-        dy_win = keep.tile([P, T + WIDE], I32, name="dy_win", align_bytes=64)
-        xs_win = keep.tile([P, 1, WIDEST], U8, name="xs_win", align_bytes=64)
-        dys_win = keep.tile([P, WIDEST], U8, name="dys_win", tag="reused", align_bytes=64)
-        dys_both = keep.tile([P, S], U8, name="dys_both", align_bytes=64)
-        dys_second = keep.tile([P, S], U8, name="dys_second", align_bytes=64)
-        xg = keep.tile([P, S], U32, name="xg", align_bytes=64)
-        xgs = keep.tile([P, S], U8, name="xgs", align_bytes=64)
+        x_win = keep.tile([P, WIDE], I32, name="x_win", tag="x_win", align_bytes=64)
+        dy_win = keep.tile([P, 2 * T], I32, name="dy_win", align_bytes=64)
+        xs_win = placed.tile([P, 1, WIDE], U8, name="xs_win", align_bytes=64, offset=XS_AT)
+        xs_again = keep.tile([P, WIDE], U8, name="xs_again", align_bytes=64)
+        dys_win = placed.tile([P, WIDEST], U8, name="dys_win", align_bytes=64, offset=4 * T - 64)
+        dys_rows = placed.tile([P, S], U8, name="dys_rows", align_bytes=64, offset=XS_AT + 64 - S)
+        dys = keep.tile([P, 2, S], U8, name="dys", align_bytes=64)
         early = keep.tile([P, 10, ROW], U8, name="early", align_bytes=64)
         w1s = keep.tile([P, E, H], U8, name="w1s", align_bytes=64)
         w3s = keep.tile([P, E, H], U8, name="w3s", align_bytes=64)
@@ -63,18 +65,21 @@ def tile_moe_rec_glu_sigmoid_kernel(
         }
         scales = keep.tile([P, TILES * 2 * P], U8, name="scales", align_bytes=64)
 
-        for plane in (dys_win[:], xs_win[:], w2ts[:]):
+        for plane in (xs_win[:], dys_win[:], w1s[:]):
             nc.gpsimd.memset(plane.bitcast(I32), 0)
-        for plane in (x_win[:, T:], w1s[:].bitcast(I32), w3s[:].bitcast(I32)):
+        for plane in (w3s[:].bitcast(I32), x_win[:, T:], w2ts[:].bitcast(I32)):
             nc.vector.memset(plane, 0)
+        nc.gpsimd.dma_start(
+            dys_win[0:32, 0:T].bitcast(I32), dy_scales.bitcast(I32).rearrange("s b c -> b s c")
+        )
+        nc.gpsimd.dma_start(gate_rows[:], gate[0:P // TILES, :].rearrange("r (c m) -> (r c) m", m=P))
         make_identity(nc, ident[:])
-        for spare in (dys_second[:].bitcast(I32), dy_win[:, 2 * T:]):
-            nc.gpsimd.memset(spare, 0)
+        nc.gpsimd.memset(dys[:].bitcast(I32), 0)
 
-        def load_planes(planes, rows, queue):
+        def load_planes(planes, rows):
             for q in range(4):
                 src = rows.bitcast(I32)[:, 4 * q:4 * q + 4, :].rearrange("g j c -> j g c")
-                queue.dma_start(planes[32 * q:32 * q + 4].bitcast(I32), src)
+                nc.sync.dma_start(planes[32 * q:32 * q + 4].bitcast(I32), src)
 
         def load_words(dst, words, first, last):
             nc.sync.dma_start(dst.bitcast(I32), words.bitcast(I32)[first:last].rearrange("e s p b -> p (e s) b"))
@@ -84,98 +89,115 @@ def tile_moe_rec_glu_sigmoid_kernel(
 
         nc.sync.dma_start(offs_sb[:], offs)
         nc.sync.dma_start(x_win[:, 0:T], x_words[0].rearrange("p t d -> p (t d)").bitcast(I32))
-        for q in range(4):
-            nc.sync.dma_start(dys_win[32 * q:32 * q + 8, 0:T].bitcast(I32), dy_scales.bitcast(I32)[:, 4 * q:4 * q + 4, :])
-        load_planes(xs_win[:, :, 0:T], x_scales, nc.sync)
+        load_planes(xs_win[:, :, 0:T], x_scales)
+        load_words(early[:, 0:4, :], w1_words, 0, E)
+        load_words(early[:, 8:10, :], w3_words, 0, 2)
+        load_planes(w1s, all_passes(w1_scales))
+        load_planes(w3s, all_passes(w3_scales))
         nc.sync.dma_start(
             dy_win[:, 0:2 * T].rearrange("p (s t) -> p s t", s=2), dy_words.rearrange("s p t d -> p s (t d)").bitcast(I32)
         )
-        nc.sync.dma_start(gate_rows[:], gate[0:P // TILES, :].rearrange("r (c m) -> (r c) m", m=P))
-        load_words(early[:, 0:4, :], w1_words, 0, E)
-        load_planes(w1s, all_passes(w1_scales), nc.sync)
-        load_planes(w2ts, all_passes(w2t_scales), nc.gpsimd)
         load_words(early[:, 4:8, :], w2t_words, 0, 2)
-        load_words(early[:, 8:10, :], w3_words, 0, 2)
-        load_planes(w3s, all_passes(w3_scales), nc.sync)
+        load_planes(w2ts, all_passes(w2t_scales))
         nc.sync.dma_start(pos1_sb[:], pos1)
         nc.sync.dma_start(pos2_sb[:], pos2)
 
-        nc.vector.tensor_copy(xg[:], x_win[:].bitcast(U32).indirect(offs_sb[:]))
-        nc.vector.tensor_copy(dys_both[:], dys_win[:].indirect(offs_sb[:]))
-        nc.gpsimd.dma_start(dys_second[0:100, :].bitcast(I32), dys_both[4:104, :].bitcast(I32))
-        nc.vector.tensor_copy(xgs[:], xs_win[:, 0, :].indirect(offs_sb[:]))
+        halves_of_offs = [offs_sb[:, 0:S // 32], offs_sb[:, S // 32:S // 16]]
+        xg = [keep.tile([P, S // 2], U32, name="xg0", align_bytes=64)]
+        xgs = [keep.tile([P, S // 2], U8, name="xgs0", align_bytes=64)]
+        nc.vector.tensor_copy(xg[0][:], x_win[:].bitcast(U32).indirect(halves_of_offs[0]))
+        nc.vector.tensor_copy(xs_again[:].bitcast(I32), xs_win[:, 0, :].bitcast(I32))
+        nc.vector.tensor_copy(xgs[0][:], xs_win[:, 0, :].indirect(halves_of_offs[0]))
+        nc.vector.tensor_copy(dys_rows[:], dys_win[:].indirect(offs_sb[:]))
+        for q in range(4):
+            nc.sync.dma_start(dys[32 * q:32 * q + 4].bitcast(I32), dys_rows[8 * q:8 * q + 8, :].bitcast(I32))
+        dyg = {}
 
-        gate_t = psum.tile([P, 4, P], F32, name="gate_t", tag="turn", bufs=2)
-        nc.tensor.transpose(gate_t[:, 0, :], gate_rows[:], ident[:])
-        nc.scalar.activation(neg_gates[:], gate_t[:, 0, 0:TILES], ACT.Copy, scale=-1.0)
+        def gather_gradients(e, s, words):
+            window = dy_win[:, s * T:(s + 1) * T].bitcast(U32)
+            nc.vector.tensor_copy(words, window.indirect(offs_sb[:, e * (C // 16):(e + 1) * (C // 16)]))
+            for c in range(2):
+                dyg.setdefault((2 * e + c, s), words[:, c * P:(c + 1) * P])
 
-        late = keep.tile([P, 18, ROW], U8, name="late", tag="reused", align_bytes=64)
-        w1ts, w3ts = [late[:, r:r + 2, :].rearrange("p a (b c) -> p (a b) c", b=2) for r in (14, 16)]
-        nc.gpsimd.memset(late[:, 14:18, :].bitcast(I32), 0)
+        dyg_first = placed.tile([P, 2, C], U32, name="dyg_first", align_bytes=64, offset=XS_AT + 64)
+        for s in range(2):
+            gather_gradients(0, s, dyg_first[:, s, :])
+        xg.append(placed.tile([P, S // 2], U32, name="xg1", align_bytes=64, offset=0))
+        nc.vector.tensor_copy(xg[1][:], x_win[:].bitcast(U32).indirect(halves_of_offs[1]))
+        xgs.append(placed.tile([P, S // 2], U8, name="xgs1", align_bytes=64, offset=4 * T))
+        nc.vector.tensor_copy(xgs[1][:], xs_again[:].indirect(halves_of_offs[1]))
+        dyg_next = keep.tile([P, 2, C], U32, name="dyg_next", tag="x_win", align_bytes=64)
+        for s in range(2):
+            gather_gradients(1, s, dyg_next[:, s, :])
+
+        late = placed.tile([P, 6, ROW], U8, name="late", align_bytes=64, offset=5 * T)
+        back_planes = keep.tile([P, 2 * E, K], U8, name="back_planes", align_bytes=64)
+        w1ts, w3ts = back_planes[:, 0:E, :], back_planes[:, E:2 * E, :]
+        nc.gpsimd.memset(back_planes[:].bitcast(I32), 0)
         load_words(late[:, 0:4, :], w2t_words, 2, E)
         load_words(late[:, 4:6, :], w3_words, 2, E)
-        load_planes(w1ts, all_passes(w1t_scales), nc.sync)
-        load_planes(w3ts, all_passes(w3t_scales), nc.sync)
-        load_words(late[:, 6:10, :], w1t_words, 0, E)
-        load_words(late[:, 10:14, :], w3t_words, 0, E)
+        load_planes(w1ts, all_passes(w1t_scales))
+        load_planes(w3ts, all_passes(w3t_scales))
         w1 = early[:, 0:4, :]
         w2t = [early[:, r, :] for r in range(4, 8)] + [late[:, r, :] for r in range(0, 4)]
         w3 = [early[:, 8, :], early[:, 9, :], late[:, 4, :], late[:, 5, :]]
-        w1t = late[:, 6:10, :]
-        w3t = late[:, 10:14, :]
 
-        dyg = {}
+        taken = []
 
-        def gather_gradients(first, last, s, tag):
-            words = keep.tile([P, (last - first) * C], U32, name="dyg%d%d" % (first, s), tag=tag, align_bytes=64)
-            window = dy_win[:, s * T:s * T + (T if last - first == 1 else WIDE)].bitcast(U32)
-            nc.vector.tensor_copy(words[:], window.indirect(offs_sb[:, first * (C // 16):last * (C // 16)]))
-            for c in range(2 * first, 2 * last):
-                dyg.setdefault((c, s), words[:, (c - 2 * first) * P:(c - 2 * first + 1) * P])
-
-        for first, last in ((0, 2), (2, 3)):
-            for s in range(2):
-                gather_gradients(first, last, s, "dyg%d%d" % (first, s))
-
-        def bank(name, turn_no):
-            return psum.tile([P, H], F32, name=name, tag="sums%d" % (turn_no % 6), bufs=1)
+        def bank(name):
+            taken.append(name)
+            return psum.tile([P, H], F32, name=name, tag="sums%d" % (len(taken) % 6), bufs=1)
 
         def tokens(c):
-            return xg[:, c * P:(c + 1) * P].bitcast(FP8X4), xgs[:, c * P:(c + 1) * P]
+            cols = slice((c % 4) * P, (c % 4 + 1) * P)
+            return xg[c // 4][:, cols].bitcast(FP8X4), xgs[c // 4][:, cols]
 
-        def sigmoid(c):
-            a1 = bank("a1", c)
+        def rest(c, a1):
             nc.tensor.matmul_mx(a1[:], *tokens(c), w1[:, c // 2, :].bitcast(FP4X4), w1s[:, c // 2, :], start=True, stop=True)
-            sig = keep.tile([P, H], F32, name="sig%d" % c, align_bytes=64)
-            nc.scalar.activation(sig[:], a1[:], ACT.Sigmoid)
-            return sig
+            out_tile = keep.tile([P, H], F32, name="sig%d" % c, align_bytes=64)
+            nc.scalar.activation(out_tile[:], a1[:], ACT.Sigmoid, scale=-1.0)
+            return out_tile
 
-        def sums(c):
+        def sum_a3(c):
+            a3 = bank("a3")
+            nc.tensor.matmul_mx(a3[:], *tokens(c), w3[c // 2].bitcast(FP4X4), w3s[:, c // 2, :], start=True, stop=True)
+            return a3
+
+        def sum_dh(c):
             e = c // 2
-            dh = bank("dh", TILES + 2 * c)
-            for s, plane in enumerate((dys_both, dys_second)):
+            dh = bank("dh")
+            for s in range(2):
                 nc.tensor.matmul_mx(
-                    dh[:], dyg[(c, s)].bitcast(FP8X4), plane[:, c * P:(c + 1) * P],
+                    dh[:], dyg[(c, s)].bitcast(FP8X4), dys[:, s, c * P:(c + 1) * P],
                     w2t[2 * e + s].bitcast(FP4X4), w2ts[:, 2 * e + s, :], start=(s == 0), stop=(s == 1),
                 )
-            a3 = bank("a3", TILES + 2 * c + 1)
-            nc.tensor.matmul_mx(a3[:], *tokens(c), w3[e].bitcast(FP4X4), w3s[:, e, :], start=True, stop=True)
-            return dh, a3
+            return dh
 
-        def products(c, sig, dh, a3):
-            neg3 = work.tile([P, H], F32, name="neg3")
+        def token_factor_early(c):
+            a3 = sum_a3(c)
+            gated = keep.tile([P, H], F32, name="gated%d" % c, align_bytes=64)
+            negq = keep.tile([P, H], F32, name="negq%d" % c)
+            nc.scalar.activation(gated[:], a3[:], ACT.Copy, scale=neg_gates[:, c:c + 1])
+            nc.gpsimd.tensor_tensor(negq[:], gated[:], rests[c][:], ALU.mult)
+            return negq
+
+        def token_factor(c, a3):
             negq = work.tile([P, H], F32, name="negq")
+            nc.vector.scalar_tensor_tensor(negq[:], a3[:], neg_gates[:, c:c + 1], rests[c][:], ALU.mult, ALU.mult)
+            return negq
+
+        def gradient_factor(c, dh):
+            neg3 = work.tile([P, H], F32, name="neg3")
             da = work.tile([P, 2, H], BF16, name="da", align_bytes=64)
-            nc.vector.scalar_tensor_tensor(neg3[:], dh[:], neg_gates[:, c:c + 1], sig[:], ALU.mult, ALU.mult)
-            nc.scalar.activation(da[:, 1, :], neg3[:], ACT.Copy, scale=-1.0)
-            nc.vector.scalar_tensor_tensor(negq[:], sig[:], 1.0, a3[:], ALU.subtract, ALU.mult)
-            return neg3, negq, da
+            nc.vector.scalar_tensor_tensor(neg3[:], rests[c][:], 1.0, dh[:], ALU.subtract, ALU.mult)
+            nc.scalar.activation(da[:, 1, :], neg3[:], ACT.Copy, scale=neg_gates[:, c:c + 1])
+            return neg3, da
 
         def turn(c, neg3, negq, da):
             engine = nc.vector if c == LAST else nc.gpsimd
             engine.tensor_tensor(da[:, 0, :], neg3[:], negq[:], ALU.mult)
             words = da[:].rearrange("p a i -> p (a i)").bitcast(F32)
-            turned = psum.tile([P, 4, P], F32, name="turned", tag="turn", bufs=2)
+            turned = psum.tile([P, 4, P], F32, name="turned", tag="turn%d" % (c % 2), bufs=1)
             turned_words = turned[:].rearrange("p (a u) s -> p a s u", u=2)
             for a in (1, 0):
                 for u in range(2):
@@ -209,15 +231,42 @@ def tile_moe_rec_glu_sigmoid_kernel(
             if first in first_rows:
                 group(0, *first_rows[first])
 
-        sigmoids = [sigmoid(c) for c in range(TILES)]
-        ahead = [sums(c) for c in range(3)]
+        rests = [rest(0, psum.tile([P, H], F32, name="a1", tag="turn0", bufs=1))]
+        gate_t = psum.tile([P, 4, P], F32, name="gate_t", tag="turn0", bufs=1)
+        nc.tensor.transpose(gate_t[:, 0, :], gate_rows[:], ident[:])
+        nc.scalar.activation(neg_gates[:], gate_t[:, 0, 0:TILES], ACT.Copy, scale=-1.0)
+        negqs = {0: token_factor_early(0)}
+        for c in range(1, TILES):
+            if c == TILES // 2:
+                dhs = {n: sum_dh(n) for n in range(2)}
+            rests.append(rest(c, bank("a1")))
+            if c < EARLY:
+                negqs[c] = token_factor_early(c)
+
+        back = keep.tile([P, 8, ROW], U8, name="back", tag="gated%d" % (EARLY - 1), align_bytes=64)
+        load_words(back[:, 0:4, :], w1t_words, 0, E)
+        load_words(back[:, 4:8, :], w3t_words, 0, E)
+        w1t = back[:, 0:4, :]
+        w3t = back[:, 4:8, :]
+        a3s = {}
+        held = {1: [(2, 0, "sig0"), (2, 1, "sig1")], 2: [(3, 0, "sig2")], 4: [(3, 1, "sig3")]}
+        more = {
+            0: [("dh", 2)], 1: [("dh", 3), ("a3", 3), ("a3", 4), ("dh", 4), ("dh", 5)], 2: [("a3", 5)],
+            3: [("a3", 6)], 4: [("dh", 6), ("a3", 7), ("dh", 7)],
+        }
         for c in range(TILES):
-            made = products(c, sigmoids[c], *ahead[c])
-            if c in (0, 2):
-                gather_gradients(E - 1, E, c // 2, "sig%d" % c)
-            if c + 3 < TILES:
-                ahead.append(sums(c + 3))
-            turn(c, *made)
+            neg3, da = gradient_factor(c, dhs[c])
+            if c >= EARLY:
+                negqs[c] = token_factor(c, a3s[c])
+            for e, s, lender in held.get(c, []):
+                words = keep.tile([P, C], U32, name="dyg%d%d" % (e, s), tag=lender, align_bytes=64)
+                gather_gradients(e, s, words[:])
+            for kind, n in more.get(c, []):
+                if kind == "dh":
+                    dhs[n] = sum_dh(n)
+                else:
+                    a3s[n] = sum_a3(n)
+            turn(c, neg3, negqs[c], da)
         for call in CALLS:
             quantise(*call)
 

@@ -12,7 +12,7 @@ KT = K // P
 ROW = 2 * H
 FLOPS = 2 * S * (2 * K * H + N * H + 2 * H * K)
 
-CALLS = ((0, 8), (8, 12), (12, 14), (15, 16), (14, 15))
+CALLS = ((0, 4), (4, 8), (8, 12), (12, 14), (15, 16), (14, 15))
 EARLY = 3
 XS_AT = 12288
 WIDE = 704
@@ -55,7 +55,8 @@ def tile_moe_rec_glu_sigmoid_kernel(
         w1s = keep.tile([P, E, H], U8, name="w1s", align_bytes=64)
         w3s = keep.tile([P, E, H], U8, name="w3s", align_bytes=64)
         w2ts = keep.tile([P, 2 * E, H], U8, name="w2ts", align_bytes=64)
-        gate_rows = keep.tile([P, P], F32, name="gate_rows")
+        gate_rows = keep.tile([P, 32], F32, name="gate_rows", align_bytes=64)
+        gates = keep.tile([P, 32], F32, name="gates", align_bytes=64)
         neg_gates = keep.tile([P, TILES], F32, name="neg_gates")
         ident = keep.tile([P, P], F32, name="ident")
         dx = [keep.tile([P, S], F32, name="dx%d" % kt) for kt in range(KT)]
@@ -72,7 +73,6 @@ def tile_moe_rec_glu_sigmoid_kernel(
         nc.gpsimd.dma_start(
             dys_win[0:32, 0:T].bitcast(I32), dy_scales.bitcast(I32).rearrange("s b c -> b s c")
         )
-        nc.gpsimd.dma_start(gate_rows[:], gate[0:P // TILES, :].rearrange("r (c m) -> (r c) m", m=P))
         make_identity(nc, ident[:])
         nc.gpsimd.memset(dys[:].bitcast(I32), 0)
 
@@ -87,8 +87,11 @@ def tile_moe_rec_glu_sigmoid_kernel(
         def all_passes(rows):
             return rows.rearrange("e s b c -> (e s) b c")
 
-        nc.sync.dma_start(offs_sb[:], offs)
         nc.sync.dma_start(x_win[:, 0:T], x_words[0].rearrange("p t d -> p (t d)").bitcast(I32))
+        nc.sync.dma_start(offs_sb[:], offs)
+        nc.sync.dma_start(gate_rows[:], gate[0:4, :].rearrange("r (c b i) -> b (r c) i", b=4, i=32))
+        nc.vector.transpose(gates[:], gate_rows[:])
+        nc.gpsimd.tensor_scalar(neg_gates[:], gates[:, 0:TILES], -1.0, 0.0, ALU.mult, ALU.add)
         load_planes(xs_win[:, :, 0:T], x_scales)
         load_words(early[:, 0:4, :], w1_words, 0, E)
         load_words(early[:, 8:10, :], w3_words, 0, 2)
@@ -200,6 +203,9 @@ def tile_moe_rec_glu_sigmoid_kernel(
             turned = psum.tile([P, 4, P], F32, name="turned", tag="turn%d" % (c % 2), bufs=1)
             turned_words = turned[:].rearrange("p (a u) s -> p a s u", u=2)
             for a in (1, 0):
+                if c == LAST and a == 0:
+                    turned = psum.tile([P, 4, P], F32, name="turned", tag="sums3", bufs=1)
+                    turned_words = turned[:].rearrange("p (a u) s -> p a s u", u=2)
                 for u in range(2):
                     nc.tensor.transpose(turned[:, 2 * a + u, :], words[:, 2 * a * P + u:2 * (a + 1) * P:2], ident[:])
                 if c == LAST:
@@ -223,7 +229,7 @@ def tile_moe_rec_glu_sigmoid_kernel(
             nc.scalar.copy(dx[kt][:, tiles[0] * P:(tiles[-1] + 1) * P], acc[:])
 
         codes = keep.tile([P, TILES * 2 * P], U32, name="codes", tag="sig%d" % LAST, align_bytes=64)
-        first_rows = {0: ([0, 1, 2, 3], "sums0"), 8: ([4, 5], "sums1"), 14: ([6, 7], "sums2")}
+        first_rows = {4: ([0, 1, 2, 3], "sums0"), 12: ([4, 5, 6], "sums1"), 14: ([7], "sums2")}
 
         def quantise(first, last):
             words = codes[:, first * P:last * P]
@@ -232,9 +238,6 @@ def tile_moe_rec_glu_sigmoid_kernel(
                 group(0, *first_rows[first])
 
         rests = [rest(0, psum.tile([P, H], F32, name="a1", tag="turn0", bufs=1))]
-        gate_t = psum.tile([P, 4, P], F32, name="gate_t", tag="turn0", bufs=1)
-        nc.tensor.transpose(gate_t[:, 0, :], gate_rows[:], ident[:])
-        nc.scalar.activation(neg_gates[:], gate_t[:, 0, 0:TILES], ACT.Copy, scale=-1.0)
         negqs = {0: token_factor_early(0)}
         for c in range(1, TILES):
             if c == TILES // 2:
@@ -249,7 +252,7 @@ def tile_moe_rec_glu_sigmoid_kernel(
         w1t = back[:, 0:4, :]
         w3t = back[:, 4:8, :]
         a3s = {}
-        held = {1: [(2, 0, "sig0"), (2, 1, "sig1")], 2: [(3, 0, "sig2")], 4: [(3, 1, "sig3")]}
+        held = {1: [(2, 0, "sig0"), (2, 1, "sig1")], 3: [(3, 0, "sig2")], 4: [(3, 1, "sig3")]}
         more = {
             0: [("dh", 2)], 1: [("dh", 3), ("a3", 3), ("a3", 4), ("dh", 4), ("dh", 5)], 2: [("a3", 5)],
             3: [("a3", 6)], 4: [("dh", 6), ("a3", 7), ("dh", 7)],
@@ -274,13 +277,21 @@ def tile_moe_rec_glu_sigmoid_kernel(
             group(kt, [4, 5, 6, 7], "sums%d" % (kt + 2))
             group(kt, [0, 1, 2, 3], "sums%d" % (kt + 1))
 
-        halves = [slice(0, T // 2), slice(T // 2, T)]
-        entries = [slice(0, T // 32), slice(T // 32, T // 16)]
+        ones = [keep.tile([P, T], F32, name="one%d" % kt) for kt in range(KT)]
+
+        def first_slots(kt, lo, hi):
+            nc.vector.tensor_copy(ones[kt][:, lo:hi], dx[kt][:].indirect(pos1_sb[:, lo // 16:hi // 16]))
+
+        def second_slots(kt, lo, hi):
+            total = work.tile([P, hi - lo], F32, name="total")
+            nc.vector.tensor_tensor(total[:], dx[kt][:].indirect(pos2_sb[:, lo // 16:hi // 16]), ones[kt][:, lo:hi], ALU.add)
+            nc.sync.dma_start(out[kt * P:(kt + 1) * P, lo:hi], total[:])
+
         for kt in range(KT):
-            one = work.tile([P, T], F32, name="one")
-            for h in range(2):
-                nc.vector.tensor_copy(one[:, halves[h]], dx[kt][:].indirect(pos1_sb[:, entries[h]]))
-            for h in range(2):
-                total = work.tile([P, T // 2], F32, name="total")
-                nc.vector.tensor_tensor(total[:], dx[kt][:].indirect(pos2_sb[:, entries[h]]), one[:, halves[h]], ALU.add)
-                nc.sync.dma_start(out[kt * P:(kt + 1) * P, halves[h]], total[:])
+            first_slots(kt, 0, T // 2)
+            first_slots(kt, T // 2, T)
+            second_slots(kt, 0, T // 2)
+            if kt < KT - 1:
+                second_slots(kt, T // 2, T)
+        second_slots(KT - 1, T // 2, 3 * T // 4)
+        second_slots(KT - 1, 3 * T // 4, T)

@@ -13,8 +13,10 @@ ROW = 2 * H
 FLOPS = 2 * S * (2 * K * H + N * H + 2 * H * K)
 
 CALLS = ((0, 4), (4, 8), (8, 12), (12, 14), (15, 16), (14, 15))
-EARLY = 3
-XS_AT = 12288
+EARLY = 4
+DYS_AT = 6144
+GATE_AT = 12800
+DY0_AT = DYS_AT + 576
 WIDE = 704
 WIDEST = 1408
 
@@ -44,18 +46,19 @@ def tile_moe_rec_glu_sigmoid_kernel(
         offs_sb = keep.tile([P, S // 16], U16, name="offs_sb")
         pos1_sb = keep.tile([P, T // 16], U16, name="pos1_sb")
         pos2_sb = keep.tile([P, T // 16], U16, name="pos2_sb")
-        x_win = keep.tile([P, WIDE], I32, name="x_win", tag="x_win", align_bytes=64)
-        dy_win = keep.tile([P, 2 * T], I32, name="dy_win", align_bytes=64)
-        xs_win = placed.tile([P, 1, WIDE], U8, name="xs_win", align_bytes=64, offset=XS_AT)
-        xs_again = keep.tile([P, WIDE], U8, name="xs_again", align_bytes=64)
-        dys_win = placed.tile([P, WIDEST], U8, name="dys_win", align_bytes=64, offset=4 * T - 64)
-        dys_rows = placed.tile([P, S], U8, name="dys_rows", align_bytes=64, offset=XS_AT + 64 - S)
+        x_win = keep.tile([P, WIDE], I32, name="x_win", align_bytes=64)
+        dy_win = placed.tile([P, 2 * T], I32, name="dy_win", align_bytes=64, offset=GATE_AT + 64 - 8 * T)
+        xs_win = keep.tile([P, 1, WIDE], U8, name="xs_win", tag="xs_win", align_bytes=64)
+        dys_win = placed.tile([P, WIDEST], U8, name="dys_win", align_bytes=64, offset=DYS_AT)
+        dys_rows = keep.tile([P, S], U8, name="dys_rows", align_bytes=64)
         dys = keep.tile([P, 2, S], U8, name="dys", align_bytes=64)
-        early = keep.tile([P, 10, ROW], U8, name="early", align_bytes=64)
+        w1 = keep.tile([P, E, ROW], U8, name="w1", align_bytes=64)
+        w3_first = [keep.tile([P, 1, ROW], U8, name="w3_%d" % e, align_bytes=64) for e in range(2)]
+        w2t_first = placed.tile([P, 4, ROW], U8, name="w2t_first", align_bytes=64, offset=GATE_AT + 64)
         w1s = keep.tile([P, E, H], U8, name="w1s", align_bytes=64)
         w3s = keep.tile([P, E, H], U8, name="w3s", align_bytes=64)
         w2ts = keep.tile([P, 2 * E, H], U8, name="w2ts", align_bytes=64)
-        gate_rows = keep.tile([P, 32], F32, name="gate_rows", align_bytes=64)
+        gate_rows = placed.tile([P, 32], F32, name="gate_rows", align_bytes=64, offset=GATE_AT)
         gates = keep.tile([P, 32], F32, name="gates", align_bytes=64)
         neg_gates = keep.tile([P, TILES], F32, name="neg_gates")
         ident = keep.tile([P, P], F32, name="ident")
@@ -66,51 +69,61 @@ def tile_moe_rec_glu_sigmoid_kernel(
         }
         scales = keep.tile([P, TILES * 2 * P], U8, name="scales", align_bytes=64)
 
-        for plane in (xs_win[:], dys_win[:], w1s[:]):
-            nc.gpsimd.memset(plane.bitcast(I32), 0)
-        for plane in (w3s[:].bitcast(I32), x_win[:, T:], w2ts[:].bitcast(I32)):
+        nc.gpsimd.memset(w3s[:].bitcast(I32), 0)
+        for plane in (
+            w1s[:].bitcast(I32), dys_win[:].bitcast(I32), xs_win[:, 0, T:].bitcast(I32),
+            x_win[:, T:],
+        ):
             nc.vector.memset(plane, 0)
-        nc.gpsimd.dma_start(
-            dys_win[0:32, 0:T].bitcast(I32), dy_scales.bitcast(I32).rearrange("s b c -> b s c")
-        )
-        make_identity(nc, ident[:])
-        nc.gpsimd.memset(dys[:].bitcast(I32), 0)
+
+        def load_rows(queue, planes, rows, q):
+            src = rows.bitcast(I32)[:, 4 * q:4 * q + 4, :].rearrange("g j c -> j g c")
+            queue.dma_start(planes[32 * q:32 * q + 4].bitcast(I32), src)
 
         def load_planes(planes, rows):
             for q in range(4):
-                src = rows.bitcast(I32)[:, 4 * q:4 * q + 4, :].rearrange("g j c -> j g c")
-                nc.sync.dma_start(planes[32 * q:32 * q + 4].bitcast(I32), src)
+                load_rows(nc.sync, planes, rows, q)
 
-        def load_words(dst, words, first, last):
-            nc.sync.dma_start(dst.bitcast(I32), words.bitcast(I32)[first:last].rearrange("e s p b -> p (e s) b"))
+        def load_words(dst, words, first, last, queue=nc.sync):
+            queue.dma_start(dst.bitcast(I32), words.bitcast(I32)[first:last].rearrange("e s p b -> p (e s) b"))
 
         def all_passes(rows):
             return rows.rearrange("e s b c -> (e s) b c")
 
-        nc.sync.dma_start(x_win[:, 0:T], x_words[0].rearrange("p t d -> p (t d)").bitcast(I32))
+        load_words(w3_first[0][:], w3_words, 0, 1, nc.gpsimd)
+        load_rows(nc.gpsimd, w1s, all_passes(w1_scales), 0)
+        load_words(w3_first[1][:], w3_words, 1, 2, nc.gpsimd)
         nc.sync.dma_start(offs_sb[:], offs)
-        nc.sync.dma_start(gate_rows[:], gate[0:4, :].rearrange("r (c b i) -> b (r c) i", b=4, i=32))
+        nc.scalar.dma_start(gate_rows[:], gate[0:4, :].rearrange("r (c b i) -> b (r c) i", b=4, i=32))
         nc.vector.transpose(gates[:], gate_rows[:])
         nc.gpsimd.tensor_scalar(neg_gates[:], gates[:, 0:TILES], -1.0, 0.0, ALU.mult, ALU.add)
-        load_planes(xs_win[:, :, 0:T], x_scales)
-        load_words(early[:, 0:4, :], w1_words, 0, E)
-        load_words(early[:, 8:10, :], w3_words, 0, 2)
-        load_planes(w1s, all_passes(w1_scales))
+        nc.gpsimd.memset(w2ts[:].bitcast(I32), 0)
+        nc.gpsimd.memset(dys[:].bitcast(I32), 0)
+        make_identity(nc, ident[:])
+        for q in range(4):
+            rows = x_scales.bitcast(I32)[0, 4 * q:4 * q + 4, :].rearrange("j c -> (j c)")
+            queue = nc.sync if q < 2 else nc.scalar
+            queue.dma_start(xs_win[32 * q:32 * q + 32, 0, 0:T].bitcast(I32), rows.partition_broadcast(8))
+        nc.sync.dma_start(x_win[:, 0:T], x_words[0].rearrange("p t d -> p (t d)").bitcast(I32))
+        load_words(w1[:], w1_words, 0, E)
         load_planes(w3s, all_passes(w3_scales))
+        for q in range(1, 4):
+            load_rows(nc.scalar, w1s, all_passes(w1_scales), q)
+        nc.scalar.dma_start(
+            dys_win[0:32, 0:T].bitcast(I32), dy_scales.bitcast(I32).rearrange("s b c -> b s c")
+        )
+        load_planes(w2ts, all_passes(w2t_scales))
         nc.sync.dma_start(
             dy_win[:, 0:2 * T].rearrange("p (s t) -> p s t", s=2), dy_words.rearrange("s p t d -> p s (t d)").bitcast(I32)
         )
-        load_words(early[:, 4:8, :], w2t_words, 0, 2)
-        load_planes(w2ts, all_passes(w2t_scales))
-        nc.sync.dma_start(pos1_sb[:], pos1)
-        nc.sync.dma_start(pos2_sb[:], pos2)
+        load_words(w2t_first[:], w2t_words, 0, 2)
 
         halves_of_offs = [offs_sb[:, 0:S // 32], offs_sb[:, S // 32:S // 16]]
-        xg = [keep.tile([P, S // 2], U32, name="xg0", align_bytes=64)]
+        xg = [keep.tile([P, S // 2], U32, name="xg%d" % h, align_bytes=64) for h in range(2)]
         xgs = [keep.tile([P, S // 2], U8, name="xgs0", align_bytes=64)]
-        nc.vector.tensor_copy(xg[0][:], x_win[:].bitcast(U32).indirect(halves_of_offs[0]))
-        nc.vector.tensor_copy(xs_again[:].bitcast(I32), xs_win[:, 0, :].bitcast(I32))
         nc.vector.tensor_copy(xgs[0][:], xs_win[:, 0, :].indirect(halves_of_offs[0]))
+        nc.vector.tensor_copy(xg[0][:], x_win[:].bitcast(U32).indirect(halves_of_offs[0]))
+        nc.vector.tensor_copy(xg[1][:], x_win[:].bitcast(U32).indirect(halves_of_offs[1]))
         nc.vector.tensor_copy(dys_rows[:], dys_win[:].indirect(offs_sb[:]))
         for q in range(4):
             nc.sync.dma_start(dys[32 * q:32 * q + 4].bitcast(I32), dys_rows[8 * q:8 * q + 8, :].bitcast(I32))
@@ -122,53 +135,46 @@ def tile_moe_rec_glu_sigmoid_kernel(
             for c in range(2):
                 dyg.setdefault((2 * e + c, s), words[:, c * P:(c + 1) * P])
 
-        dyg_first = placed.tile([P, 2, C], U32, name="dyg_first", align_bytes=64, offset=XS_AT + 64)
+        xgs.append(placed.tile([P, S // 2], U8, name="xgs1", align_bytes=64, offset=DYS_AT + 64))
+        nc.vector.tensor_copy(xgs[1][:], xs_win[:, 0, :].indirect(halves_of_offs[1]))
+        words = placed.tile([P, 2, C], U32, name="dyg0", align_bytes=64, offset=DY0_AT)
         for s in range(2):
-            gather_gradients(0, s, dyg_first[:, s, :])
-        xg.append(placed.tile([P, S // 2], U32, name="xg1", align_bytes=64, offset=0))
-        nc.vector.tensor_copy(xg[1][:], x_win[:].bitcast(U32).indirect(halves_of_offs[1]))
-        xgs.append(placed.tile([P, S // 2], U8, name="xgs1", align_bytes=64, offset=4 * T))
-        nc.vector.tensor_copy(xgs[1][:], xs_again[:].indirect(halves_of_offs[1]))
-        dyg_next = keep.tile([P, 2, C], U32, name="dyg_next", tag="x_win", align_bytes=64)
-        for s in range(2):
-            gather_gradients(1, s, dyg_next[:, s, :])
+            gather_gradients(0, s, words[:, s, :])
+        words = keep.tile([P, 5, C], U32, name="dyg1", tag="xs_win", align_bytes=64)
+        for n, (e, s) in enumerate(((1, 0), (1, 1), (2, 0), (2, 1), (3, 0))):
+            gather_gradients(e, s, words[:, n, :])
 
-        late = placed.tile([P, 6, ROW], U8, name="late", align_bytes=64, offset=5 * T)
-        back_planes = keep.tile([P, 2 * E, K], U8, name="back_planes", align_bytes=64)
-        w1ts, w3ts = back_planes[:, 0:E, :], back_planes[:, E:2 * E, :]
-        nc.gpsimd.memset(back_planes[:].bitcast(I32), 0)
-        load_words(late[:, 0:4, :], w2t_words, 2, E)
-        load_words(late[:, 4:6, :], w3_words, 2, E)
-        load_planes(w1ts, all_passes(w1t_scales))
-        load_planes(w3ts, all_passes(w3t_scales))
-        w1 = early[:, 0:4, :]
-        w2t = [early[:, r, :] for r in range(4, 8)] + [late[:, r, :] for r in range(0, 4)]
-        w3 = [early[:, 8, :], early[:, 9, :], late[:, 4, :], late[:, 5, :]]
+        late = placed.tile([P, 6, ROW], U8, name="late", align_bytes=64, offset=DYS_AT + 64 - 6 * ROW)
+        w2t_last = late[:, 2:6, :]
+        load_words(late[:, 0:2, :], w3_words, 2, E)
+        load_words(w2t_last, w2t_words, 2, E)
+        w3 = [w3_first[0][:, 0, :], w3_first[1][:, 0, :], late[:, 0, :], late[:, 1, :]]
+        nc.sync.dma_start(pos1_sb[:], pos1)
+        nc.sync.dma_start(pos2_sb[:], pos2)
+        w2t = [w2t_first[:, r, :] for r in range(4)] + [w2t_last[:, r, :] for r in range(4)]
 
-        taken = []
-
-        def bank(name):
-            taken.append(name)
-            return psum.tile([P, H], F32, name=name, tag="sums%d" % (len(taken) % 6), bufs=1)
+        def bank(name, n):
+            return psum.tile([P, H], F32, name=name, tag="sums%d" % n, bufs=1)
 
         def tokens(c):
             cols = slice((c % 4) * P, (c % 4 + 1) * P)
             return xg[c // 4][:, cols].bitcast(FP8X4), xgs[c // 4][:, cols]
 
-        def rest(c, a1):
+        def rest(c, n):
+            a1 = bank("a1", n)
             nc.tensor.matmul_mx(a1[:], *tokens(c), w1[:, c // 2, :].bitcast(FP4X4), w1s[:, c // 2, :], start=True, stop=True)
             out_tile = keep.tile([P, H], F32, name="sig%d" % c, align_bytes=64)
             nc.scalar.activation(out_tile[:], a1[:], ACT.Sigmoid, scale=-1.0)
             return out_tile
 
-        def sum_a3(c):
-            a3 = bank("a3")
+        def sum_a3(c, n):
+            a3 = bank("a3", n)
             nc.tensor.matmul_mx(a3[:], *tokens(c), w3[c // 2].bitcast(FP4X4), w3s[:, c // 2, :], start=True, stop=True)
             return a3
 
-        def sum_dh(c):
+        def sum_dh(c, n):
             e = c // 2
-            dh = bank("dh")
+            dh = bank("dh", n)
             for s in range(2):
                 nc.tensor.matmul_mx(
                     dh[:], dyg[(c, s)].bitcast(FP8X4), dys[:, s, c * P:(c + 1) * P],
@@ -176,35 +182,35 @@ def tile_moe_rec_glu_sigmoid_kernel(
                 )
             return dh
 
-        def token_factor_early(c):
-            a3 = sum_a3(c)
+        def token_factor_early(c, n):
+            a3 = sum_a3(c, n)
             gated = keep.tile([P, H], F32, name="gated%d" % c, align_bytes=64)
-            negq = keep.tile([P, H], F32, name="negq%d" % c)
+            negq = keep.tile([P, H], F32, name="negq%d" % c, align_bytes=64)
             nc.scalar.activation(gated[:], a3[:], ACT.Copy, scale=neg_gates[:, c:c + 1])
             nc.gpsimd.tensor_tensor(negq[:], gated[:], rests[c][:], ALU.mult)
             return negq
 
-        def token_factor(c, a3):
-            negq = work.tile([P, H], F32, name="negq")
+        def token_factor(c, a3, tag):
+            negq = keep.tile([P, H], F32, name="negq%d" % c, tag=tag, align_bytes=64)
             nc.vector.scalar_tensor_tensor(negq[:], a3[:], neg_gates[:, c:c + 1], rests[c][:], ALU.mult, ALU.mult)
             return negq
 
         def gradient_factor(c, dh):
-            neg3 = work.tile([P, H], F32, name="neg3")
+            neg3 = work.tile([P, H], F32, name="neg3", bufs=4)
             da = work.tile([P, 2, H], BF16, name="da", align_bytes=64)
             nc.vector.scalar_tensor_tensor(neg3[:], rests[c][:], 1.0, dh[:], ALU.subtract, ALU.mult)
             nc.scalar.activation(da[:, 1, :], neg3[:], ACT.Copy, scale=neg_gates[:, c:c + 1])
             return neg3, da
 
         def turn(c, neg3, negq, da):
-            engine = nc.vector if c == LAST else nc.gpsimd
+            engine = nc.vector if c >= LAST - 1 else nc.gpsimd
             engine.tensor_tensor(da[:, 0, :], neg3[:], negq[:], ALU.mult)
             words = da[:].rearrange("p a i -> p (a i)").bitcast(F32)
             turned = psum.tile([P, 4, P], F32, name="turned", tag="turn%d" % (c % 2), bufs=1)
             turned_words = turned[:].rearrange("p (a u) s -> p a s u", u=2)
             for a in (1, 0):
                 if c == LAST and a == 0:
-                    turned = psum.tile([P, 4, P], F32, name="turned", tag="sums3", bufs=1)
+                    turned = psum.tile([P, 4, P], F32, name="turned", tag="sums5", bufs=1)
                     turned_words = turned[:].rearrange("p (a u) s -> p a s u", u=2)
                 for u in range(2):
                     nc.tensor.transpose(turned[:, 2 * a + u, :], words[:, 2 * a * P + u:2 * (a + 1) * P:2], ident[:])
@@ -229,7 +235,7 @@ def tile_moe_rec_glu_sigmoid_kernel(
             nc.scalar.copy(dx[kt][:, tiles[0] * P:(tiles[-1] + 1) * P], acc[:])
 
         codes = keep.tile([P, TILES * 2 * P], U32, name="codes", tag="sig%d" % LAST, align_bytes=64)
-        first_rows = {4: ([0, 1, 2, 3], "sums0"), 12: ([4, 5, 6], "sums1"), 14: ([7], "sums2")}
+        first_rows = {4: ([0, 1, 2, 3], "sums4"), 12: ([4, 5, 6], "sums0"), 14: ([7], "sums1")}
 
         def quantise(first, last):
             words = codes[:, first * P:last * P]
@@ -237,39 +243,37 @@ def tile_moe_rec_glu_sigmoid_kernel(
             if first in first_rows:
                 group(0, *first_rows[first])
 
-        rests = [rest(0, psum.tile([P, H], F32, name="a1", tag="turn0", bufs=1))]
-        negqs = {0: token_factor_early(0)}
-        for c in range(1, TILES):
-            if c == TILES // 2:
-                dhs = {n: sum_dh(n) for n in range(2)}
-            rests.append(rest(c, bank("a1")))
-            if c < EARLY:
-                negqs[c] = token_factor_early(c)
-
-        back = keep.tile([P, 8, ROW], U8, name="back", tag="gated%d" % (EARLY - 1), align_bytes=64)
-        load_words(back[:, 0:4, :], w1t_words, 0, E)
-        load_words(back[:, 4:8, :], w3t_words, 0, E)
-        w1t = back[:, 0:4, :]
-        w3t = back[:, 4:8, :]
-        a3s = {}
-        held = {1: [(2, 0, "sig0"), (2, 1, "sig1")], 3: [(3, 0, "sig2")], 4: [(3, 1, "sig3")]}
-        more = {
-            0: [("dh", 2)], 1: [("dh", 3), ("a3", 3), ("a3", 4), ("dh", 4), ("dh", 5)], 2: [("a3", 5)],
-            3: [("a3", 6)], 4: [("dh", 6), ("a3", 7), ("dh", 7)],
-        }
+        rests, negqs, dhs, a3s, made = [], {}, {}, {}, {}
+        for c in range(EARLY):
+            rests.append(rest(c, 2 * (c % 2) + c // 2))
+            negqs[c] = token_factor_early(c, 2 * (c % 2) + 1 - c // 2)
+        for c in range(EARLY, TILES):
+            rests.append(rest(c, (0, 2, 1, 3)[c - EARLY]))
+        for c, n in enumerate((4, 5, 0, 2)):
+            dhs[c] = sum_dh(c, n)
+        a3s[4] = sum_a3(4, 1)
+        a3s[5] = sum_a3(5, 3)
+        load_words(w1[:], w1t_words, 0, E)
+        load_planes(w1s, all_passes(w1t_scales))
+        load_words(w2t_first[:], w3t_words, 0, E)
+        load_planes(w2ts[:, 0:E, :], all_passes(w3t_scales))
+        w1t, w1ts, w3t, w3ts = w1, w1s, w2t_first, w2ts
         for c in range(TILES):
             neg3, da = gradient_factor(c, dhs[c])
-            if c >= EARLY:
-                negqs[c] = token_factor(c, a3s[c])
-            for e, s, lender in held.get(c, []):
-                words = keep.tile([P, C], U32, name="dyg%d%d" % (e, s), tag=lender, align_bytes=64)
-                gather_gradients(e, s, words[:])
-            for kind, n in more.get(c, []):
-                if kind == "dh":
-                    dhs[n] = sum_dh(n)
-                else:
-                    a3s[n] = sum_a3(n)
-            turn(c, neg3, negqs[c], da)
+            if c == 0:
+                words = placed.tile([P, C], U32, name="dyg31", align_bytes=64, offset=DY0_AT)
+                gather_gradients(3, 1, words[:])
+            elif c <= EARLY:
+                negqs[c + 3] = token_factor(c + 3, a3s[c + 3], "sig%d" % (c - 1))
+            if c < 4:
+                dhs[c + 4] = sum_dh(c + 4, (4, 5, 0, 2)[c])
+            if c in (1, 2):
+                a3s[c + 5] = sum_a3(c + 5, 2 * c - 1)
+            made[c] = (neg3, negqs[c], da)
+            if c < LAST - 1:
+                turn(c, *made[c])
+        for c in (LAST - 1, LAST):
+            turn(c, *made[c])
         for call in CALLS:
             quantise(*call)
 

@@ -13,9 +13,12 @@ ROW = 2 * H
 FLOPS = 2 * S * (2 * K * H + N * H + 2 * H * K)
 
 CALLS = ((0, 4), (4, 8), (8, 12), (12, 14), (15, 16), (14, 15))
-EARLY = 4
+TURN_BANKS = ("turn0", "turn1", "turn0", "turn1", "turn0", "turn1", "sums4", "sums2")
+SHARED = 5
+EARLY = 5
 DYS_AT = 6144
 GATE_AT = 12800
+NEGQ_AT = 18432
 DY0_AT = DYS_AT + 576
 WIDE = 704
 WIDEST = 1408
@@ -53,7 +56,7 @@ def tile_moe_rec_glu_sigmoid_kernel(
         dys_rows = keep.tile([P, S], U8, name="dys_rows", align_bytes=64)
         dys = keep.tile([P, 2, S], U8, name="dys", align_bytes=64)
         w1 = keep.tile([P, E, ROW], U8, name="w1", align_bytes=64)
-        w3_first = [keep.tile([P, 1, ROW], U8, name="w3_%d" % e, align_bytes=64) for e in range(2)]
+        w3_first = [keep.tile([P, 1 + e, ROW], U8, name="w3_%d" % e, align_bytes=64) for e in range(2)]
         w2t_first = placed.tile([P, 4, ROW], U8, name="w2t_first", align_bytes=64, offset=GATE_AT + 64)
         w1s = keep.tile([P, E, H], U8, name="w1s", align_bytes=64)
         w3s = keep.tile([P, E, H], U8, name="w3s", align_bytes=64)
@@ -92,7 +95,7 @@ def tile_moe_rec_glu_sigmoid_kernel(
 
         load_words(w3_first[0][:], w3_words, 0, 1, nc.gpsimd)
         load_rows(nc.gpsimd, w1s, all_passes(w1_scales), 0)
-        load_words(w3_first[1][:], w3_words, 1, 2, nc.gpsimd)
+        load_words(w3_first[1][:], w3_words, 1, 3, nc.gpsimd)
         nc.sync.dma_start(offs_sb[:], offs)
         nc.scalar.dma_start(gate_rows[:], gate[0:4, :].rearrange("r (c b i) -> b (r c) i", b=4, i=32))
         nc.vector.transpose(gates[:], gate_rows[:])
@@ -144,11 +147,11 @@ def tile_moe_rec_glu_sigmoid_kernel(
         for n, (e, s) in enumerate(((1, 0), (1, 1), (2, 0), (2, 1), (3, 0))):
             gather_gradients(e, s, words[:, n, :])
 
-        late = placed.tile([P, 6, ROW], U8, name="late", align_bytes=64, offset=DYS_AT + 64 - 6 * ROW)
-        w2t_last = late[:, 2:6, :]
-        load_words(late[:, 0:2, :], w3_words, 2, E)
+        late = placed.tile([P, 5, ROW], U8, name="late", align_bytes=64, offset=DYS_AT + 64 - 5 * ROW)
+        w2t_last = late[:, 1:5, :]
         load_words(w2t_last, w2t_words, 2, E)
-        w3 = [w3_first[0][:, 0, :], w3_first[1][:, 0, :], late[:, 0, :], late[:, 1, :]]
+        load_words(late[:, 0:1, :], w3_words, 3, E)
+        w3 = [w3_first[0][:, 0, :], w3_first[1][:, 0, :], w3_first[1][:, 1, :], late[:, 0, :]]
         nc.sync.dma_start(pos1_sb[:], pos1)
         nc.sync.dma_start(pos2_sb[:], pos2)
         w2t = [w2t_first[:, r, :] for r in range(4)] + [w2t_last[:, r, :] for r in range(4)]
@@ -185,7 +188,10 @@ def tile_moe_rec_glu_sigmoid_kernel(
         def token_factor_early(c, n):
             a3 = sum_a3(c, n)
             gated = keep.tile([P, H], F32, name="gated%d" % c, align_bytes=64)
-            negq = keep.tile([P, H], F32, name="negq%d" % c, align_bytes=64)
+            if c == SHARED - 1:
+                negq = placed.tile([P, H], F32, name="negq_last", align_bytes=64, offset=NEGQ_AT)
+            else:
+                negq = keep.tile([P, H], F32, name="negq%d" % c, align_bytes=64)
             nc.scalar.activation(gated[:], a3[:], ACT.Copy, scale=neg_gates[:, c:c + 1])
             nc.gpsimd.tensor_tensor(negq[:], gated[:], rests[c][:], ALU.mult)
             return negq
@@ -203,17 +209,21 @@ def tile_moe_rec_glu_sigmoid_kernel(
             return neg3, da
 
         def turn(c, neg3, negq, da):
-            engine = nc.vector if c >= LAST - 1 else nc.gpsimd
-            engine.tensor_tensor(da[:, 0, :], neg3[:], negq[:], ALU.mult)
-            words = da[:].rearrange("p a i -> p (a i)").bitcast(F32)
-            turned = psum.tile([P, 4, P], F32, name="turned", tag="turn%d" % (c % 2), bufs=1)
+            engine, da1 = nc.gpsimd, da[:, 0, :]
+            if c >= SHARED:
+                at = NEGQ_AT + (64 - 2 * H, H, 4 * H - 64)[c - SHARED]
+                own = placed.tile([P, H], BF16, name="da1_%d" % c, align_bytes=64, offset=at)
+                engine, da1 = nc.vector, own[:]
+            engine.tensor_tensor(da1, neg3[:], negq[:], ALU.mult)
+            words = [da1.bitcast(F32), da[:, 1, :].bitcast(F32)]
+            turned = psum.tile([P, 4, P], F32, name="turned", tag=TURN_BANKS[c], bufs=1)
             turned_words = turned[:].rearrange("p (a u) s -> p a s u", u=2)
             for a in (1, 0):
                 if c == LAST and a == 0:
                     turned = psum.tile([P, 4, P], F32, name="turned", tag="sums5", bufs=1)
                     turned_words = turned[:].rearrange("p (a u) s -> p a s u", u=2)
                 for u in range(2):
-                    nc.tensor.transpose(turned[:, 2 * a + u, :], words[:, 2 * a * P + u:2 * (a + 1) * P:2], ident[:])
+                    nc.tensor.transpose(turned[:, 2 * a + u, :], words[a][:, u:2 * P:2], ident[:])
                 if c == LAST:
                     half = grouped[2 * c + a][:].bitcast(F32).rearrange("p (s u) -> p s u", u=2)
                     nc.scalar.copy(half, turned_words[:, a])
@@ -234,8 +244,8 @@ def tile_moe_rec_glu_sigmoid_kernel(
                     )
             nc.scalar.copy(dx[kt][:, tiles[0] * P:(tiles[-1] + 1) * P], acc[:])
 
-        codes = keep.tile([P, TILES * 2 * P], U32, name="codes", tag="sig%d" % LAST, align_bytes=64)
-        first_rows = {4: ([0, 1, 2, 3], "sums4"), 12: ([4, 5, 6], "sums0"), 14: ([7], "sums1")}
+        codes = keep.tile([P, TILES * 2 * P], U32, name="codes", tag="sig2", align_bytes=64)
+        first_rows = {4: ([0, 1, 2, 3], "sums0"), 12: ([4, 5, 6], "sums1"), 14: ([7], "sums3")}
 
         def quantise(first, last):
             words = codes[:, first * P:last * P]
@@ -244,15 +254,14 @@ def tile_moe_rec_glu_sigmoid_kernel(
                 group(0, *first_rows[first])
 
         rests, negqs, dhs, a3s, made = [], {}, {}, {}, {}
-        for c in range(EARLY):
-            rests.append(rest(c, 2 * (c % 2) + c // 2))
-            negqs[c] = token_factor_early(c, 2 * (c % 2) + 1 - c // 2)
-        for c in range(EARLY, TILES):
-            rests.append(rest(c, (0, 2, 1, 3)[c - EARLY]))
-        for c, n in enumerate((4, 5, 0, 2)):
+        for c, (n1, n3) in enumerate(((0, 1), (2, 3), (1, 0), (3, 2), (0, 1))):
+            rests.append(rest(c, n1))
+            negqs[c] = token_factor_early(c, n3)
+        for c, n in ((5, 3), (6, 2), (7, 0)):
+            rests.append(rest(c, n))
+        for c, n in enumerate((4, 5, 1, 3)):
             dhs[c] = sum_dh(c, n)
-        a3s[4] = sum_a3(4, 1)
-        a3s[5] = sum_a3(5, 3)
+        a3s[6] = sum_a3(6, 0)
         load_words(w1[:], w1t_words, 0, E)
         load_planes(w1s, all_passes(w1t_scales))
         load_words(w2t_first[:], w3t_words, 0, E)
@@ -263,23 +272,23 @@ def tile_moe_rec_glu_sigmoid_kernel(
             if c == 0:
                 words = placed.tile([P, C], U32, name="dyg31", align_bytes=64, offset=DY0_AT)
                 gather_gradients(3, 1, words[:])
-            elif c <= EARLY:
-                negqs[c + 3] = token_factor(c + 3, a3s[c + 3], "sig%d" % (c - 1))
+            if c in (2, 3, 4):
+                negqs[c + 3] = token_factor(c + 3, a3s[c + 3], "sig2" if c == 3 else "negq%d" % (c + 3))
             if c < 4:
-                dhs[c + 4] = sum_dh(c + 4, (4, 5, 0, 2)[c])
+                dhs[c + 4] = sum_dh(c + 4, (4, 2, 1, 3)[c])
             if c in (1, 2):
-                a3s[c + 5] = sum_a3(c + 5, 2 * c - 1)
+                a3s[2 * c + 3] = sum_a3(2 * c + 3, 5)
             made[c] = (neg3, negqs[c], da)
-            if c < LAST - 1:
+            if c < SHARED:
                 turn(c, *made[c])
-        for c in (LAST - 1, LAST):
+        for c in range(SHARED, TILES):
             turn(c, *made[c])
         for call in CALLS:
             quantise(*call)
 
-        for kt in range(1, KT):
-            group(kt, [4, 5, 6, 7], "sums%d" % (kt + 2))
-            group(kt, [0, 1, 2, 3], "sums%d" % (kt + 1))
+        for kt, banks in ((1, ("sums4", "turn0")), (2, ("sums2", "sums4")), (3, ("sums5", "sums2"))):
+            group(kt, [4, 5, 6, 7], banks[0])
+            group(kt, [0, 1, 2, 3], banks[1])
 
         ones = [keep.tile([P, T], F32, name="one%d" % kt) for kt in range(KT)]
 

@@ -13,12 +13,11 @@ ROW = 2 * H
 FLOPS = 2 * S * (2 * K * H + N * H + 2 * H * K)
 
 CALLS = ((0, 4), (4, 8), (8, 12), (12, 14), (15, 16), (14, 15))
-TURN_BANKS = ("turn0", "turn1", "turn0", "turn1", "turn0", "turn1", "sums4", "sums2")
+TURN_BANKS = ("turn0", "turn1", "turn0", "turn1", "turn0", "sums4", "sums0", "sums5")
 SHARED = 5
 EARLY = 5
 DYS_AT = 6144
 GATE_AT = 12800
-NEGQ_AT = 18432
 DY0_AT = DYS_AT + 576
 WIDE = 704
 WIDEST = 1408
@@ -167,7 +166,10 @@ def tile_moe_rec_glu_sigmoid_kernel(
             a1 = bank("a1", n)
             nc.tensor.matmul_mx(a1[:], *tokens(c), w1[:, c // 2, :].bitcast(FP4X4), w1s[:, c // 2, :], start=True, stop=True)
             out_tile = keep.tile([P, H], F32, name="sig%d" % c, align_bytes=64)
-            nc.scalar.activation(out_tile[:], a1[:], ACT.Sigmoid, scale=-1.0)
+            nc.scalar.activation(out_tile[:], a1[:], ACT.Sigmoid, scale=-1.0 if c < SHARED else 1.0)
+            if c >= SHARED:
+                squares[c] = keep.tile([P, H], F32, name="square%d" % c, align_bytes=64)
+                nc.scalar.activation(squares[c][:], out_tile[:], ACT.Square, bias=-0.5)
             return out_tile
 
         def sum_a3(c, n):
@@ -188,39 +190,36 @@ def tile_moe_rec_glu_sigmoid_kernel(
         def token_factor_early(c, n):
             a3 = sum_a3(c, n)
             gated = keep.tile([P, H], F32, name="gated%d" % c, align_bytes=64)
-            if c == SHARED - 1:
-                negq = placed.tile([P, H], F32, name="negq_last", align_bytes=64, offset=NEGQ_AT)
-            else:
-                negq = keep.tile([P, H], F32, name="negq%d" % c, align_bytes=64)
+            negq = keep.tile([P, H], F32, name="negq%d" % c, align_bytes=64)
             nc.scalar.activation(gated[:], a3[:], ACT.Copy, scale=neg_gates[:, c:c + 1])
             nc.gpsimd.tensor_tensor(negq[:], gated[:], rests[c][:], ALU.mult)
             return negq
 
-        def token_factor(c, a3, tag):
-            negq = keep.tile([P, H], F32, name="negq%d" % c, tag=tag, align_bytes=64)
-            nc.vector.scalar_tensor_tensor(negq[:], a3[:], neg_gates[:, c:c + 1], rests[c][:], ALU.mult, ALU.mult)
-            return negq
+        def slope_factor(c, a3):
+            factor = keep.tile([P, H], F32, name="slope%d" % c, align_bytes=64)
+            nc.vector.scalar_tensor_tensor(factor[:], squares[c][:], 0.25, a3[:], ALU.subtract, ALU.mult)
+            return factor
+
+        def products(c, dh, factor):
+            da = work.tile([P, 2, H], BF16, name="da", bufs=8, align_bytes=64)
+            nc.vector.scalar_tensor_tensor(da[:, 1, :], dh[:], gates[:, c:c + 1], rests[c][:], ALU.mult, ALU.mult)
+            nc.vector.scalar_tensor_tensor(da[:, 0, :], dh[:], neg_gates[:, c:c + 1], factor[:], ALU.mult, ALU.mult)
+            return da
 
         def gradient_factor(c, dh):
-            neg3 = work.tile([P, H], F32, name="neg3", bufs=4)
-            da = work.tile([P, 2, H], BF16, name="da", align_bytes=64)
+            neg3 = work.tile([P, H], F32, name="neg3", bufs=5)
+            da = work.tile([P, 2, H], BF16, name="da", bufs=8, align_bytes=64)
             nc.vector.scalar_tensor_tensor(neg3[:], rests[c][:], 1.0, dh[:], ALU.subtract, ALU.mult)
             nc.scalar.activation(da[:, 1, :], neg3[:], ACT.Copy, scale=neg_gates[:, c:c + 1])
             return neg3, da
 
-        def turn(c, neg3, negq, da):
-            engine, da1 = nc.gpsimd, da[:, 0, :]
-            if c >= SHARED:
-                at = NEGQ_AT + (64 - 2 * H, H, 4 * H - 64)[c - SHARED]
-                own = placed.tile([P, H], BF16, name="da1_%d" % c, align_bytes=64, offset=at)
-                engine, da1 = nc.vector, own[:]
-            engine.tensor_tensor(da1, neg3[:], negq[:], ALU.mult)
-            words = [da1.bitcast(F32), da[:, 1, :].bitcast(F32)]
+        def turn(c, da):
+            words = [da[:, a, :].bitcast(F32) for a in range(2)]
             turned = psum.tile([P, 4, P], F32, name="turned", tag=TURN_BANKS[c], bufs=1)
             turned_words = turned[:].rearrange("p (a u) s -> p a s u", u=2)
             for a in (1, 0):
                 if c == LAST and a == 0:
-                    turned = psum.tile([P, 4, P], F32, name="turned", tag="sums5", bufs=1)
+                    turned = psum.tile([P, 4, P], F32, name="turned", tag="sums2", bufs=1)
                     turned_words = turned[:].rearrange("p (a u) s -> p a s u", u=2)
                 for u in range(2):
                     nc.tensor.transpose(turned[:, 2 * a + u, :], words[a][:, u:2 * P:2], ident[:])
@@ -244,8 +243,8 @@ def tile_moe_rec_glu_sigmoid_kernel(
                     )
             nc.scalar.copy(dx[kt][:, tiles[0] * P:(tiles[-1] + 1) * P], acc[:])
 
-        codes = keep.tile([P, TILES * 2 * P], U32, name="codes", tag="sig2", align_bytes=64)
-        first_rows = {4: ([0, 1, 2, 3], "sums0"), 12: ([4, 5, 6], "sums1"), 14: ([7], "sums3")}
+        codes = keep.tile([P, TILES * 2 * P], U32, name="codes", tag="negq%d" % (SHARED - 1), align_bytes=64)
+        first_rows = {4: ([0, 1, 2, 3], "sums1"), 12: ([4, 5, 6], "sums4"), 14: ([7], "sums3")}
 
         def quantise(first, last):
             words = codes[:, first * P:last * P]
@@ -253,7 +252,7 @@ def tile_moe_rec_glu_sigmoid_kernel(
             if first in first_rows:
                 group(0, *first_rows[first])
 
-        rests, negqs, dhs, a3s, made = [], {}, {}, {}, {}
+        rests, negqs, dhs, a3s, squares, slopes = [], {}, {}, {}, {}, {}
         for c, (n1, n3) in enumerate(((0, 1), (2, 3), (1, 0), (3, 2), (0, 1))):
             rests.append(rest(c, n1))
             negqs[c] = token_factor_early(c, n3)
@@ -267,26 +266,25 @@ def tile_moe_rec_glu_sigmoid_kernel(
         load_words(w2t_first[:], w3t_words, 0, E)
         load_planes(w2ts[:, 0:E, :], all_passes(w3t_scales))
         w1t, w1ts, w3t, w3ts = w1, w1s, w2t_first, w2ts
-        for c in range(TILES):
+        for c in range(SHARED):
             neg3, da = gradient_factor(c, dhs[c])
             if c == 0:
                 words = placed.tile([P, C], U32, name="dyg31", align_bytes=64, offset=DY0_AT)
                 gather_gradients(3, 1, words[:])
-            if c in (2, 3, 4):
-                negqs[c + 3] = token_factor(c + 3, a3s[c + 3], "sig2" if c == 3 else "negq%d" % (c + 3))
+            if c >= 2:
+                slopes[c + 3] = slope_factor(c + 3, a3s[c + 3])
             if c < 4:
                 dhs[c + 4] = sum_dh(c + 4, (4, 2, 1, 3)[c])
             if c in (1, 2):
                 a3s[2 * c + 3] = sum_a3(2 * c + 3, 5)
-            made[c] = (neg3, negqs[c], da)
-            if c < SHARED:
-                turn(c, *made[c])
+            nc.gpsimd.tensor_tensor(da[:, 0, :], neg3[:], negqs[c][:], ALU.mult)
+            turn(c, da)
         for c in range(SHARED, TILES):
-            turn(c, *made[c])
+            turn(c, products(c, dhs[c], slopes[c]))
         for call in CALLS:
             quantise(*call)
 
-        for kt, banks in ((1, ("sums4", "turn0")), (2, ("sums2", "sums4")), (3, ("sums5", "sums2"))):
+        for kt, banks in ((1, ("sums0", "turn1")), (2, ("sums5", "sums0")), (3, ("sums2", "sums5"))):
             group(kt, [4, 5, 6, 7], banks[0])
             group(kt, [0, 1, 2, 3], banks[1])
 

@@ -291,7 +291,11 @@ def tile_moe_rec_glu_sigmoid_kernel(
         ones = [keep.tile([P, T], F32, name="one%d" % kt) for kt in range(KT)]
 
         def first_slots(kt, lo, hi):
-            nc.vector.tensor_copy(ones[kt][:, lo:hi], dx[kt][:].indirect(pos1_sb[:, lo // 16:hi // 16]))
+            picked = dx[kt][:].indirect(pos1_sb[:, lo // 16:hi // 16])
+            if kt == 0 or (kt == 1 and lo == 0):
+                nc.vector.tensor_copy(ones[kt][:, lo:hi], picked)
+            else:
+                nc.scalar.activation(ones[kt][:, lo:hi], picked, ACT.Copy)
 
         def second_slots(kt, lo, hi):
             total = work.tile([P, hi - lo], F32, name="total")

@@ -114,10 +114,10 @@ def tile_moe_rec_glu_sigmoid_kernel(
         nc.scalar.dma_start(
             dys_win[0:32, 0:T].bitcast(I32), dy_scales.bitcast(I32).rearrange("s b c -> b s c")
         )
-        load_planes(w2ts, all_passes(w2t_scales))
         nc.sync.dma_start(
             dy_win[:, 0:2 * T].rearrange("p (s t) -> p s t", s=2), dy_words.rearrange("s p t d -> p s (t d)").bitcast(I32)
         )
+        load_planes(w2ts, all_passes(w2t_scales))
         load_words(w2t_first[:], w2t_words, 0, 2)
 
         halves_of_offs = [offs_sb[:, 0:S // 32], offs_sb[:, S // 32:S // 16]]

@@ -292,13 +292,13 @@ def tile_moe_rec_glu_sigmoid_kernel(
 
         def first_slots(kt, lo, hi):
             picked = dx[kt][:].indirect(pos1_sb[:, lo // 16:hi // 16])
-            if kt == 0 or (kt == 1 and lo == 0):
+            if kt == 0 or (kt == 1 and lo > 0):
                 nc.vector.tensor_copy(ones[kt][:, lo:hi], picked)
             else:
                 nc.scalar.activation(ones[kt][:, lo:hi], picked, ACT.Copy)
 
         def second_slots(kt, lo, hi):
-            total = work.tile([P, hi - lo], F32, name="total")
+            total = work.tile([P, hi - lo], F32, name="total", bufs=9)
             nc.vector.tensor_tensor(total[:], dx[kt][:].indirect(pos2_sb[:, lo // 16:hi // 16]), ones[kt][:, lo:hi], ALU.add)
             nc.sync.dma_start(out[kt * P:(kt + 1) * P, lo:hi], total[:])
 

@@ -17,7 +17,7 @@ TURN_BANKS = ("turn0", "turn1", "turn0", "turn1", "turn0", "sums4", "sums0", "su
 SHARED = 5
 EARLY = 5
 DYS_AT = 6144
-GATE_AT = 12800
+GATE_AT = 13824
 DY0_AT = DYS_AT + 576
 WIDE = 704
 WIDEST = 1408
@@ -48,9 +48,9 @@ def tile_moe_rec_glu_sigmoid_kernel(
         offs_sb = keep.tile([P, S // 16], U16, name="offs_sb")
         pos1_sb = keep.tile([P, T // 16], U16, name="pos1_sb")
         pos2_sb = keep.tile([P, T // 16], U16, name="pos2_sb")
-        x_win = keep.tile([P, WIDE], I32, name="x_win", align_bytes=64)
+        x_win = keep.tile([P, S], I32, name="x_win", align_bytes=64)
         dy_win = placed.tile([P, 2 * T], I32, name="dy_win", align_bytes=64, offset=GATE_AT + 64 - 8 * T)
-        xs_win = keep.tile([P, 1, WIDE], U8, name="xs_win", tag="xs_win", align_bytes=64)
+        xs_win = keep.tile([P, 1, WIDEST], U8, name="xs_win", tag="xs_win", align_bytes=64)
         dys_win = placed.tile([P, WIDEST], U8, name="dys_win", align_bytes=64, offset=DYS_AT)
         dys_rows = keep.tile([P, S], U8, name="dys_rows", align_bytes=64)
         dys = keep.tile([P, 2, S], U8, name="dys", align_bytes=64)
@@ -120,31 +120,31 @@ def tile_moe_rec_glu_sigmoid_kernel(
         load_planes(w2ts, all_passes(w2t_scales))
         load_words(w2t_first[:], w2t_words, 0, 2)
 
-        halves_of_offs = [offs_sb[:, 0:S // 32], offs_sb[:, S // 32:S // 16]]
-        xg = [keep.tile([P, S // 2], U32, name="xg%d" % h, align_bytes=64) for h in range(2)]
-        xgs = [keep.tile([P, S // 2], U8, name="xgs0", align_bytes=64)]
-        nc.vector.tensor_copy(xgs[0][:], xs_win[:, 0, :].indirect(halves_of_offs[0]))
-        nc.vector.tensor_copy(xg[0][:], x_win[:].bitcast(U32).indirect(halves_of_offs[0]))
-        nc.vector.tensor_copy(xg[1][:], x_win[:].bitcast(U32).indirect(halves_of_offs[1]))
+        def entries(first, last):
+            return offs_sb[:, first * (C // 16):last * (C // 16)]
+
+        xg = keep.tile([P, S], U32, name="xg", align_bytes=64)
+        xgs = keep.tile([P, S], U8, name="xgs", align_bytes=64)
+        nc.vector.tensor_copy(xgs[:], xs_win[:, 0, :].indirect(offs_sb[:]))
+        for first, last in ((0, 1), (1, E)):
+            nc.vector.tensor_copy(xg[:, first * C:last * C], x_win[:].bitcast(U32).indirect(entries(first, last)))
         nc.vector.tensor_copy(dys_rows[:], dys_win[:].indirect(offs_sb[:]))
         for q in range(4):
             nc.sync.dma_start(dys[32 * q:32 * q + 4].bitcast(I32), dys_rows[8 * q:8 * q + 8, :].bitcast(I32))
         dyg = {}
 
-        def gather_gradients(e, s, words):
-            window = dy_win[:, s * T:(s + 1) * T].bitcast(U32)
-            nc.vector.tensor_copy(words, window.indirect(offs_sb[:, e * (C // 16):(e + 1) * (C // 16)]))
-            for c in range(2):
-                dyg.setdefault((2 * e + c, s), words[:, c * P:(c + 1) * P])
+        def gather_gradients(first, last, s, words):
+            window = dy_win[:, s * T:s * T + (WIDE if s == 0 else T)].bitcast(U32)
+            nc.vector.tensor_copy(words, window.indirect(entries(first, last)))
+            for c in range(2 * (last - first)):
+                dyg[(2 * first + c, s)] = words[:, c * P:(c + 1) * P]
 
-        xgs.append(placed.tile([P, S // 2], U8, name="xgs1", align_bytes=64, offset=DYS_AT + 64))
-        nc.vector.tensor_copy(xgs[1][:], xs_win[:, 0, :].indirect(halves_of_offs[1]))
-        words = placed.tile([P, 2, C], U32, name="dyg0", align_bytes=64, offset=DY0_AT)
-        for s in range(2):
-            gather_gradients(0, s, words[:, s, :])
-        words = keep.tile([P, 5, C], U32, name="dyg1", tag="xs_win", align_bytes=64)
-        for n, (e, s) in enumerate(((1, 0), (1, 1), (2, 0), (2, 1), (3, 0))):
-            gather_gradients(e, s, words[:, n, :])
+        words = keep.tile([P, 6 * C], U32, name="dyg", align_bytes=64)
+        gather_gradients(0, 2, 0, words[:, 0:2 * C])
+        gather_gradients(0, 1, 1, placed.tile([P, C], U32, name="dyg01", align_bytes=64, offset=DY0_AT)[:])
+        gather_gradients(1, 2, 1, words[:, 2 * C:3 * C])
+        gather_gradients(2, E, 0, words[:, 3 * C:5 * C])
+        gather_gradients(2, 3, 1, words[:, 5 * C:6 * C])
 
         late = placed.tile([P, 5, ROW], U8, name="late", align_bytes=64, offset=DYS_AT + 64 - 5 * ROW)
         w2t_last = late[:, 1:5, :]
@@ -159,8 +159,8 @@ def tile_moe_rec_glu_sigmoid_kernel(
             return psum.tile([P, H], F32, name=name, tag="sums%d" % n, bufs=1)
 
         def tokens(c):
-            cols = slice((c % 4) * P, (c % 4 + 1) * P)
-            return xg[c // 4][:, cols].bitcast(FP8X4), xgs[c // 4][:, cols]
+            cols = slice(c * P, (c + 1) * P)
+            return xg[:, cols].bitcast(FP8X4), xgs[:, cols]
 
         def rest(c, n):
             a1 = bank("a1", n)
@@ -270,7 +270,7 @@ def tile_moe_rec_glu_sigmoid_kernel(
             neg3, da = gradient_factor(c, dhs[c])
             if c == 0:
                 words = placed.tile([P, C], U32, name="dyg31", align_bytes=64, offset=DY0_AT)
-                gather_gradients(3, 1, words[:])
+                gather_gradients(3, E, 1, words[:])
             if c >= 2:
                 slopes[c + 3] = slope_factor(c + 3, a3s[c + 3])
             if c < 4:

@@ -139,12 +139,13 @@ def tile_moe_rec_glu_sigmoid_kernel(
             for c in range(2 * (last - first)):
                 dyg[(2 * first + c, s)] = words[:, c * P:(c + 1) * P]
 
-        words = keep.tile([P, 6 * C], U32, name="dyg", align_bytes=64)
+        words = keep.tile([P, 8 * C], U32, name="dyg", align_bytes=64)
         gather_gradients(0, 2, 0, words[:, 0:2 * C])
-        gather_gradients(0, 1, 1, placed.tile([P, C], U32, name="dyg01", align_bytes=64, offset=DY0_AT)[:])
+        gather_gradients(0, 1, 1, words[:, 6 * C:7 * C])
         gather_gradients(1, 2, 1, words[:, 2 * C:3 * C])
         gather_gradients(2, E, 0, words[:, 3 * C:5 * C])
         gather_gradients(2, 3, 1, words[:, 5 * C:6 * C])
+        gather_gradients(3, E, 1, words[:, 7 * C:8 * C])
 
         late = placed.tile([P, 5, ROW], U8, name="late", align_bytes=64, offset=DYS_AT + 64 - 5 * ROW)
         w2t_last = late[:, 1:5, :]
@@ -268,9 +269,6 @@ def tile_moe_rec_glu_sigmoid_kernel(
         w1t, w1ts, w3t, w3ts = w1, w1s, w2t_first, w2ts
         for c in range(SHARED):
             neg3, da = gradient_factor(c, dhs[c])
-            if c == 0:
-                words = placed.tile([P, C], U32, name="dyg31", align_bytes=64, offset=DY0_AT)
-                gather_gradients(3, E, 1, words[:])
             if c >= 2:
                 slopes[c + 3] = slope_factor(c + 3, a3s[c + 3])
             if c < 4:

from contextlib import ExitStack

import concourse.mybir as mybir
from concourse.masks import make_identity

K, T, E, C, H, N = 512, 512, 4, 256, 512, 1024
S = E * C
P = 128
TILES = S // P
LAST = TILES - 1
KT = K // P
ROW = 2 * H
FLOPS = 2 * S * (2 * K * H + N * H + 2 * H * K)

CALLS = ((0, 4), (4, 8), (8, 12), (12, 14), (15, 16), (14, 15))
TURN_BANKS = ("turn0", "turn1", "turn0", "turn1", "turn0", "sums4", "sums0", "sums5")
SHARED = 5
EARLY = 5
DYS_AT = 6144
GATE_AT = 13824
DY0_AT = DYS_AT + 576
WIDE = 704
WIDEST = 1408

F32 = mybir.dt.float32
BF16 = mybir.dt.bfloat16
I32 = mybir.dt.int32
U32 = mybir.dt.uint32
U16 = mybir.dt.uint16
U8 = mybir.dt.uint8
FP8X4 = mybir.dt.float8_e4m3fn_x4
FP4X4 = mybir.dt.float4_e2m1fn_x4
ALU = mybir.AluOpType
ACT = mybir.ActivationFunctionType


def tile_moe_rec_glu_sigmoid_kernel(
    tc, x_words, x_scales, dy_words, dy_scales, w1_words, w1_scales, w3_words, w3_scales, w2t_words, w2t_scales,
    w1t_words, w1t_scales, w3t_words, w3t_scales, gate, offs, pos1, pos2, out,
):
    nc = tc.nc
    with ExitStack() as ctx:
        keep = ctx.enter_context(tc.tile_pool(name="keep", bufs=1))
        placed = ctx.enter_context(tc.tile_pool(name="placed", bufs=1))
        work = ctx.enter_context(tc.tile_pool(name="work", bufs=5))
        psum = ctx.enter_context(tc.psum_pool(name="psum", bufs=1))

        offs_sb = keep.tile([P, S // 16], U16, name="offs_sb")
        pos1_sb = keep.tile([P, T // 16], U16, name="pos1_sb")
        pos2_sb = keep.tile([P, T // 16], U16, name="pos2_sb")
        x_win = keep.tile([P, S], I32, name="x_win", align_bytes=64)
        dy_win = placed.tile([P, 2 * T], I32, name="dy_win", align_bytes=64, offset=GATE_AT + 64 - 8 * T)
        xs_win = keep.tile([P, 1, WIDEST], U8, name="xs_win", tag="xs_win", align_bytes=64)
        dys_win = placed.tile([P, WIDEST], U8, name="dys_win", align_bytes=64, offset=DYS_AT)
        dys_rows = keep.tile([P, S], U8, name="dys_rows", align_bytes=64)
        dys = keep.tile([P, 2, S], U8, name="dys", align_bytes=64)
        w1 = keep.tile([P, E, ROW], U8, name="w1", align_bytes=64)
        w3_first = [keep.tile([P, 1 + e, ROW], U8, name="w3_%d" % e, align_bytes=64) for e in range(2)]
        w2t_first = placed.tile([P, 4, ROW], U8, name="w2t_first", align_bytes=64, offset=GATE_AT + 64)
        w1s = keep.tile([P, E, H], U8, name="w1s", align_bytes=64)
        w3s = keep.tile([P, E, H], U8, name="w3s", align_bytes=64)
        w2ts = keep.tile([P, 2 * E, H], U8, name="w2ts", align_bytes=64)
        gate_rows = placed.tile([P, 32], F32, name="gate_rows", align_bytes=64, offset=GATE_AT)
        gates = keep.tile([P, 32], F32, name="gates", align_bytes=64)
        neg_gates = keep.tile([P, TILES], F32, name="neg_gates")
        ident = keep.tile([P, P], F32, name="ident")
        dx = [keep.tile([P, S], F32, name="dx%d" % kt) for kt in range(KT)]
        grouped = {
            first: keep.tile([P, (last - first) * H], BF16, name="grouped%d" % first, align_bytes=64)
            for first, last in CALLS
        }
        scales = keep.tile([P, TILES * 2 * P], U8, name="scales", align_bytes=64)

        nc.gpsimd.memset(w3s[:].bitcast(I32), 0)
        for plane in (
            w1s[:].bitcast(I32), dys_win[:].bitcast(I32), xs_win[:, 0, T:].bitcast(I32),
            x_win[:, T:],
        ):
            nc.vector.memset(plane, 0)

        def load_rows(queue, planes, rows, q):
            src = rows.bitcast(I32)[:, 4 * q:4 * q + 4, :].rearrange("g j c -> j g c")
            queue.dma_start(planes[32 * q:32 * q + 4].bitcast(I32), src)

        def load_planes(planes, rows):
            for q in range(4):
                load_rows(nc.sync, planes, rows, q)

        def load_words(dst, words, first, last, queue=nc.sync):
            queue.dma_start(dst.bitcast(I32), words.bitcast(I32)[first:last].rearrange("e s p b -> p (e s) b"))

        def all_passes(rows):
            return rows.rearrange("e s b c -> (e s) b c")

        load_words(w3_first[0][:], w3_words, 0, 1, nc.gpsimd)
        load_rows(nc.gpsimd, w1s, all_passes(w1_scales), 0)
        load_words(w3_first[1][:], w3_words, 1, 3, nc.gpsimd)
        nc.sync.dma_start(offs_sb[:], offs)
        nc.scalar.dma_start(gate_rows[:], gate[0:4, :].rearrange("r (c b i) -> b (r c) i", b=4, i=32))
        nc.vector.transpose(gates[:], gate_rows[:])
        nc.gpsimd.tensor_scalar(neg_gates[:], gates[:, 0:TILES], -1.0, 0.0, ALU.mult, ALU.add)
        nc.gpsimd.memset(w2ts[:].bitcast(I32), 0)
        nc.gpsimd.memset(dys[:].bitcast(I32), 0)
        make_identity(nc, ident[:])
        for q in range(4):
            rows = x_scales.bitcast(I32)[0, 4 * q:4 * q + 4, :].rearrange("j c -> (j c)")
            queue = nc.sync if q < 2 else nc.scalar
            queue.dma_start(xs_win[32 * q:32 * q + 32, 0, 0:T].bitcast(I32), rows.partition_broadcast(8))
        nc.sync.dma_start(x_win[:, 0:T], x_words[0].rearrange("p t d -> p (t d)").bitcast(I32))
        load_words(w1[:], w1_words, 0, E)
        load_planes(w3s, all_passes(w3_scales))
        for q in range(1, 4):
            load_rows(nc.scalar, w1s, all_passes(w1_scales), q)
        nc.scalar.dma_start(
            dys_win[0:32, 0:T].bitcast(I32), dy_scales.bitcast(I32).rearrange("s b c -> b s c")
        )
        nc.sync.dma_start(
            dy_win[:, 0:2 * T].rearrange("p (s t) -> p s t", s=2), dy_words.rearrange("s p t d -> p s (t d)").bitcast(I32)
        )
        load_planes(w2ts, all_passes(w2t_scales))
        load_words(w2t_first[:], w2t_words, 0, 2)

        def entries(first, last):
            return offs_sb[:, first * (C // 16):last * (C // 16)]

        xg = keep.tile([P, S], U32, name="xg", align_bytes=64)
        xgs = keep.tile([P, S], U8, name="xgs", align_bytes=64)
        nc.vector.tensor_copy(xgs[:], xs_win[:, 0, :].indirect(offs_sb[:]))
        for first, last in ((0, 1), (1, E)):
            nc.vector.tensor_copy(xg[:, first * C:last * C], x_win[:].bitcast(U32).indirect(entries(first, last)))
        nc.vector.tensor_copy(dys_rows[:], dys_win[:].indirect(offs_sb[:]))
        for q in range(4):
            nc.sync.dma_start(dys[32 * q:32 * q + 4].bitcast(I32), dys_rows[8 * q:8 * q + 8, :].bitcast(I32))
        dyg = {}

        def gather_gradients(first, last, s, words):
            window = dy_win[:, s * T:s * T + (WIDE if s == 0 else T)].bitcast(U32)
            nc.vector.tensor_copy(words, window.indirect(entries(first, last)))
            for c in range(2 * (last - first)):
                dyg[(2 * first + c, s)] = words[:, c * P:(c + 1) * P]

        words = keep.tile([P, 8 * C], U32, name="dyg", align_bytes=64)
        gather_gradients(0, 2, 0, words[:, 0:2 * C])
        gather_gradients(0, 1, 1, words[:, 6 * C:7 * C])
        gather_gradients(1, 2, 1, words[:, 2 * C:3 * C])
        gather_gradients(2, E, 0, words[:, 3 * C:5 * C])
        gather_gradients(2, 3, 1, words[:, 5 * C:6 * C])
        gather_gradients(3, E, 1, words[:, 7 * C:8 * C])

        late = placed.tile([P, 5, ROW], U8, name="late", align_bytes=64, offset=DYS_AT + 64 - 5 * ROW)
        w2t_last = late[:, 1:5, :]
        load_words(w2t_last, w2t_words, 2, E)
        load_words(late[:, 0:1, :], w3_words, 3, E)
        w3 = [w3_first[0][:, 0, :], w3_first[1][:, 0, :], w3_first[1][:, 1, :], late[:, 0, :]]
        nc.sync.dma_start(pos1_sb[:], pos1)
        nc.sync.dma_start(pos2_sb[:], pos2)
        w2t = [w2t_first[:, r, :] for r in range(4)] + [w2t_last[:, r, :] for r in range(4)]

        def bank(name, n):
            return psum.tile([P, H], F32, name=name, tag="sums%d" % n, bufs=1)

        def tokens(c):
            cols = slice(c * P, (c + 1) * P)
            return xg[:, cols].bitcast(FP8X4), xgs[:, cols]

        def rest(c, n):
            a1 = bank("a1", n)
            nc.tensor.matmul_mx(a1[:], *tokens(c), w1[:, c // 2, :].bitcast(FP4X4), w1s[:, c // 2, :], start=True, stop=True)
            out_tile = keep.tile([P, H], F32, name="sig%d" % c, align_bytes=64)
            nc.scalar.activation(out_tile[:], a1[:], ACT.Sigmoid, scale=-1.0 if c < SHARED else 1.0)
            if c >= SHARED:
                squares[c] = keep.tile([P, H], F32, name="square%d" % c, align_bytes=64)
                nc.scalar.activation(squares[c][:], out_tile[:], ACT.Square, bias=-0.5)
            return out_tile

        def sum_a3(c, n):
            a3 = bank("a3", n)
            nc.tensor.matmul_mx(a3[:], *tokens(c), w3[c // 2].bitcast(FP4X4), w3s[:, c // 2, :], start=True, stop=True)
            return a3

        def sum_dh(c, n):
            e = c // 2
            dh = bank("dh", n)
            for s in range(2):
                nc.tensor.matmul_mx(
                    dh[:], dyg[(c, s)].bitcast(FP8X4), dys[:, s, c * P:(c + 1) * P],
                    w2t[2 * e + s].bitcast(FP4X4), w2ts[:, 2 * e + s, :], start=(s == 0), stop=(s == 1),
                )
            return dh

        def token_factor_early(c, n):
            a3 = sum_a3(c, n)
            gated = keep.tile([P, H], F32, name="gated%d" % c, align_bytes=64)
            negq = keep.tile([P, H], F32, name="negq%d" % c, align_bytes=64)
            nc.scalar.activation(gated[:], a3[:], ACT.Copy, scale=neg_gates[:, c:c + 1])
            nc.gpsimd.tensor_tensor(negq[:], gated[:], rests[c][:], ALU.mult)
            return negq

        def slope_factor(c, a3):
            factor = keep.tile([P, H], F32, name="slope%d" % c, align_bytes=64)
            nc.vector.scalar_tensor_tensor(factor[:], squares[c][:], 0.25, a3[:], ALU.subtract, ALU.mult)
            return factor

        def products(c, dh, factor):
            da = work.tile([P, 2, H], BF16, name="da", bufs=8, align_bytes=64)
            nc.vector.scalar_tensor_tensor(da[:, 1, :], dh[:], gates[:, c:c + 1], rests[c][:], ALU.mult, ALU.mult)
            nc.vector.scalar_tensor_tensor(da[:, 0, :], dh[:], neg_gates[:, c:c + 1], factor[:], ALU.mult, ALU.mult)
            return da

        def gradient_factor(c, dh):
            neg3 = work.tile([P, H], F32, name="neg3", bufs=5)
            da = work.tile([P, 2, H], BF16, name="da", bufs=8, align_bytes=64)
            nc.vector.scalar_tensor_tensor(neg3[:], rests[c][:], 1.0, dh[:], ALU.subtract, ALU.mult)
            nc.scalar.activation(da[:, 1, :], neg3[:], ACT.Copy, scale=neg_gates[:, c:c + 1])
            return neg3, da

        def turn(c, da):
            words = [da[:, a, :].bitcast(F32) for a in range(2)]
            turned = psum.tile([P, 4, P], F32, name="turned", tag=TURN_BANKS[c], bufs=1)
            turned_words = turned[:].rearrange("p (a u) s -> p a s u", u=2)
            for a in (1, 0):
                if c == LAST and a == 0:
                    turned = psum.tile([P, 4, P], F32, name="turned", tag="sums2", bufs=1)
                    turned_words = turned[:].rearrange("p (a u) s -> p a s u", u=2)
                for u in range(2):
                    nc.tensor.transpose(turned[:, 2 * a + u, :], words[a][:, u:2 * P:2], ident[:])
                if c == LAST:
                    half = grouped[2 * c + a][:].bitcast(F32).rearrange("p (s u) -> p s u", u=2)
                    nc.scalar.copy(half, turned_words[:, a])
            if c < LAST:
                first = max(f for f in grouped if f <= 2 * c)
                both = grouped[first][:, (2 * c - first) * H:(2 * c + 2 - first) * H]
                nc.scalar.copy(both.bitcast(F32).rearrange("p (a s u) -> p a s u", a=2, u=2), turned_words)

        def group(kt, tiles, tag):
            acc = psum.tile([P, len(tiles) * P], F32, name="acc", tag=tag, bufs=1)
            for n, c in enumerate(tiles):
                e = c // 2
                for a, w, ws in ((1, w3t, w3ts), (0, w1t, w1ts)):
                    nc.tensor.matmul_mx(
                        acc[:, n * P:(n + 1) * P], w[:, e, 2 * P * kt:2 * P * (kt + 1)].bitcast(FP4X4),
                        ws[:, e, P * kt:P * (kt + 1)], codes[:, (2 * c + a) * P:(2 * c + a + 1) * P].bitcast(FP8X4),
                        scales[:, (2 * c + a) * P:(2 * c + a + 1) * P], start=(a == 1), stop=(a == 0),
                    )
            nc.scalar.copy(dx[kt][:, tiles[0] * P:(tiles[-1] + 1) * P], acc[:])

        codes = keep.tile([P, TILES * 2 * P], U32, name="codes", tag="negq%d" % (SHARED - 1), align_bytes=64)
        first_rows = {4: ([0, 1, 2, 3], "sums1"), 12: ([4, 5, 6], "sums4"), 14: ([7], "sums3")}

        def quantise(first, last):
            words = codes[:, first * P:last * P]
            nc.vector.quantize_mx(words.bitcast(FP8X4), scales[:, first * P:last * P], grouped[first][:])
            if first in first_rows:
                group(0, *first_rows[first])

        rests, negqs, dhs, a3s, squares, slopes = [], {}, {}, {}, {}, {}
        for c, (n1, n3) in enumerate(((0, 1), (2, 3), (1, 0), (3, 2), (0, 1))):
            rests.append(rest(c, n1))
            negqs[c] = token_factor_early(c, n3)
        for c, n in ((5, 3), (6, 2), (7, 0)):
            rests.append(rest(c, n))
        for c, n in enumerate((4, 5, 1, 3)):
            dhs[c] = sum_dh(c, n)
        a3s[6] = sum_a3(6, 0)
        load_words(w1[:], w1t_words, 0, E)
        load_planes(w1s, all_passes(w1t_scales))
        load_words(w2t_first[:], w3t_words, 0, E)
        load_planes(w2ts[:, 0:E, :], all_passes(w3t_scales))
        w1t, w1ts, w3t, w3ts = w1, w1s, w2t_first, w2ts
        for c in range(SHARED):
            neg3, da = gradient_factor(c, dhs[c])
            if c >= 2:
                slopes[c + 3] = slope_factor(c + 3, a3s[c + 3])
            if c < 4:
                dhs[c + 4] = sum_dh(c + 4, (4, 2, 1, 3)[c])
            if c in (1, 2):
                a3s[2 * c + 3] = sum_a3(2 * c + 3, 5)
            nc.gpsimd.tensor_tensor(da[:, 0, :], neg3[:], negqs[c][:], ALU.mult)
            turn(c, da)
        for c in range(SHARED, TILES):
            turn(c, products(c, dhs[c], slopes[c]))
        for call in CALLS:
            quantise(*call)

        for kt, banks in ((1, ("sums0", "turn1")), (2, ("sums5", "sums0")), (3, ("sums2", "sums5"))):
            group(kt, [4, 5, 6, 7], banks[0])
            group(kt, [0, 1, 2, 3], banks[1])

        ones = [keep.tile([P, T], F32, name="one%d" % kt) for kt in range(KT)]

        def first_slots(kt, lo, hi):
            picked = dx[kt][:].indirect(pos1_sb[:, lo // 16:hi // 16])
            if kt == 0 or (kt == 1 and lo > 0):
                nc.vector.tensor_copy(ones[kt][:, lo:hi], picked)
            else:
                nc.scalar.activation(ones[kt][:, lo:hi], picked, ACT.Copy)

        def second_slots(kt, lo, hi):
            total = work.tile([P, hi - lo], F32, name="total", bufs=9)
            nc.vector.tensor_tensor(total[:], dx[kt][:].indirect(pos2_sb[:, lo // 16:hi // 16]), ones[kt][:, lo:hi], ALU.add)
            nc.sync.dma_start(out[kt * P:(kt + 1) * P, lo:hi], total[:])

        for kt in range(KT):
            first_slots(kt, 0, T // 2)
            first_slots(kt, T // 2, T)
            second_slots(kt, 0, T // 2)
            if kt < KT - 1:
                second_slots(kt, T // 2, T)
        second_slots(KT - 1, T // 2, 3 * T // 4)
        second_slots(KT - 1, 3 * T // 4, T)
